import numpy as np
import ml_dtypes


def mxq(x, axis, fmt="e4m3"):
    dtype, down = {"e4m3": (ml_dtypes.float8_e4m3fn, 7), "e5m2": (ml_dtypes.float8_e5m2, 14)}[fmt]
    v = np.moveaxis(np.asarray(x, np.float32).astype(ml_dtypes.bfloat16).astype(np.float64), axis, -1)
    blocks = v.reshape(v.shape[:-1] + (-1, 32))
    amax = np.abs(blocks).max(-1, keepdims=True)
    byte = np.maximum(np.where(amax > 0, np.frexp(amax)[1] - 1 + 127, 0) - down, 1)
    scale = np.exp2(byte - 127.0)
    codes = (blocks / scale).astype(np.float32).astype(dtype).astype(np.float64)
    return np.moveaxis((codes * scale).reshape(v.shape), -1, axis)


WIDE = False


def mx_kscale(k):
    if not WIDE:
        return np.ones(k)
    levels = np.array([24, -24, 12, -12, 0])
    if k % 512:
        return np.exp2(np.random.permutation(np.resize(levels, k // 32))).repeat(32)
    a = np.empty((k // 512, 16))
    for p in range(k // 512):
        a[p, :8] = np.random.permutation(np.resize(levels, 8))
        for g in range(8):
            far = levels[np.abs(levels - a[p, g]) >= 10]
            a[p, g + 8] = far[np.random.randint(len(far))]
    return np.exp2(a.ravel()).repeat(32)


def f64(x):
    return np.asarray(x).astype(np.float64)


def striped(idx):
    return np.tile(idx.reshape(-1, 16).T, (8, 1)).astype(np.uint16)


def unstriped(offs):
    return offs[:16].T.reshape(-1).astype(np.int64)


E2M1 = np.array([0.0, 0.5, 1.0, 1.5, 2.0, 3.0, 4.0, 6.0, -0.0, -0.5, -1.0, -1.5, -2.0, -3.0, -4.0, -6.0])


def pack_weight(w, fmt):
    k, n = w.shape
    w = f64(np.asarray(w, np.float32).astype(ml_dtypes.bfloat16)).reshape(k // 32, 32, n)
    amax = np.abs(w).max(1)
    if fmt == "e4m3":
        byte = np.frexp(amax)[1] - 1 + 127 - 7
    else:
        mant, ex = np.frexp(amax / 6.0)
        byte = np.where(mant > 0.5, ex, ex - 1) + 127
    byte = np.clip(np.where(amax > 0, byte, 1), 1, 254)
    scaled = (w * np.exp2(127.0 - byte)[:, None, :]).reshape(k, n).astype(np.float32)
    by_word = np.ascontiguousarray(scaled.reshape(k // 512, 128, 4, n).transpose(0, 1, 3, 2))
    if fmt == "e4m3":
        words = by_word.astype(ml_dtypes.float8_e4m3fn).view(np.uint8)
    else:
        c = by_word.astype(ml_dtypes.float4_e2m1fn).view(np.uint8) & 0xF
        words = (c[..., 0::2] | (c[..., 1::2] << 4)).reshape(k // 512, 128, 2 * n)
    return np.ascontiguousarray(words), np.ascontiguousarray(byte.astype(np.uint8).reshape(k // 512, 16, n))


def unpack_weight(words, scales, fmt):
    g, _, n = scales.shape
    words = np.ascontiguousarray(words).reshape(g, 128, n, -1)
    if fmt == "e4m3":
        vals = words.view(ml_dtypes.float8_e4m3fn).astype(np.float64)
    else:
        nib = np.empty((g, 128, n, 4), np.uint8)
        nib[..., 0::2] = words & 0xF
        nib[..., 1::2] = words >> 4
        vals = E2M1[nib]
    vals = vals * np.repeat(np.exp2(scales.astype(np.float64) - 127.0), 8, axis=1)[..., None]
    return vals.transpose(0, 1, 3, 2).reshape(g * 512, n)


def silu(f):
    return f / (1.0 + np.exp(-np.maximum(f, -700.0)))


K, R, T, M, J = 512, 1024, 4096, 1024, 1024


def setup_inputs():
    n = np.random.standard_normal
    s = mx_kscale(K)[:, None]
    u = mx_kscale(R)[:, None]
    p_tab = pack_weight(n((K, T)) * s, "e4m3")
    p_tab2 = pack_weight(n((K, T)) * s, "e4m3")
    p_wa = pack_weight(n((K, R)) / np.sqrt(K) / s, "e4m3")
    return {
        "tab_words": p_tab[0],
        "tab_scales": p_tab[1],
        "tab2_words": p_tab2[0],
        "tab2_scales": p_tab2[1],
        "wa_words": p_wa[0],
        "wa_scales": p_wa[1],
        "wb": (n((K, R)) / np.sqrt(K) / s).astype(np.float32),
        "sa": (np.random.uniform(0.5, 2.0, R) * u[:, 0]).astype(np.float32),
        "sb": (np.random.uniform(0.5, 2.0, R) / u[:, 0]).astype(np.float32),
        "b": (0.3 * n(J)).astype(np.float32),
        "offs": striped(np.random.permutation(T)[:M]),
        "offs2": striped(np.random.permutation(T)[:J]),
    }


def reference(tab_words, tab_scales, tab2_words, tab2_scales, wa_words, wa_scales, wb, sa, sb, b, offs, offs2):
    idx = unstriped(offs)
    idx2 = unstriped(offs2)
    tab_ = unpack_weight(tab_words, tab_scales, "e4m3")[:, idx]
    tab2_ = unpack_weight(tab2_words, tab2_scales, "e4m3")[:, idx2]
    wa_ = unpack_weight(wa_words, wa_scales, "e4m3")
    wb_ = mxq(f64(wb), 0, "e4m3")
    za = wa_.T @ tab_
    zb = wb_.T @ tab2_
    ha = f64(sa)[:, None] * silu(za)
    hb = f64(sb)[:, None] * silu(zb)
    ha_ = mxq(ha, 0, "e4m3")
    hb_ = mxq(hb, 0, "e4m3")
    y = ha_.T @ hb_
    return y * 0.03125 + f64(b)[None, :]

@@ -1,0 +1,247 @@
+from contextlib import ExitStack
+
+import concourse.mybir as mybir
+from concourse.masks import make_identity
+
+K, R, T, M, J = 512, 1024, 4096, 1024, 1024
+FLOPS = 2 * K * R * M + 2 * K * R * J + 2 * R * M * J
+
+F32 = mybir.dt.float32
+BF16 = mybir.dt.bfloat16
+I32 = mybir.dt.int32
+U32 = mybir.dt.uint32
+U16 = mybir.dt.uint16
+U8 = mybir.dt.uint8
+FP8X4 = mybir.dt.float8_e4m3fn_x4
+MULT = mybir.AluOpType.mult
+ADD = mybir.AluOpType.add
+SILU = mybir.ActivationFunctionType.Silu
+
+P = 128
+PACK = 4
+PASSES = R // (P * PACK)
+HALF = 512
+OUT_SCALE = 0.03125
+A_ROW = 4
+B_POOL = 0
+A_POOL = 0
+
+
+def tile_list_biaff_silu_bias_kernel(
+    tc, tab_words, tab_scales, tab2_words, tab2_scales, wa_words, wa_scales, wb, sa, sb, b, offs, offs2, out
+):
+    nc = tc.nc
+    with ExitStack() as ctx:
+        lists = ctx.enter_context(tc.tile_pool(name="lists", bufs=1))
+        keep = ctx.enter_context(tc.tile_pool(name="keep", bufs=1))
+        ring = ctx.enter_context(tc.tile_pool(name="ring", bufs=3))
+        psum = ctx.enter_context(tc.psum_pool(name="psum", bufs=4))
+
+        def words_of(dram):
+            return dram[0].rearrange("p n i -> p (n i)").bitcast(I32)
+
+        def load_scale_rows(plane, dram, first_row, engines):
+            rows = dram[0].bitcast(I32)
+            for r in range(4):
+                engines[r].dma_start(out=plane[first_row + r : P : 32, :], in_=rows[r:16:4, :])
+
+        def gather(dst, window, offsets):
+            nc.vector.tensor_copy(out=dst, in_=window.indirect(offsets))
+
+        list_b = lists.tile([P, J // 16], U16, name="list_b")
+        list_a = lists.tile([P, M // 16], U16, name="list_a")
+        nc.sync.dma_start(list_b[:], offs2)
+        nc.sync.dma_start(list_a[:], offs)
+
+        def load_wb(engine, g, tag):
+            raw = keep.tile([P, PACK, HALF], F32, name="wb_raw%d" % g, tag=tag, align_bytes=64)
+            engine.dma_start(out=raw[:], in_=wb[:, g * HALF : (g + 1) * HALF].rearrange("(p j) c -> p j c", j=PACK))
+            return raw
+
+        wb_raw0 = load_wb(nc.sync, 0, "slot_d")
+        table_b = keep.tile([P, T], I32, name="table_b", tag="slot_a", align_bytes=64)
+        nc.sync.dma_start(out=table_b[:], in_=words_of(tab2_words))
+
+        plane_b = keep.tile([P, T // 4], I32, name="plane_b", tag="slot_b", align_bytes=64)
+        plane_a = keep.tile([P, T // 4], I32, name="plane_a", tag="slot_c", align_bytes=64)
+        nc.vector.memset(plane_b[:], 0)
+        load_scale_rows(plane_b, tab2_scales, 0, [nc.scalar] * 4)
+        nc.vector.memset(plane_a[:], 0)
+        load_scale_rows(plane_a, tab_scales, A_ROW, [nc.scalar, nc.scalar, nc.gpsimd, nc.gpsimd])
+
+        s_rows = keep.tile([P, PASSES, P], F32, name="s_rows")
+        nc.gpsimd.memset(s_rows[:], 0.0)
+        for side, vec in enumerate((sa, sb)):
+            nc.gpsimd.dma_start(
+                out=s_rows[PACK * side : PACK * (side + 1)].rearrange("t g (q i) -> t (g q) i", i=8),
+                in_=vec.rearrange("(gq t i) -> t gq i", t=PACK, i=8),
+            )
+        ident = keep.tile([P, P], F32, name="ident")
+        make_identity(nc, ident[:])
+        warm = keep.tile([P, 1], F32, name="warm")
+        nc.scalar.activation(warm[:], ident[:, 0:1], SILU)
+        s_psum = psum.tile([P, PASSES, P], F32, name="s_psum", tag="s_psum", bufs=1)
+        for g in range(PASSES):
+            nc.tensor.transpose(s_psum[:, g, :], s_rows[:, g, :], ident[:])
+        s_cols = keep.tile([P, PASSES, 2 * PACK], F32, name="s_cols")
+        nc.scalar.copy(out=s_cols[:], in_=s_psum[:, :, 0 : 2 * PACK])
+
+
+        vb_words = keep.tile([P, J], U32, name="vb_words", align_bytes=64)
+        vb_scales = keep.tile([P, J], U8, name="vb_scales", align_bytes=64)
+        va_words = keep.tile([P, M], U32, name="va_words", align_bytes=64)
+        va_scales = keep.tile([P, M], U8, name="va_scales", align_bytes=64)
+        gather(vb_scales[:], plane_b[:].bitcast(U8), list_b[:])
+        wb_raw1 = load_wb(nc.sync, 1, "slot_b")
+        gather(va_scales[:], plane_a[:].bitcast(U8), list_a[:])
+
+        wb_words = keep.tile([P, PASSES, HALF], U32, name="wb_words", align_bytes=64)
+        wb_scales = keep.tile([P, PASSES, HALF], U8, name="wb_scales", align_bytes=64)
+
+        def quantise_wb(g, raw):
+            grouped = keep.tile([P, PACK, 16, 8, PACK], BF16, name="wb_grouped%d" % g, align_bytes=64)
+            source = raw[:].rearrange("p j (q t i) -> p t q i j", t=PACK, i=8)
+            for t in range(PACK):
+                nc.scalar.copy(out=grouped[:, t], in_=source[:, t])
+            nc.vector.quantize_mx(
+                out=wb_words[:, g, :].bitcast(FP8X4),
+                scales=wb_scales[:, g, :],
+                in_=grouped[:].rearrange("p t q i j -> p (t q i j)"),
+            )
+
+        quantise_wb(0, wb_raw0)
+        table_a = keep.tile([P, T], I32, name="table_a", tag="slot_d", align_bytes=64)
+        wa_raw = keep.tile([P, R], I32, name="wa_raw", tag="slot_c", align_bytes=64)
+        nc.sync.dma_start(out=wa_raw[:], in_=words_of(wa_words))
+        nc.sync.dma_start(out=table_a[:], in_=words_of(tab_words))
+
+        def gather_words(dst, table, offsets, h):
+            gather(dst[:, h * HALF : (h + 1) * HALF], table[:].bitcast(U32), offsets[:, h * HALF // 16 : (h + 1) * HALF // 16])
+
+        for h in range(2):
+            gather_words(vb_words, table_b, list_b, h)
+
+        bias = keep.tile([P, J], F32, name="bias", tag="slot_a", align_bytes=64)
+        nc.sync.dma_start(out=bias[:], in_=b.partition_broadcast(P))
+
+        def hidden(dst, w_words, w_scales, g, v_words, v_scales, first_row, n):
+            cols = slice(n * P, (n + 1) * P)
+            bank = psum.tile([P, PACK, P], F32, name="bank", tag="hidden", bufs=3)
+            for t in range(PACK):
+                nc.tensor.matmul_mx(
+                    out=bank[:, t, :],
+                    lhsT=w_words[:, g, t * P : (t + 1) * P].bitcast(FP8X4),
+                    lhsT_scale=w_scales[:, g, t * P : (t + 1) * P],
+                    rhs=v_words[:, cols].bitcast(FP8X4),
+                    rhs_scale=v_scales[first_row:P, cols],
+                    start=True,
+                    stop=True,
+                )
+            nc.scalar.activation(dst, bank[:].rearrange("p t n -> p n t"), SILU)
+
+        hb_words = keep.tile([P, PASSES, J], U32, name="hb_words", align_bytes=64)
+        hb_scales = keep.tile([P, PASSES, J], U8, name="hb_scales", align_bytes=64)
+
+        def b_act(g, c):
+            act = ring.tile([P, 2, P, PACK], F32, name="act", tag="act", bufs=4)
+            for u in range(2):
+                hidden(act[:, u], wb_words, wb_scales, g, vb_words, vb_scales, 0, 2 * c + u)
+            return act
+
+        def scale(engine, factors, h, act):
+            engine.tensor_tensor(out=h, in0=act, in1=factors.unsqueeze(1).to_broadcast(list(h.shape)), op=MULT)
+
+        def b_front(g, c):
+            act = b_act(g, c)[:].rearrange("p u n t -> p (u n) t")
+            h = ring.tile([P, 2 * P, PACK], BF16, name="h", tag="h", bufs=2, align_bytes=64)
+            cut = 2 * P - B_POOL
+            if B_POOL:
+                scale(nc.gpsimd, s_cols[:, g, PACK : 2 * PACK], h[:, cut:], act[:, cut:])
+            scale(nc.vector, s_psum[:, g, PACK : 2 * PACK], h[:, :cut], act[:, :cut])
+            return h
+
+        def b_back(g, c, h):
+            cols = slice(c * 2 * P, (c + 1) * 2 * P)
+            nc.vector.quantize_mx(
+                out=hb_words[:, g, cols].bitcast(FP8X4), scales=hb_scales[:, g, cols], in_=h[:].rearrange("p n t -> p (n t)")
+            )
+
+        wa_plane = keep.tile([P, R // 4], I32, name="wa_plane", tag="slot_b", align_bytes=64)
+        wa_sorted = keep.tile([P, PASSES, HALF], I32, name="wa_sorted", align_bytes=64)
+        wa_sorted_scales = keep.tile([P, PASSES, HALF // 4], I32, name="wa_sorted_scales", align_bytes=64)
+
+        def sort_wa():
+            nc.gpsimd.memset(wa_plane[:], 0)
+            load_scale_rows(wa_plane, wa_scales, 0, [nc.sync] * 4)
+            for g in range(PASSES):
+                nc.vector.tensor_copy(
+                    out=wa_sorted[:, g, :].rearrange("p (t q i) -> p t q i", t=PACK, i=8),
+                    in_=wa_raw[:, g * HALF : (g + 1) * HALF].rearrange("p (q t i) -> p t q i", t=PACK, i=8),
+                )
+                nc.vector.tensor_copy(
+                    out=wa_sorted_scales[:, g, :].rearrange("p (t q i) -> p t q i", t=PACK, i=2),
+                    in_=wa_plane[:, g * HALF // 4 : (g + 1) * HALF // 4].rearrange("p (q t i) -> p t q i", t=PACK, i=2),
+                )
+
+        b_steps = [(g, c) for g in range(PASSES) for c in range(J // (2 * P))]
+        hs = {0: b_front(*b_steps[0]), 1: b_front(*b_steps[1])}
+        quantise_wb(1, wb_raw1)
+        for step, (g, c) in enumerate(b_steps):
+            b_back(g, c, hs[step])
+            if step + 2 < len(b_steps):
+                hs[step + 2] = b_front(*b_steps[step + 2])
+            if step == 4:
+                sort_wa()
+                gather_words(va_words, table_a, list_a, 0)
+
+        wa_scale_bytes = wa_sorted_scales[:].bitcast(U8)
+
+        def a_front(mt):
+            act = ring.tile([P, PASSES, P, PACK], F32, name="act", tag="act", bufs=4)
+            for g in range(PASSES):
+                hidden(act[:, g], wa_sorted, wa_scale_bytes, g, va_words, va_scales, A_ROW, mt)
+            h = ring.tile([P, PASSES, P, PACK], BF16, name="h", tag="h", bufs=2, align_bytes=64)
+            if A_POOL:
+                scale(nc.gpsimd, s_cols[:, 1, 0:PACK], h[:, 1], act[:, 1])
+                scale(nc.vector, s_psum[:, 0, 0:PACK], h[:, 0], act[:, 0])
+            else:
+                nc.vector.tensor_tensor(
+                    out=h[:], in0=act[:], in1=s_psum[:, :, 0:PACK].unsqueeze(2).to_broadcast([P, PASSES, P, PACK]), op=MULT
+                )
+            return h
+
+        def a_back(h):
+            words = ring.tile([P, PASSES * P], U32, name="ha_words", tag="ha_words", align_bytes=64)
+            scales = ring.tile([P, PASSES * P], U8, name="ha_scales", tag="ha_scales", align_bytes=64)
+            nc.vector.quantize_mx(out=words[:].bitcast(FP8X4), scales=scales[:], in_=h[:].rearrange("p g n t -> p (g n t)"))
+            return words, scales
+
+        def scores(mt, words, scales):
+            for jh in range(J // HALF):
+                cols = slice(jh * HALF, (jh + 1) * HALF)
+                acc = psum.tile([P, HALF], F32, name="acc", tag="scores")
+                for g in range(PASSES):
+                    nc.tensor.matmul_mx(
+                        out=acc[:],
+                        lhsT=words[:, g * P : (g + 1) * P].bitcast(FP8X4),
+                        lhsT_scale=scales[:, g * P : (g + 1) * P],
+                        rhs=hb_words[:, g, cols].bitcast(FP8X4),
+                        rhs_scale=hb_scales[:, g, cols],
+                        start=(g == 0),
+                        stop=(g == PASSES - 1),
+                    )
+                res = ring.tile([P, HALF], F32, name="res", tag="res", bufs=6)
+                nc.vector.scalar_tensor_tensor(out=res[:], in0=acc[:], scalar=OUT_SCALE, in1=bias[:, cols], op0=MULT, op1=ADD)
+                nc.sync.dma_start(out=out[mt * P : (mt + 1) * P, cols], in_=res[:])
+
+        tiles = M // P
+        hs = {0: a_front(0), 1: a_front(1)}
+        gather_words(va_words, table_a, list_a, 1)
+        qs = {}
+        for step in range(tiles + 1):
+            if step < tiles:
+                qs[step] = a_back(hs[step])
+            if step + 2 < tiles:
+                hs[step + 2] = a_front(step + 2)
+            if step >= 1:
+                scores(step - 1, *qs[step - 1])

@@ -23,8 +23,8 @@ PASSES = R // (P * PACK)
 HALF = 512
 OUT_SCALE = 0.03125
 A_ROW = 4
-B_POOL = 0
-A_POOL = 0
+B_POOL = 64
+A_POOL = 1
 
 
 def tile_list_biaff_silu_bias_kernel(
@@ -65,14 +65,17 @@ def tile_list_biaff_silu_bias_kernel(
         plane_b = keep.tile([P, T // 4], I32, name="plane_b", tag="slot_b", align_bytes=64)
         plane_a = keep.tile([P, T // 4], I32, name="plane_a", tag="slot_c", align_bytes=64)
         nc.vector.memset(plane_b[:], 0)
-        load_scale_rows(plane_b, tab2_scales, 0, [nc.scalar] * 4)
-        nc.vector.memset(plane_a[:], 0)
-        load_scale_rows(plane_a, tab_scales, A_ROW, [nc.scalar, nc.scalar, nc.gpsimd, nc.gpsimd])
-
+        load_scale_rows(plane_b, tab2_scales, 0, [nc.gpsimd] * 4)
         s_rows = keep.tile([P, PASSES, P], F32, name="s_rows")
-        nc.gpsimd.memset(s_rows[:], 0.0)
+        nc.vector.memset(s_rows[:], 0.0)
+        nc.vector.memset(plane_a[:], 0)
+        load_scale_rows(plane_a, tab_scales, A_ROW, [nc.gpsimd] * 4)
+
+        wa_plane = keep.tile([P, R // 4], I32, name="wa_plane", align_bytes=64)
+        nc.vector.memset(wa_plane[:], 0)
+        load_scale_rows(wa_plane, wa_scales, 0, [nc.sync] * 4)
         for side, vec in enumerate((sa, sb)):
-            nc.gpsimd.dma_start(
+            nc.scalar.dma_start(
                 out=s_rows[PACK * side : PACK * (side + 1)].rearrange("t g (q i) -> t (g q) i", i=8),
                 in_=vec.rearrange("(gq t i) -> t gq i", t=PACK, i=8),
             )
@@ -143,7 +146,7 @@ def tile_list_biaff_silu_bias_kernel(
         hb_scales = keep.tile([P, PASSES, J], U8, name="hb_scales", align_bytes=64)
 
         def b_act(g, c):
-            act = ring.tile([P, 2, P, PACK], F32, name="act", tag="act", bufs=4)
+            act = ring.tile([P, 2, P, PACK], F32, name="act", tag="act", bufs=5)
             for u in range(2):
                 hidden(act[:, u], wb_words, wb_scales, g, vb_words, vb_scales, 0, 2 * c + u)
             return act
@@ -153,7 +156,7 @@ def tile_list_biaff_silu_bias_kernel(
 
         def b_front(g, c):
             act = b_act(g, c)[:].rearrange("p u n t -> p (u n) t")
-            h = ring.tile([P, 2 * P, PACK], BF16, name="h", tag="h", bufs=2, align_bytes=64)
+            h = ring.tile([P, 2 * P, PACK], BF16, name="h", tag="h", bufs=3, align_bytes=64)
             cut = 2 * P - B_POOL
             if B_POOL:
                 scale(nc.gpsimd, s_cols[:, g, PACK : 2 * PACK], h[:, cut:], act[:, cut:])
@@ -166,13 +169,10 @@ def tile_list_biaff_silu_bias_kernel(
                 out=hb_words[:, g, cols].bitcast(FP8X4), scales=hb_scales[:, g, cols], in_=h[:].rearrange("p n t -> p (n t)")
             )
 
-        wa_plane = keep.tile([P, R // 4], I32, name="wa_plane", tag="slot_b", align_bytes=64)
         wa_sorted = keep.tile([P, PASSES, HALF], I32, name="wa_sorted", align_bytes=64)
         wa_sorted_scales = keep.tile([P, PASSES, HALF // 4], I32, name="wa_sorted_scales", align_bytes=64)
 
         def sort_wa():
-            nc.gpsimd.memset(wa_plane[:], 0)
-            load_scale_rows(wa_plane, wa_scales, 0, [nc.sync] * 4)
             for g in range(PASSES):
                 nc.vector.tensor_copy(
                     out=wa_sorted[:, g, :].rearrange("p (t q i) -> p t q i", t=PACK, i=8),
@@ -197,10 +197,10 @@ def tile_list_biaff_silu_bias_kernel(
         wa_scale_bytes = wa_sorted_scales[:].bitcast(U8)
 
         def a_front(mt):
-            act = ring.tile([P, PASSES, P, PACK], F32, name="act", tag="act", bufs=4)
+            act = ring.tile([P, PASSES, P, PACK], F32, name="act", tag="act", bufs=5)
             for g in range(PASSES):
                 hidden(act[:, g], wa_sorted, wa_scale_bytes, g, va_words, va_scales, A_ROW, mt)
-            h = ring.tile([P, PASSES, P, PACK], BF16, name="h", tag="h", bufs=2, align_bytes=64)
+            h = ring.tile([P, PASSES, P, PACK], BF16, name="h", tag="h", bufs=3, align_bytes=64)
             if A_POOL:
                 scale(nc.gpsimd, s_cols[:, 1, 0:PACK], h[:, 1], act[:, 1])
                 scale(nc.vector, s_psum[:, 0, 0:PACK], h[:, 0], act[:, 0])
@@ -241,7 +241,7 @@ def tile_list_biaff_silu_bias_kernel(
         for step in range(tiles + 1):
             if step < tiles:
                 qs[step] = a_back(hs[step])
-            if step + 2 < tiles:
-                hs[step + 2] = a_front(step + 2)
             if step >= 1:
                 scores(step - 1, *qs[step - 1])
+            if step + 2 < tiles:
+                hs[step + 2] = a_front(step + 2)

@@ -23,8 +23,8 @@ PASSES = R // (P * PACK)
 HALF = 512
 OUT_SCALE = 0.03125
 A_ROW = 4
-B_POOL = 64
-A_POOL = 1
+B_POOL = 56
+A_POOL = (0, 0, 24, 72, 72, 72, 72, 72)
 
 
 def tile_list_biaff_silu_bias_kernel(
@@ -62,7 +62,11 @@ def tile_list_biaff_silu_bias_kernel(
         table_b = keep.tile([P, T], I32, name="table_b", tag="slot_a", align_bytes=64)
         nc.sync.dma_start(out=table_b[:], in_=words_of(tab2_words))
 
-        plane_b = keep.tile([P, T // 4], I32, name="plane_b", tag="slot_b", align_bytes=64)
+        ident = keep.tile([P, P], F32, name="ident")
+        make_identity(nc, ident[:])
+        warm = keep.tile([P, 1], F32, name="warm")
+        nc.scalar.activation(warm[:], ident[:, 0:1], SILU)
+        plane_b = keep.tile([P, T // 4], I32, name="plane_b", tag="slot_e", align_bytes=64)
         plane_a = keep.tile([P, T // 4], I32, name="plane_a", tag="slot_c", align_bytes=64)
         nc.vector.memset(plane_b[:], 0)
         load_scale_rows(plane_b, tab2_scales, 0, [nc.gpsimd] * 4)
@@ -79,10 +83,6 @@ def tile_list_biaff_silu_bias_kernel(
                 out=s_rows[PACK * side : PACK * (side + 1)].rearrange("t g (q i) -> t (g q) i", i=8),
                 in_=vec.rearrange("(gq t i) -> t gq i", t=PACK, i=8),
             )
-        ident = keep.tile([P, P], F32, name="ident")
-        make_identity(nc, ident[:])
-        warm = keep.tile([P, 1], F32, name="warm")
-        nc.scalar.activation(warm[:], ident[:, 0:1], SILU)
         s_psum = psum.tile([P, PASSES, P], F32, name="s_psum", tag="s_psum", bufs=1)
         for g in range(PASSES):
             nc.tensor.transpose(s_psum[:, g, :], s_rows[:, g, :], ident[:])
@@ -90,19 +90,15 @@ def tile_list_biaff_silu_bias_kernel(
         nc.scalar.copy(out=s_cols[:], in_=s_psum[:, :, 0 : 2 * PACK])
 
 
-        vb_words = keep.tile([P, J], U32, name="vb_words", align_bytes=64)
         vb_scales = keep.tile([P, J], U8, name="vb_scales", align_bytes=64)
-        va_words = keep.tile([P, M], U32, name="va_words", align_bytes=64)
-        va_scales = keep.tile([P, M], U8, name="va_scales", align_bytes=64)
         gather(vb_scales[:], plane_b[:].bitcast(U8), list_b[:])
-        wb_raw1 = load_wb(nc.sync, 1, "slot_b")
-        gather(va_scales[:], plane_a[:].bitcast(U8), list_a[:])
+        vb_words = keep.tile([P, J], U32, name="vb_words", tag="slot_e", align_bytes=64)
 
         wb_words = keep.tile([P, PASSES, HALF], U32, name="wb_words", align_bytes=64)
         wb_scales = keep.tile([P, PASSES, HALF], U8, name="wb_scales", align_bytes=64)
 
         def quantise_wb(g, raw):
-            grouped = keep.tile([P, PACK, 16, 8, PACK], BF16, name="wb_grouped%d" % g, align_bytes=64)
+            grouped = keep.tile([P, PACK, 16, 8, PACK], BF16, name="wb_grouped%d" % g, tag="slot_g%d" % g, align_bytes=64)
             source = raw[:].rearrange("p j (q t i) -> p t q i j", t=PACK, i=8)
             for t in range(PACK):
                 nc.scalar.copy(out=grouped[:, t], in_=source[:, t])
@@ -113,9 +109,8 @@ def tile_list_biaff_silu_bias_kernel(
             )
 
         quantise_wb(0, wb_raw0)
-        table_a = keep.tile([P, T], I32, name="table_a", tag="slot_d", align_bytes=64)
-        wa_raw = keep.tile([P, R], I32, name="wa_raw", tag="slot_c", align_bytes=64)
-        nc.sync.dma_start(out=wa_raw[:], in_=words_of(wa_words))
+        wb_raw1 = load_wb(nc.sync, 1, "slot_d")
+        table_a = keep.tile([P, T], I32, name="table_a", tag="slot_g0", align_bytes=64)
         nc.sync.dma_start(out=table_a[:], in_=words_of(tab_words))
 
         def gather_words(dst, table, offsets, h):
@@ -123,9 +118,11 @@ def tile_list_biaff_silu_bias_kernel(
 
         for h in range(2):
             gather_words(vb_words, table_b, list_b, h)
+        va_scales = keep.tile([P, M], U8, name="va_scales", tag="slot_a", align_bytes=64)
+        gather(va_scales[:], plane_a[:].bitcast(U8), list_a[:])
+        wa_raw = keep.tile([P, R], I32, name="wa_raw", tag="slot_c", align_bytes=64)
+        nc.sync.dma_start(out=wa_raw[:], in_=words_of(wa_words))
 
-        bias = keep.tile([P, J], F32, name="bias", tag="slot_a", align_bytes=64)
-        nc.sync.dma_start(out=bias[:], in_=b.partition_broadcast(P))
 
         def hidden(dst, w_words, w_scales, g, v_words, v_scales, first_row, n):
             cols = slice(n * P, (n + 1) * P)
@@ -186,6 +183,9 @@ def tile_list_biaff_silu_bias_kernel(
         b_steps = [(g, c) for g in range(PASSES) for c in range(J // (2 * P))]
         hs = {0: b_front(*b_steps[0]), 1: b_front(*b_steps[1])}
         quantise_wb(1, wb_raw1)
+        va_words = keep.tile([P, M], U32, name="va_words", tag="slot_g1", align_bytes=64)
+        bias = keep.tile([P, J], F32, name="bias", tag="slot_d", align_bytes=64)
+        nc.sync.dma_start(out=bias[:], in_=b.partition_broadcast(P))
         for step, (g, c) in enumerate(b_steps):
             b_back(g, c, hs[step])
             if step + 2 < len(b_steps):
@@ -200,14 +200,16 @@ def tile_list_biaff_silu_bias_kernel(
             act = ring.tile([P, PASSES, P, PACK], F32, name="act", tag="act", bufs=5)
             for g in range(PASSES):
                 hidden(act[:, g], wa_sorted, wa_scale_bytes, g, va_words, va_scales, A_ROW, mt)
-            h = ring.tile([P, PASSES, P, PACK], BF16, name="h", tag="h", bufs=3, align_bytes=64)
-            if A_POOL:
-                scale(nc.gpsimd, s_cols[:, 1, 0:PACK], h[:, 1], act[:, 1])
-                scale(nc.vector, s_psum[:, 0, 0:PACK], h[:, 0], act[:, 0])
-            else:
-                nc.vector.tensor_tensor(
-                    out=h[:], in0=act[:], in1=s_psum[:, :, 0:PACK].unsqueeze(2).to_broadcast([P, PASSES, P, PACK]), op=MULT
-                )
+            h = ring.tile([P, PASSES, P, PACK], BF16, name="ha", tag="ha", bufs=2, align_bytes=64)
+            cut = P - A_POOL[mt]
+            for engine, factors, cols in ((nc.gpsimd, s_cols, slice(cut, P)), (nc.vector, s_psum, slice(0, cut))):
+                if cols.stop > cols.start:
+                    engine.tensor_tensor(
+                        out=h[:, :, cols],
+                        in0=act[:, :, cols],
+                        in1=factors[:, :, 0:PACK].unsqueeze(2).to_broadcast([P, PASSES, cols.stop - cols.start, PACK]),
+                        op=MULT,
+                    )
             return h
 
         def a_back(h):

@@ -22,9 +22,9 @@ PACK = 4
 PASSES = R // (P * PACK)
 HALF = 512
 OUT_SCALE = 0.03125
-A_ROW = 4
-B_POOL = 56
-A_POOL = (0, 0, 24, 72, 72, 72, 72, 72)
+SCALE_ROWS = K // 32
+B_STEPS = ((128, 48), (128, 48), (256, 128), (256, 128), (256, 128))
+A_STEPS = ((256, 128), (256, 304), (256, 304), (128, 176), (128, 136))
 
 
 def tile_list_biaff_silu_bias_kernel(
@@ -40,183 +40,168 @@ def tile_list_biaff_silu_bias_kernel(
         def words_of(dram):
             return dram[0].rearrange("p n i -> p (n i)").bitcast(I32)
 
-        def load_scale_rows(plane, dram, first_row, engines):
-            rows = dram[0].bitcast(I32)
-            for r in range(4):
-                engines[r].dma_start(out=plane[first_row + r : P : 32, :], in_=rows[r:16:4, :])
-
         def gather(dst, window, offsets):
             nc.vector.tensor_copy(out=dst, in_=window.indirect(offsets))
+
+        def zeroed(name, shape, dtype, tag=None):
+            tile = keep.tile(shape, dtype, name=name, tag=tag or name, align_bytes=64)
+            nc.vector.memset(tile[:], 0)
+            return tile
 
         list_b = lists.tile([P, J // 16], U16, name="list_b")
         list_a = lists.tile([P, M // 16], U16, name="list_a")
         nc.sync.dma_start(list_b[:], offs2)
         nc.sync.dma_start(list_a[:], offs)
 
-        def load_wb(engine, g, tag):
-            raw = keep.tile([P, PACK, HALF], F32, name="wb_raw%d" % g, tag=tag, align_bytes=64)
-            engine.dma_start(out=raw[:], in_=wb[:, g * HALF : (g + 1) * HALF].rearrange("(p j) c -> p j c", j=PACK))
+        def load_wb(g):
+            raw = keep.tile([P, PACK, HALF], F32, name="wb_raw%d" % g, tag="raw%d" % g, align_bytes=64)
+            nc.sync.dma_start(out=raw[:], in_=wb[:, g * HALF : (g + 1) * HALF].rearrange("(p j) c -> p j c", j=PACK))
             return raw
 
-        wb_raw0 = load_wb(nc.sync, 0, "slot_d")
-        table_b = keep.tile([P, T], I32, name="table_b", tag="slot_a", align_bytes=64)
-        nc.sync.dma_start(out=table_b[:], in_=words_of(tab2_words))
-
-        ident = keep.tile([P, P], F32, name="ident")
-        make_identity(nc, ident[:])
-        warm = keep.tile([P, 1], F32, name="warm")
-        nc.scalar.activation(warm[:], ident[:, 0:1], SILU)
-        plane_b = keep.tile([P, T // 4], I32, name="plane_b", tag="slot_e", align_bytes=64)
-        plane_a = keep.tile([P, T // 4], I32, name="plane_a", tag="slot_c", align_bytes=64)
-        nc.vector.memset(plane_b[:], 0)
-        load_scale_rows(plane_b, tab2_scales, 0, [nc.gpsimd] * 4)
-        s_rows = keep.tile([P, PASSES, P], F32, name="s_rows")
-        nc.vector.memset(s_rows[:], 0.0)
-        nc.vector.memset(plane_a[:], 0)
-        load_scale_rows(plane_a, tab_scales, A_ROW, [nc.gpsimd] * 4)
-
-        wa_plane = keep.tile([P, R // 4], I32, name="wa_plane", align_bytes=64)
-        nc.vector.memset(wa_plane[:], 0)
-        load_scale_rows(wa_plane, wa_scales, 0, [nc.sync] * 4)
+        wb_raw = [load_wb(0)]
+        rows_b = zeroed("rows_b", [P, T // 4], I32)
+        nc.sync.dma_start(out=rows_b[0:P:8, :], in_=tab2_scales[0].bitcast(I32))
+        rows_a = zeroed("rows_a", [P, T // 4], I32)
+        nc.sync.dma_start(out=rows_a[4:P:8, :], in_=tab_scales[0].bitcast(I32))
+        s_rows = zeroed("s_rows", [P, PASSES, P], F32)
         for side, vec in enumerate((sa, sb)):
-            nc.scalar.dma_start(
+            nc.sync.dma_start(
                 out=s_rows[PACK * side : PACK * (side + 1)].rearrange("t g (q i) -> t (g q) i", i=8),
                 in_=vec.rearrange("(gq t i) -> t gq i", t=PACK, i=8),
             )
-        s_psum = psum.tile([P, PASSES, P], F32, name="s_psum", tag="s_psum", bufs=1)
-        for g in range(PASSES):
-            nc.tensor.transpose(s_psum[:, g, :], s_rows[:, g, :], ident[:])
-        s_cols = keep.tile([P, PASSES, 2 * PACK], F32, name="s_cols")
-        nc.scalar.copy(out=s_cols[:], in_=s_psum[:, :, 0 : 2 * PACK])
+        nc.sync.dma_start(out=s_rows[2 * PACK : 2 * PACK + J // P, 0, :], in_=b.rearrange("(c p) -> c p", p=P))
+        wb_raw.append(load_wb(1))
+        table_b = keep.tile([P, T], I32, name="table_b", align_bytes=64)
+        nc.sync.dma_start(out=table_b[:], in_=words_of(tab2_words))
 
+        ident = zeroed("ident", [P, P], F32)
+        make_identity(nc, ident[:], nomemset=True)
+        warm = keep.tile([P, 1], F32, name="warm")
+        nc.scalar.activation(warm[:], ident[:, 0:1], SILU)
 
-        vb_scales = keep.tile([P, J], U8, name="vb_scales", align_bytes=64)
-        gather(vb_scales[:], plane_b[:].bitcast(U8), list_b[:])
-        vb_words = keep.tile([P, J], U32, name="vb_words", tag="slot_e", align_bytes=64)
+        vb_plane = zeroed("vb_plane", [P, J // 4], I32)
+        va_plane = zeroed("va_plane", [P, M // 4], I32)
+
+        def gather_scales(name, rows, first, offsets, plane, engine):
+            picked = keep.tile([P, J], U8, name=name, align_bytes=64)
+            gather(picked[:], rows[:].bitcast(U8), offsets[:])
+            for r in range(4):
+                engine.dma_start(out=plane[r:P:32, :], in_=picked[:].bitcast(I32)[first + 8 * r : P : 32, :])
 
         wb_words = keep.tile([P, PASSES, HALF], U32, name="wb_words", align_bytes=64)
         wb_scales = keep.tile([P, PASSES, HALF], U8, name="wb_scales", align_bytes=64)
 
-        def quantise_wb(g, raw):
-            grouped = keep.tile([P, PACK, 16, 8, PACK], BF16, name="wb_grouped%d" % g, tag="slot_g%d" % g, align_bytes=64)
-            source = raw[:].rearrange("p j (q t i) -> p t q i j", t=PACK, i=8)
+        def cast_wb(g):
+            grouped = keep.tile([P, PACK, 16, 8, PACK], BF16, name="wb_grouped%d" % g, align_bytes=64)
+            source = wb_raw[g][:].rearrange("p j (q t i) -> p t q i j", t=PACK, i=8)
             for t in range(PACK):
                 nc.scalar.copy(out=grouped[:, t], in_=source[:, t])
+            return grouped
+
+        def quantise_wb(g, grouped):
             nc.vector.quantize_mx(
                 out=wb_words[:, g, :].bitcast(FP8X4),
                 scales=wb_scales[:, g, :],
                 in_=grouped[:].rearrange("p t q i j -> p (t q i j)"),
             )
 
-        quantise_wb(0, wb_raw0)
-        wb_raw1 = load_wb(nc.sync, 1, "slot_d")
-        table_a = keep.tile([P, T], I32, name="table_a", tag="slot_g0", align_bytes=64)
+        grouped0 = cast_wb(0)
+        gather_scales("picked_b", rows_b, 0, list_b, vb_plane, nc.scalar)
+        wa_raw = keep.tile([P, R], I32, name="wa_raw", tag="rows_b", align_bytes=64)
+        nc.sync.dma_start(out=wa_raw[:], in_=words_of(wa_words))
+        table_a = keep.tile([P, T], I32, name="table_a", tag="raw0", align_bytes=64)
         nc.sync.dma_start(out=table_a[:], in_=words_of(tab_words))
+        grouped1 = cast_wb(1)
+        gather_scales("picked_a", rows_a, 4, list_a, va_plane, nc.sync)
+        wa_plane = zeroed("wa_plane", [P, R // 4], I32, tag="rows_a")
+        for r in range(4):
+            nc.sync.dma_start(out=wa_plane[r:P:32, :], in_=wa_scales[0].bitcast(I32)[r:SCALE_ROWS:4, :])
+        quantise_wb(0, grouped0)
+        quantise_wb(1, grouped1)
+
+        s_psum = psum.tile([P, PASSES, P], F32, name="s_psum", tag="s_psum", bufs=1)
+        for g in range(PASSES):
+            nc.tensor.transpose(s_psum[:, g, :], s_rows[:, g, :], ident[:])
+        s_cols = keep.tile([P, PASSES, 4 * PACK], F32, name="s_cols")
+        nc.scalar.copy(out=s_cols[:], in_=s_psum[:, :, 0 : 4 * PACK])
+        bias = keep.tile([P, J], F32, name="bias", align_bytes=64)
+        for jh in range(J // HALF):
+            spread = psum.tile([P, HALF], F32, name="spread", tag="scores")
+            for c in range(HALF // P):
+                col = 2 * PACK + jh * (HALF // P) + c
+                nc.tensor.transpose(spread[:, c * P : (c + 1) * P], s_cols[:, 0, col : col + 1].to_broadcast([P, P]), ident[:])
+            nc.scalar.copy(out=bias[:, jh * HALF : (jh + 1) * HALF], in_=spread[:])
+
+        vb_words = keep.tile([P, J], U32, name="vb_words", align_bytes=64)
+        va_words = keep.tile([P, M], U32, name="va_words", align_bytes=64)
 
         def gather_words(dst, table, offsets, h):
             gather(dst[:, h * HALF : (h + 1) * HALF], table[:].bitcast(U32), offsets[:, h * HALF // 16 : (h + 1) * HALF // 16])
 
         for h in range(2):
             gather_words(vb_words, table_b, list_b, h)
-        va_scales = keep.tile([P, M], U8, name="va_scales", tag="slot_a", align_bytes=64)
-        gather(va_scales[:], plane_a[:].bitcast(U8), list_a[:])
-        wa_raw = keep.tile([P, R], I32, name="wa_raw", tag="slot_c", align_bytes=64)
-        nc.sync.dma_start(out=wa_raw[:], in_=words_of(wa_words))
-
-
-        def hidden(dst, w_words, w_scales, g, v_words, v_scales, first_row, n):
-            cols = slice(n * P, (n + 1) * P)
-            bank = psum.tile([P, PACK, P], F32, name="bank", tag="hidden", bufs=3)
-            for t in range(PACK):
-                nc.tensor.matmul_mx(
-                    out=bank[:, t, :],
-                    lhsT=w_words[:, g, t * P : (t + 1) * P].bitcast(FP8X4),
-                    lhsT_scale=w_scales[:, g, t * P : (t + 1) * P],
-                    rhs=v_words[:, cols].bitcast(FP8X4),
-                    rhs_scale=v_scales[first_row:P, cols],
-                    start=True,
-                    stop=True,
-                )
-            nc.scalar.activation(dst, bank[:].rearrange("p t n -> p n t"), SILU)
-
-        hb_words = keep.tile([P, PASSES, J], U32, name="hb_words", align_bytes=64)
-        hb_scales = keep.tile([P, PASSES, J], U8, name="hb_scales", align_bytes=64)
-
-        def b_act(g, c):
-            act = ring.tile([P, 2, P, PACK], F32, name="act", tag="act", bufs=5)
-            for u in range(2):
-                hidden(act[:, u], wb_words, wb_scales, g, vb_words, vb_scales, 0, 2 * c + u)
-            return act
-
-        def scale(engine, factors, h, act):
-            engine.tensor_tensor(out=h, in0=act, in1=factors.unsqueeze(1).to_broadcast(list(h.shape)), op=MULT)
-
-        def b_front(g, c):
-            act = b_act(g, c)[:].rearrange("p u n t -> p (u n) t")
-            h = ring.tile([P, 2 * P, PACK], BF16, name="h", tag="h", bufs=3, align_bytes=64)
-            cut = 2 * P - B_POOL
-            if B_POOL:
-                scale(nc.gpsimd, s_cols[:, g, PACK : 2 * PACK], h[:, cut:], act[:, cut:])
-            scale(nc.vector, s_psum[:, g, PACK : 2 * PACK], h[:, :cut], act[:, :cut])
-            return h
-
-        def b_back(g, c, h):
-            cols = slice(c * 2 * P, (c + 1) * 2 * P)
-            nc.vector.quantize_mx(
-                out=hb_words[:, g, cols].bitcast(FP8X4), scales=hb_scales[:, g, cols], in_=h[:].rearrange("p n t -> p (n t)")
-            )
 
         wa_sorted = keep.tile([P, PASSES, HALF], I32, name="wa_sorted", align_bytes=64)
         wa_sorted_scales = keep.tile([P, PASSES, HALF // 4], I32, name="wa_sorted_scales", align_bytes=64)
 
         def sort_wa():
-            for g in range(PASSES):
-                nc.vector.tensor_copy(
-                    out=wa_sorted[:, g, :].rearrange("p (t q i) -> p t q i", t=PACK, i=8),
-                    in_=wa_raw[:, g * HALF : (g + 1) * HALF].rearrange("p (q t i) -> p t q i", t=PACK, i=8),
-                )
-                nc.vector.tensor_copy(
-                    out=wa_sorted_scales[:, g, :].rearrange("p (t q i) -> p t q i", t=PACK, i=2),
-                    in_=wa_plane[:, g * HALF // 4 : (g + 1) * HALF // 4].rearrange("p (q t i) -> p t q i", t=PACK, i=2),
-                )
+            nc.vector.tensor_copy(
+                out=wa_sorted[:].rearrange("p g (t q i) -> p g t q i", t=PACK, i=8),
+                in_=wa_raw[:].rearrange("p (g q t i) -> p g t q i", g=PASSES, t=PACK, i=8),
+            )
+            nc.vector.tensor_copy(
+                out=wa_sorted_scales[:].rearrange("p g (t q i) -> p g t q i", t=PACK, i=2),
+                in_=wa_plane[:].rearrange("p (g q t i) -> p g t q i", g=PASSES, t=PACK, i=2),
+            )
 
-        b_steps = [(g, c) for g in range(PASSES) for c in range(J // (2 * P))]
-        hs = {0: b_front(*b_steps[0]), 1: b_front(*b_steps[1])}
-        quantise_wb(1, wb_raw1)
-        va_words = keep.tile([P, M], U32, name="va_words", tag="slot_g1", align_bytes=64)
-        bias = keep.tile([P, J], F32, name="bias", tag="slot_d", align_bytes=64)
-        nc.sync.dma_start(out=bias[:], in_=b.partition_broadcast(P))
-        for step, (g, c) in enumerate(b_steps):
-            b_back(g, c, hs[step])
-            if step + 2 < len(b_steps):
-                hs[step + 2] = b_front(*b_steps[step + 2])
-            if step == 4:
-                sort_wa()
-                gather_words(va_words, table_a, list_a, 0)
+        towers = {
+            "a": (0, wa_sorted, wa_sorted_scales[:].bitcast(U8), va_words, va_plane[:].bitcast(U8)),
+            "b": (1, wb_words, wb_scales, vb_words, vb_plane[:].bitcast(U8)),
+        }
 
-        wa_scale_bytes = wa_sorted_scales[:].bitcast(U8)
+        def front(tower, first, width, pool_share):
+            side, w_words, w_scales, v_words, v_scales = towers[tower]
+            act = ring.tile([P, PASSES, width, PACK], F32, name="act", tag="act", bufs=4)
+            for g in reversed(range(PASSES)):
+                for u in range(width // P):
+                    cols = slice(first + u * P, first + (u + 1) * P)
+                    bank = psum.tile([P, PACK, P], F32, name="bank", tag="hidden", bufs=3)
+                    for t in range(PACK):
+                        nc.tensor.matmul_mx(
+                            out=bank[:, t, :],
+                            lhsT=w_words[:, g, t * P : (t + 1) * P].bitcast(FP8X4),
+                            lhsT_scale=w_scales[:, g, t * P : (t + 1) * P],
+                            rhs=v_words[:, cols].bitcast(FP8X4),
+                            rhs_scale=v_scales[:, cols],
+                            start=True,
+                            stop=True,
+                        )
+                    nc.scalar.activation(act[:, g, u * P : (u + 1) * P], bank[:].rearrange("p t n -> p n t"), SILU)
+            h = [
+                ring.tile([P, width, PACK], BF16, name="h0", tag="h0", bufs=2, align_bytes=64),
+                ring.tile([P, width, PACK], BF16, name="h1", tag="h1", bufs=1, align_bytes=64),
+            ]
 
-        def a_front(mt):
-            act = ring.tile([P, PASSES, P, PACK], F32, name="act", tag="act", bufs=5)
-            for g in range(PASSES):
-                hidden(act[:, g], wa_sorted, wa_scale_bytes, g, va_words, va_scales, A_ROW, mt)
-            h = ring.tile([P, PASSES, P, PACK], BF16, name="ha", tag="ha", bufs=2, align_bytes=64)
-            cut = P - A_POOL[mt]
-            for engine, factors, cols in ((nc.gpsimd, s_cols, slice(cut, P)), (nc.vector, s_psum, slice(0, cut))):
-                if cols.stop > cols.start:
+            def scale(engine, factors, g, lo, hi):
+                if hi > lo:
+                    four = factors[:, g, PACK * side : PACK * (side + 1)]
                     engine.tensor_tensor(
-                        out=h[:, :, cols],
-                        in0=act[:, :, cols],
-                        in1=factors[:, :, 0:PACK].unsqueeze(2).to_broadcast([P, PASSES, cols.stop - cols.start, PACK]),
-                        op=MULT,
+                        out=h[g][:, lo:hi], in0=act[:, g, lo:hi], in1=four.unsqueeze(1).to_broadcast([P, hi - lo, PACK]), op=MULT
                     )
+
+            cut = PASSES * width - pool_share
+            for g in reversed(range(PASSES)):
+                scale(nc.gpsimd, s_cols, g, max(cut - g * width, 0), width)
+            for g in reversed(range(PASSES)):
+                scale(nc.vector, s_psum, g, 0, min(cut - g * width, width))
             return h
 
-        def a_back(h):
-            words = ring.tile([P, PASSES * P], U32, name="ha_words", tag="ha_words", align_bytes=64)
-            scales = ring.tile([P, PASSES * P], U8, name="ha_scales", tag="ha_scales", align_bytes=64)
-            nc.vector.quantize_mx(out=words[:].bitcast(FP8X4), scales=scales[:], in_=h[:].rearrange("p g n t -> p (g n t)"))
-            return words, scales
+        def quantise(h, words, scales):
+            for g in reversed(range(PASSES)):
+                nc.vector.quantize_mx(out=words[g].bitcast(FP8X4), scales=scales[g], in_=h[g][:].rearrange("p n t -> p (n t)"))
+
+        hb_words = keep.tile([P, PASSES, J], U32, name="hb_words", align_bytes=64)
+        hb_scales = keep.tile([P, PASSES, J], U8, name="hb_scales", align_bytes=64)
 
         def scores(mt, words, scales):
             for jh in range(J // HALF):
@@ -225,25 +210,42 @@ def tile_list_biaff_silu_bias_kernel(
                 for g in range(PASSES):
                     nc.tensor.matmul_mx(
                         out=acc[:],
-                        lhsT=words[:, g * P : (g + 1) * P].bitcast(FP8X4),
-                        lhsT_scale=scales[:, g * P : (g + 1) * P],
+                        lhsT=words[g].bitcast(FP8X4),
+                        lhsT_scale=scales[g],
                         rhs=hb_words[:, g, cols].bitcast(FP8X4),
                         rhs_scale=hb_scales[:, g, cols],
                         start=(g == 0),
                         stop=(g == PASSES - 1),
                     )
-                res = ring.tile([P, HALF], F32, name="res", tag="res", bufs=6)
+                res = ring.tile([P, HALF], F32, name="res", tag="res", bufs=8)
                 nc.vector.scalar_tensor_tensor(out=res[:], in0=acc[:], scalar=OUT_SCALE, in1=bias[:, cols], op0=MULT, op1=ADD)
                 nc.sync.dma_start(out=out[mt * P : (mt + 1) * P, cols], in_=res[:])
 
-        tiles = M // P
-        hs = {0: a_front(0), 1: a_front(1)}
-        gather_words(va_words, table_a, list_a, 1)
-        qs = {}
-        for step in range(tiles + 1):
-            if step < tiles:
-                qs[step] = a_back(hs[step])
-            if step >= 1:
-                scores(step - 1, *qs[step - 1])
-            if step + 2 < tiles:
-                hs[step + 2] = a_front(step + 2)
+        steps = []
+        for tower, widths in (("b", B_STEPS), ("a", A_STEPS)):
+            first = 0
+            for width, pool_share in widths:
+                steps.append((tower, first, width, pool_share))
+                first = first + width
+
+        h = front(*steps[0])
+        for n, (tower, first, width, pool_share) in enumerate(steps):
+            if tower == "b":
+                words = [hb_words[:, g, first : first + width] for g in range(PASSES)]
+                scales = [hb_scales[:, g, first : first + width] for g in range(PASSES)]
+            else:
+                ha_words = ring.tile([P, PASSES, width], U32, name="ha_words", tag="ha_words", align_bytes=64)
+                ha_scales = ring.tile([P, PASSES, width], U8, name="ha_scales", tag="ha_scales", align_bytes=64)
+                words = [ha_words[:, g, :] for g in range(PASSES)]
+                scales = [ha_scales[:, g, :] for g in range(PASSES)]
+            quantise(h, words, scales)
+            if n in (2, 3):
+                gather_words(va_words, table_a, list_a, n - 2)
+            if n == 3:
+                sort_wa()
+            if n + 1 < len(steps):
+                h = front(*steps[n + 1])
+            if tower == "a":
+                for u in range(width // P):
+                    own = slice(u * P, (u + 1) * P)
+                    scores(first // P + u, [w[:, own] for w in words], [s[:, own] for s in scales])

@@ -16,6 +16,7 @@ FP8X4 = mybir.dt.float8_e4m3fn_x4
 MULT = mybir.AluOpType.mult
 ADD = mybir.AluOpType.add
 SILU = mybir.ActivationFunctionType.Silu
+COPY = mybir.ActivationFunctionType.Copy
 
 P = 128
 PACK = 4
@@ -23,8 +24,21 @@ PASSES = R // (P * PACK)
 HALF = 512
 OUT_SCALE = 0.03125
 SCALE_ROWS = K // 32
-B_STEPS = ((128, 48), (128, 48), (256, 128), (256, 128), (256, 128))
-A_STEPS = ((256, 128), (256, 304), (256, 304), (128, 176), (128, 136))
+RUN = 32
+B_STEPS = (
+    (((0, 0), (0, 128)), 128, 32, 0),
+    (((0, 256), (0, 384)), 128, 32, 0),
+    (((0, 512), (0, 768)), 256, 128, 0),
+    (((1, 0), (1, 256)), 256, 128, 0),
+    (((1, 512), (1, 768)), 256, 128, 0),
+)
+A_STEPS = (
+    (((0, 0), (1, 0)), 256, 96, 256),
+    (((0, 256), (1, 256)), 256, 256, 128),
+    (((0, 512), (1, 512)), 256, 256, 128),
+    (((0, 768), (1, 768)), 128, 160, 0),
+    (((0, 896), (1, 896)), 128, 128, 0),
+)
 
 
 def tile_list_biaff_silu_bias_kernel(
@@ -53,12 +67,12 @@ def tile_list_biaff_silu_bias_kernel(
         nc.sync.dma_start(list_b[:], offs2)
         nc.sync.dma_start(list_a[:], offs)
 
-        def load_wb(g):
-            raw = keep.tile([P, PACK, HALF], F32, name="wb_raw%d" % g, tag="raw%d" % g, align_bytes=64)
+        def load_wb(g, tag):
+            raw = keep.tile([P, PACK, HALF], F32, name="wb_raw%d" % g, tag=tag, align_bytes=64)
             nc.sync.dma_start(out=raw[:], in_=wb[:, g * HALF : (g + 1) * HALF].rearrange("(p j) c -> p j c", j=PACK))
             return raw
 
-        wb_raw = [load_wb(0)]
+        wb_raw = [load_wb(0, "raw0")]
         rows_b = zeroed("rows_b", [P, T // 4], I32)
         nc.sync.dma_start(out=rows_b[0:P:8, :], in_=tab2_scales[0].bitcast(I32))
         rows_a = zeroed("rows_a", [P, T // 4], I32)
@@ -70,7 +84,6 @@ def tile_list_biaff_silu_bias_kernel(
                 in_=vec.rearrange("(gq t i) -> t gq i", t=PACK, i=8),
             )
         nc.sync.dma_start(out=s_rows[2 * PACK : 2 * PACK + J // P, 0, :], in_=b.rearrange("(c p) -> c p", p=P))
-        wb_raw.append(load_wb(1))
         table_b = keep.tile([P, T], I32, name="table_b", align_bytes=64)
         nc.sync.dma_start(out=table_b[:], in_=words_of(tab2_words))
 
@@ -83,7 +96,7 @@ def tile_list_biaff_silu_bias_kernel(
         va_plane = zeroed("va_plane", [P, M // 4], I32)
 
         def gather_scales(name, rows, first, offsets, plane, engine):
-            picked = keep.tile([P, J], U8, name=name, align_bytes=64)
+            picked = keep.tile([P, J], U8, name=name, tag=name, align_bytes=64)
             gather(picked[:], rows[:].bitcast(U8), offsets[:])
             for r in range(4):
                 engine.dma_start(out=plane[r:P:32, :], in_=picked[:].bitcast(I32)[first + 8 * r : P : 32, :])
@@ -106,8 +119,9 @@ def tile_list_biaff_silu_bias_kernel(
             )
 
         grouped0 = cast_wb(0)
-        gather_scales("picked_b", rows_b, 0, list_b, vb_plane, nc.scalar)
-        wa_raw = keep.tile([P, R], I32, name="wa_raw", tag="rows_b", align_bytes=64)
+        gather_scales("picked_b", rows_b, 0, list_b, vb_plane, nc.sync)
+        wb_raw.append(load_wb(1, "rows_b"))
+        wa_raw = keep.tile([P, R], I32, name="wa_raw", align_bytes=64, tag="picked_b")
         nc.sync.dma_start(out=wa_raw[:], in_=words_of(wa_words))
         table_a = keep.tile([P, T], I32, name="table_a", tag="raw0", align_bytes=64)
         nc.sync.dma_start(out=table_a[:], in_=words_of(tab_words))
@@ -124,6 +138,12 @@ def tile_list_biaff_silu_bias_kernel(
             nc.tensor.transpose(s_psum[:, g, :], s_rows[:, g, :], ident[:])
         s_cols = keep.tile([P, PASSES, 4 * PACK], F32, name="s_cols")
         nc.scalar.copy(out=s_cols[:], in_=s_psum[:, :, 0 : 4 * PACK])
+        s_runs = keep.tile([P, PASSES, 2, RUN, PACK], F32, name="s_runs")
+        for g in range(PASSES):
+            nc.scalar.copy(
+                out=s_runs[:, g],
+                in_=s_psum[:, g, 0 : 2 * PACK].rearrange("p (s t) -> p s t", t=PACK).unsqueeze(2).to_broadcast([P, 2, RUN, PACK]),
+            )
         bias = keep.tile([P, J], F32, name="bias", align_bytes=64)
         for jh in range(J // HALF):
             spread = psum.tile([P, HALF], F32, name="spread", tag="scores")
@@ -159,10 +179,13 @@ def tile_list_biaff_silu_bias_kernel(
             "b": (1, wb_words, wb_scales, vb_words, vb_plane[:].bitcast(U8)),
         }
 
-        def front(tower, first, width, pool_share):
+        def front(tower, slabs, width, pool_share, scalar_share, takes_over=None):
             side, w_words, w_scales, v_words, v_scales = towers[tower]
-            act = ring.tile([P, PASSES, width, PACK], F32, name="act", tag="act", bufs=4)
-            for g in reversed(range(PASSES)):
+            act = ring.tile([P, 2, width, PACK], F32, name="act", tag="act_" + tower, bufs=4 if tower == "b" else 2)
+            if scalar_share:
+                planes = ring.tile([P, PACK, scalar_share], F32, name="planes", tag="planes", bufs=2)
+            for k in (1, 0):
+                g, first = slabs[k]
                 for u in range(width // P):
                     cols = slice(first + u * P, first + (u + 1) * P)
                     bank = psum.tile([P, PACK, P], F32, name="bank", tag="hidden", bufs=3)
@@ -176,34 +199,57 @@ def tile_list_biaff_silu_bias_kernel(
                             start=True,
                             stop=True,
                         )
-                    nc.scalar.activation(act[:, g, u * P : (u + 1) * P], bank[:].rearrange("p t n -> p n t"), SILU)
-            h = [
-                ring.tile([P, width, PACK], BF16, name="h0", tag="h0", bufs=2, align_bytes=64),
-                ring.tile([P, width, PACK], BF16, name="h1", tag="h1", bufs=1, align_bytes=64),
-            ]
+                    if k == 0 and u * P < scalar_share:
+                        nc.scalar.activation(planes[:, :, u * P : (u + 1) * P], bank[:], SILU)
+                    else:
+                        nc.scalar.activation(act[:, k, u * P : (u + 1) * P], bank[:].rearrange("p t n -> p n t"), SILU)
+            if takes_over:
+                h0 = keep.tile([P, width, PACK], BF16, name="h0", tag=takes_over, align_bytes=64)
+            else:
+                h0 = ring.tile([P, width, PACK], BF16, name="h0", tag="h0", bufs=3, align_bytes=64)
+            h = [h0, ring.tile([P, width, PACK], BF16, name="h1", tag="h1", bufs=1, align_bytes=64)]
 
-            def scale(engine, factors, g, lo, hi):
+            def scale(engine, factors, k, lo, hi):
                 if hi > lo:
-                    four = factors[:, g, PACK * side : PACK * (side + 1)]
+                    four = factors[:, slabs[k][0], PACK * side : PACK * (side + 1)]
                     engine.tensor_tensor(
-                        out=h[g][:, lo:hi], in0=act[:, g, lo:hi], in1=four.unsqueeze(1).to_broadcast([P, hi - lo, PACK]), op=MULT
+                        out=h[k][:, lo:hi], in0=act[:, k, lo:hi], in1=four.unsqueeze(1).to_broadcast([P, hi - lo, PACK]), op=MULT
                     )
 
-            cut = PASSES * width - pool_share
-            for g in reversed(range(PASSES)):
-                scale(nc.gpsimd, s_cols, g, max(cut - g * width, 0), width)
-            for g in reversed(range(PASSES)):
-                scale(nc.vector, s_psum, g, 0, min(cut - g * width, width))
+            if scalar_share:
+                scaled = ring.tile([P, PACK, scalar_share], BF16, name="scaled", tag="scaled", bufs=3)
+                for t in range(PACK):
+                    col = PACK * side + t
+                    nc.scalar.activation(scaled[:, t], planes[:, t], COPY, scale=s_cols[:, slabs[0][0], col : col + 1])
+                nc.scalar.copy(out=h[0][:, 0:scalar_share], in_=scaled[:].rearrange("p t n -> p n t"))
+            cut = 2 * width - pool_share
+            for k in (1, 0):
+                lo = max(cut - k * width, 0)
+                if lo < width:
+                    run = s_runs[:, slabs[k][0], side].rearrange("p n t -> p (n t)")
+                    nc.gpsimd.tensor_tensor(
+                        out=h[k][:, lo:].rearrange("p (c n) t -> p c (n t)", n=RUN),
+                        in0=act[:, k, lo:].rearrange("p (c n) t -> p c (n t)", n=RUN),
+                        in1=run.unsqueeze(1).to_broadcast([P, (width - lo) // RUN, RUN * PACK]),
+                        op=MULT,
+                    )
+            for k in (1, 0):
+                scale(nc.vector, s_psum, k, scalar_share if k == 0 else 0, min(cut - k * width, width))
             return h
 
         def quantise(h, words, scales):
-            for g in reversed(range(PASSES)):
-                nc.vector.quantize_mx(out=words[g].bitcast(FP8X4), scales=scales[g], in_=h[g][:].rearrange("p n t -> p (n t)"))
+            for k in (1, 0):
+                nc.vector.quantize_mx(out=words[k].bitcast(FP8X4), scales=scales[k], in_=h[k][:].rearrange("p n t -> p (n t)"))
 
         hb_words = keep.tile([P, PASSES, J], U32, name="hb_words", align_bytes=64)
         hb_scales = keep.tile([P, PASSES, J], U8, name="hb_scales", align_bytes=64)
 
-        def scores(mt, words, scales):
+        def finish(mt, cols, acc):
+            res = ring.tile([P, HALF], F32, name="res", tag="res", bufs=8)
+            nc.vector.scalar_tensor_tensor(out=res[:], in0=acc[:], scalar=OUT_SCALE, in1=bias[:, cols], op0=MULT, op1=ADD)
+            nc.sync.dma_start(out=out[mt * P : (mt + 1) * P, cols], in_=res[:])
+
+        def scores(mt, words, scales, hold_last):
             for jh in range(J // HALF):
                 cols = slice(jh * HALF, (jh + 1) * HALF)
                 acc = psum.tile([P, HALF], F32, name="acc", tag="scores")
@@ -217,35 +263,34 @@ def tile_list_biaff_silu_bias_kernel(
                         start=(g == 0),
                         stop=(g == PASSES - 1),
                     )
-                res = ring.tile([P, HALF], F32, name="res", tag="res", bufs=8)
-                nc.vector.scalar_tensor_tensor(out=res[:], in0=acc[:], scalar=OUT_SCALE, in1=bias[:, cols], op0=MULT, op1=ADD)
-                nc.sync.dma_start(out=out[mt * P : (mt + 1) * P, cols], in_=res[:])
+                if hold_last and jh == J // HALF - 1:
+                    return (mt, cols, acc)
+                finish(mt, cols, acc)
+            return None
 
-        steps = []
-        for tower, widths in (("b", B_STEPS), ("a", A_STEPS)):
-            first = 0
-            for width, pool_share in widths:
-                steps.append((tower, first, width, pool_share))
-                first = first + width
-
+        steps = [("b",) + step for step in B_STEPS] + [("a",) + step for step in A_STEPS]
+        held = None
         h = front(*steps[0])
-        for n, (tower, first, width, pool_share) in enumerate(steps):
+        for n, (tower, slabs, width, pool_share, scalar_share) in enumerate(steps):
             if tower == "b":
-                words = [hb_words[:, g, first : first + width] for g in range(PASSES)]
-                scales = [hb_scales[:, g, first : first + width] for g in range(PASSES)]
+                words = [hb_words[:, g, first : first + width] for g, first in slabs]
+                scales = [hb_scales[:, g, first : first + width] for g, first in slabs]
             else:
-                ha_words = ring.tile([P, PASSES, width], U32, name="ha_words", tag="ha_words", align_bytes=64)
-                ha_scales = ring.tile([P, PASSES, width], U8, name="ha_scales", tag="ha_scales", align_bytes=64)
+                ha_words = ring.tile([P, PASSES, width], U32, name="ha_words", tag="ha_words", bufs=1, align_bytes=64)
+                ha_scales = ring.tile([P, PASSES, width], U8, name="ha_scales", tag="ha_scales", bufs=1, align_bytes=64)
                 words = [ha_words[:, g, :] for g in range(PASSES)]
                 scales = [ha_scales[:, g, :] for g in range(PASSES)]
             quantise(h, words, scales)
-            if n in (2, 3):
-                gather_words(va_words, table_a, list_a, n - 2)
-            if n == 3:
+            if held:
+                finish(*held)
+            if n == 0:
+                for half in range(2):
+                    gather_words(va_words, table_a, list_a, half)
                 sort_wa()
             if n + 1 < len(steps):
-                h = front(*steps[n + 1])
+                h = front(*steps[n + 1], takes_over={1: "rows_a"}.get(n))
             if tower == "a":
                 for u in range(width // P):
                     own = slice(u * P, (u + 1) * P)
-                    scores(first // P + u, [w[:, own] for w in words], [s[:, own] for s in scales])
+                    hold_last = u == width // P - 1 and n + 1 < len(steps)
+                    held = scores(slabs[0][1] // P + u, [w[:, own] for w in words], [s[:, own] for s in scales], hold_last)

@@ -26,14 +26,14 @@ OUT_SCALE = 0.03125
 SCALE_ROWS = K // 32
 RUN = 32
 B_STEPS = (
-    (((0, 0), (0, 128)), 128, 32, 0),
-    (((0, 256), (0, 384)), 128, 32, 0),
+    (((0, 0), (0, 128)), 128, 0, 0),
+    (((0, 256), (0, 384)), 128, 0, 0),
     (((0, 512), (0, 768)), 256, 128, 0),
     (((1, 0), (1, 256)), 256, 128, 0),
     (((1, 512), (1, 768)), 256, 128, 0),
 )
 A_STEPS = (
-    (((0, 0), (1, 0)), 256, 96, 256),
+    (((0, 0), (1, 0)), 256, 128, 128),
     (((0, 256), (1, 256)), 256, 256, 128),
     (((0, 512), (1, 512)), 256, 256, 128),
     (((0, 768), (1, 768)), 128, 160, 0),
@@ -67,12 +67,11 @@ def tile_list_biaff_silu_bias_kernel(
         nc.sync.dma_start(list_b[:], offs2)
         nc.sync.dma_start(list_a[:], offs)
 
-        def load_wb(g, tag):
-            raw = keep.tile([P, PACK, HALF], F32, name="wb_raw%d" % g, tag=tag, align_bytes=64)
+        def load_wb(g, raw):
             nc.sync.dma_start(out=raw[:], in_=wb[:, g * HALF : (g + 1) * HALF].rearrange("(p j) c -> p j c", j=PACK))
             return raw
 
-        wb_raw = [load_wb(0, "raw0")]
+        wb_raw = [load_wb(0, keep.tile([P, PACK, HALF], F32, name="wb_raw0", tag="raw0", align_bytes=64))]
         rows_b = zeroed("rows_b", [P, T // 4], I32)
         nc.sync.dma_start(out=rows_b[0:P:8, :], in_=tab2_scales[0].bitcast(I32))
         rows_a = zeroed("rows_a", [P, T // 4], I32)
@@ -83,23 +82,23 @@ def tile_list_biaff_silu_bias_kernel(
                 out=s_rows[PACK * side : PACK * (side + 1)].rearrange("t g (q i) -> t (g q) i", i=8),
                 in_=vec.rearrange("(gq t i) -> t gq i", t=PACK, i=8),
             )
-        nc.sync.dma_start(out=s_rows[2 * PACK : 2 * PACK + J // P, 0, :], in_=b.rearrange("(c p) -> c p", p=P))
         table_b = keep.tile([P, T], I32, name="table_b", align_bytes=64)
         nc.sync.dma_start(out=table_b[:], in_=words_of(tab2_words))
 
         ident = zeroed("ident", [P, P], F32)
         make_identity(nc, ident[:], nomemset=True)
-        warm = keep.tile([P, 1], F32, name="warm")
-        nc.scalar.activation(warm[:], ident[:, 0:1], SILU)
 
         vb_plane = zeroed("vb_plane", [P, J // 4], I32)
         va_plane = zeroed("va_plane", [P, M // 4], I32)
 
-        def gather_scales(name, rows, first, offsets, plane, engine):
+        def gather_scales(name, rows, offsets):
             picked = keep.tile([P, J], U8, name=name, tag=name, align_bytes=64)
             gather(picked[:], rows[:].bitcast(U8), offsets[:])
+            return picked
+
+        def move_scales(picked, first, plane):
             for r in range(4):
-                engine.dma_start(out=plane[r:P:32, :], in_=picked[:].bitcast(I32)[first + 8 * r : P : 32, :])
+                nc.sync.dma_start(out=plane[r:P:32, :], in_=picked[:].bitcast(I32)[first + 8 * r : P : 32, :])
 
         wb_words = keep.tile([P, PASSES, HALF], U32, name="wb_words", align_bytes=64)
         wb_scales = keep.tile([P, PASSES, HALF], U8, name="wb_scales", align_bytes=64)
@@ -119,25 +118,24 @@ def tile_list_biaff_silu_bias_kernel(
             )
 
         grouped0 = cast_wb(0)
-        gather_scales("picked_b", rows_b, 0, list_b, vb_plane, nc.sync)
-        wb_raw.append(load_wb(1, "rows_b"))
+        move_scales(gather_scales("picked_b", rows_b, list_b), 0, vb_plane)
+        wb_raw.append(load_wb(1, keep.tile([P, PACK, HALF], F32, name="wb_raw1", tag="rows_b", align_bytes=64)))
+        picked_a = gather_scales("picked_a", rows_a, list_a)
         wa_raw = keep.tile([P, R], I32, name="wa_raw", align_bytes=64, tag="picked_b")
         nc.sync.dma_start(out=wa_raw[:], in_=words_of(wa_words))
-        table_a = keep.tile([P, T], I32, name="table_a", tag="raw0", align_bytes=64)
-        nc.sync.dma_start(out=table_a[:], in_=words_of(tab_words))
-        grouped1 = cast_wb(1)
-        gather_scales("picked_a", rows_a, 4, list_a, va_plane, nc.sync)
-        wa_plane = zeroed("wa_plane", [P, R // 4], I32, tag="rows_a")
+        wa_plane = zeroed("wa_plane", [P, R // 4], I32)
         for r in range(4):
             nc.sync.dma_start(out=wa_plane[r:P:32, :], in_=wa_scales[0].bitcast(I32)[r:SCALE_ROWS:4, :])
+        table_a = keep.tile([P, T], I32, name="table_a", tag="raw0", align_bytes=64)
+        nc.sync.dma_start(out=table_a[:], in_=words_of(tab_words))
+        move_scales(picked_a, 4, va_plane)
         quantise_wb(0, grouped0)
-        quantise_wb(1, grouped1)
 
         s_psum = psum.tile([P, PASSES, P], F32, name="s_psum", tag="s_psum", bufs=1)
         for g in range(PASSES):
             nc.tensor.transpose(s_psum[:, g, :], s_rows[:, g, :], ident[:])
-        s_cols = keep.tile([P, PASSES, 4 * PACK], F32, name="s_cols")
-        nc.scalar.copy(out=s_cols[:], in_=s_psum[:, :, 0 : 4 * PACK])
+        s_cols = keep.tile([P, PASSES, 2 * PACK], F32, name="s_cols")
+        nc.scalar.copy(out=s_cols[:], in_=s_psum[:, :, 0 : 2 * PACK])
         s_runs = keep.tile([P, PASSES, 2, RUN, PACK], F32, name="s_runs")
         for g in range(PASSES):
             nc.scalar.copy(
@@ -145,12 +143,7 @@ def tile_list_biaff_silu_bias_kernel(
                 in_=s_psum[:, g, 0 : 2 * PACK].rearrange("p (s t) -> p s t", t=PACK).unsqueeze(2).to_broadcast([P, 2, RUN, PACK]),
             )
         bias = keep.tile([P, J], F32, name="bias", align_bytes=64)
-        for jh in range(J // HALF):
-            spread = psum.tile([P, HALF], F32, name="spread", tag="scores")
-            for c in range(HALF // P):
-                col = 2 * PACK + jh * (HALF // P) + c
-                nc.tensor.transpose(spread[:, c * P : (c + 1) * P], s_cols[:, 0, col : col + 1].to_broadcast([P, P]), ident[:])
-            nc.scalar.copy(out=bias[:, jh * HALF : (jh + 1) * HALF], in_=spread[:])
+        nc.sync.dma_start(out=bias[:], in_=b.partition_broadcast(P))
 
         vb_words = keep.tile([P, J], U32, name="vb_words", align_bytes=64)
         va_words = keep.tile([P, M], U32, name="va_words", align_bytes=64)
@@ -181,12 +174,12 @@ def tile_list_biaff_silu_bias_kernel(
 
         def front(tower, slabs, width, pool_share, scalar_share, takes_over=None):
             side, w_words, w_scales, v_words, v_scales = towers[tower]
-            act = ring.tile([P, 2, width, PACK], F32, name="act", tag="act_" + tower, bufs=4 if tower == "b" else 2)
+            act = ring.tile([P, 2, width, PACK], F32, name="act", tag="act_%s%d" % (tower, width), bufs=3 if tower == "b" else 2)
             if scalar_share:
                 planes = ring.tile([P, PACK, scalar_share], F32, name="planes", tag="planes", bufs=2)
             for k in (1, 0):
                 g, first = slabs[k]
-                for u in range(width // P):
+                for u in reversed(range(width // P)):
                     cols = slice(first + u * P, first + (u + 1) * P)
                     bank = psum.tile([P, PACK, P], F32, name="bank", tag="hidden", bufs=3)
                     for t in range(PACK):
@@ -204,10 +197,14 @@ def tile_list_biaff_silu_bias_kernel(
                     else:
                         nc.scalar.activation(act[:, k, u * P : (u + 1) * P], bank[:].rearrange("p t n -> p n t"), SILU)
             if takes_over:
-                h0 = keep.tile([P, width, PACK], BF16, name="h0", tag=takes_over, align_bytes=64)
+                h0 = keep.tile([P, width, PACK], BF16, name="h0_late", tag="picked_a", align_bytes=64)
             else:
                 h0 = ring.tile([P, width, PACK], BF16, name="h0", tag="h0", bufs=3, align_bytes=64)
-            h = [h0, ring.tile([P, width, PACK], BF16, name="h1", tag="h1", bufs=1, align_bytes=64)]
+            if slabs[1][0] == 1:
+                h1 = keep.tile([P, width, PACK], BF16, name="h1_late", tag="raw0", align_bytes=64)
+            else:
+                h1 = ring.tile([P, width, PACK], BF16, name="h1", tag="h1", bufs=1, align_bytes=64)
+            h = [h0, h1]
 
             def scale(engine, factors, k, lo, hi):
                 if hi > lo:
@@ -284,11 +281,12 @@ def tile_list_biaff_silu_bias_kernel(
             if held:
                 finish(*held)
             if n == 0:
-                for half in range(2):
-                    gather_words(va_words, table_a, list_a, half)
                 sort_wa()
+            if n == 2:
+                quantise_wb(1, cast_wb(1))
+                gather(va_words[:], table_a[:].bitcast(U32), list_a[:])
             if n + 1 < len(steps):
-                h = front(*steps[n + 1], takes_over={1: "rows_a"}.get(n))
+                h = front(*steps[n + 1], takes_over=(n == 2))
             if tower == "a":
                 for u in range(width // P):
                     own = slice(u * P, (u + 1) * P)

@@ -33,11 +33,11 @@ B_STEPS = (
     (((1, 512), (1, 768)), 256, 128, 0),
 )
 A_STEPS = (
-    (((0, 0), (1, 0)), 256, 128, 128),
-    (((0, 256), (1, 256)), 256, 256, 128),
+    (((0, 0), (1, 0)), 256, 128, 0),
+    (((0, 256), (1, 256)), 256, 256, 0),
     (((0, 512), (1, 512)), 256, 256, 128),
-    (((0, 768), (1, 768)), 128, 160, 0),
-    (((0, 896), (1, 896)), 128, 128, 0),
+    (((0, 768), (1, 768)), 128, 128, 128),
+    (((0, 896), (1, 896)), 128, 64, 128),
 )
 
 
@@ -104,7 +104,7 @@ def tile_list_biaff_silu_bias_kernel(
         wb_scales = keep.tile([P, PASSES, HALF], U8, name="wb_scales", align_bytes=64)
 
         def cast_wb(g):
-            grouped = keep.tile([P, PACK, 16, 8, PACK], BF16, name="wb_grouped%d" % g, align_bytes=64)
+            grouped = keep.tile([P, PACK, 16, 8, PACK], BF16, name="wb_grouped%d" % g, tag="grouped%d" % g, align_bytes=64)
             source = wb_raw[g][:].rearrange("p j (q t i) -> p t q i j", t=PACK, i=8)
             for t in range(PACK):
                 nc.scalar.copy(out=grouped[:, t], in_=source[:, t])
@@ -142,8 +142,6 @@ def tile_list_biaff_silu_bias_kernel(
                 out=s_runs[:, g],
                 in_=s_psum[:, g, 0 : 2 * PACK].rearrange("p (s t) -> p s t", t=PACK).unsqueeze(2).to_broadcast([P, 2, RUN, PACK]),
             )
-        bias = keep.tile([P, J], F32, name="bias", align_bytes=64)
-        nc.sync.dma_start(out=bias[:], in_=b.partition_broadcast(P))
 
         vb_words = keep.tile([P, J], U32, name="vb_words", align_bytes=64)
         va_words = keep.tile([P, M], U32, name="va_words", align_bytes=64)
@@ -197,7 +195,7 @@ def tile_list_biaff_silu_bias_kernel(
                     else:
                         nc.scalar.activation(act[:, k, u * P : (u + 1) * P], bank[:].rearrange("p t n -> p n t"), SILU)
             if takes_over:
-                h0 = keep.tile([P, width, PACK], BF16, name="h0_late", tag="picked_a", align_bytes=64)
+                h0 = keep.tile([P, width, PACK], BF16, name="h0_late", tag=takes_over, align_bytes=64)
             else:
                 h0 = ring.tile([P, width, PACK], BF16, name="h0", tag="h0", bufs=3, align_bytes=64)
             if slabs[1][0] == 1:
@@ -250,15 +248,15 @@ def tile_list_biaff_silu_bias_kernel(
             for jh in range(J // HALF):
                 cols = slice(jh * HALF, (jh + 1) * HALF)
                 acc = psum.tile([P, HALF], F32, name="acc", tag="scores")
-                for g in range(PASSES):
+                for g in reversed(range(PASSES)):
                     nc.tensor.matmul_mx(
                         out=acc[:],
                         lhsT=words[g].bitcast(FP8X4),
                         lhsT_scale=scales[g],
                         rhs=hb_words[:, g, cols].bitcast(FP8X4),
                         rhs_scale=hb_scales[:, g, cols],
-                        start=(g == 0),
-                        stop=(g == PASSES - 1),
+                        start=(g == PASSES - 1),
+                        stop=(g == 0),
                     )
                 if hold_last and jh == J // HALF - 1:
                     return (mt, cols, acc)
@@ -284,9 +282,11 @@ def tile_list_biaff_silu_bias_kernel(
                 sort_wa()
             if n == 2:
                 quantise_wb(1, cast_wb(1))
+                bias = keep.tile([P, J], F32, name="bias", tag="grouped1", align_bytes=64)
+                nc.sync.dma_start(out=bias[:], in_=b.partition_broadcast(P))
                 gather(va_words[:], table_a[:].bitcast(U32), list_a[:])
             if n + 1 < len(steps):
-                h = front(*steps[n + 1], takes_over=(n == 2))
+                h = front(*steps[n + 1], takes_over={0: "picked_b", 2: "picked_a"}.get(n))
             if tower == "a":
                 for u in range(width // P):
                     own = slice(u * P, (u + 1) * P)

@@ -24,21 +24,28 @@ PASSES = R // (P * PACK)
 HALF = 512
 OUT_SCALE = 0.03125
 SCALE_ROWS = K // 32
+BLOCK = 8
+A_FIRST = 4
 RUN = 32
+
+NARROW, WIDE = P, 2 * P
+POOL_BARE = WIDE // 2
 B_STEPS = (
-    (((0, 0), (0, 128)), 128, 0, 0),
-    (((0, 256), (0, 384)), 128, 0, 0),
-    (((0, 512), (0, 768)), 256, 128, 0),
-    (((1, 0), (1, 256)), 256, 128, 0),
-    (((1, 512), (1, 768)), 256, 128, 0),
+    (((0, 0), (0, NARROW)), NARROW, 0, 0),
+    (((0, 2 * NARROW), (0, 3 * NARROW)), NARROW, 0, 0),
+    (((0, HALF), (0, HALF + WIDE)), WIDE, POOL_BARE, 0),
+    (((1, 0), (1, WIDE)), WIDE, POOL_BARE, 0),
+    (((1, HALF), (1, HALF + WIDE)), WIDE, POOL_BARE, 0),
 )
 A_STEPS = (
-    (((0, 0), (1, 0)), 256, 128, 0),
-    (((0, 256), (1, 256)), 256, 256, 0),
-    (((0, 512), (1, 512)), 256, 256, 128),
-    (((0, 768), (1, 768)), 128, 128, 128),
-    (((0, 896), (1, 896)), 128, 64, 128),
+    (((0, 0), (1, 0)), WIDE, POOL_BARE, 0),
+    (((0, WIDE), (1, WIDE)), WIDE, WIDE, 0),
+    (((0, 2 * WIDE), (1, 2 * WIDE)), WIDE, WIDE, P),
+    (((0, 3 * WIDE), (1, 3 * WIDE)), NARROW, NARROW, P),
+    (((0, 3 * WIDE + NARROW), (1, 3 * WIDE + NARROW)), NARROW, 0, P),
 )
+SORT_AFTER = 0
+B_PASS0_END = 2
 
 
 def tile_list_biaff_silu_bias_kernel(
@@ -57,8 +64,8 @@ def tile_list_biaff_silu_bias_kernel(
         def gather(dst, window, offsets):
             nc.vector.tensor_copy(out=dst, in_=window.indirect(offsets))
 
-        def zeroed(name, shape, dtype, tag=None):
-            tile = keep.tile(shape, dtype, name=name, tag=tag or name, align_bytes=64)
+        def zeroed(name, shape, dtype):
+            tile = keep.tile(shape, dtype, name=name, tag=name, align_bytes=64)
             nc.vector.memset(tile[:], 0)
             return tile
 
@@ -67,20 +74,21 @@ def tile_list_biaff_silu_bias_kernel(
         nc.sync.dma_start(list_b[:], offs2)
         nc.sync.dma_start(list_a[:], offs)
 
-        def load_wb(g, raw):
-            nc.sync.dma_start(out=raw[:], in_=wb[:, g * HALF : (g + 1) * HALF].rearrange("(p j) c -> p j c", j=PACK))
+        def load_wb(g, tag):
+            raw = keep.tile([P, PACK, HALF], F32, name="wb_raw%d" % g, tag=tag, align_bytes=64)
+            nc.sync.dma_start(out=raw[:], in_=wb[:, g * HALF : (g + 1) * HALF].rearrange("(p i) c -> p i c", i=PACK))
             return raw
 
-        wb_raw = [load_wb(0, keep.tile([P, PACK, HALF], F32, name="wb_raw0", tag="raw0", align_bytes=64))]
+        wb_raw = [load_wb(0, "raw0")]
         rows_b = zeroed("rows_b", [P, T // 4], I32)
-        nc.sync.dma_start(out=rows_b[0:P:8, :], in_=tab2_scales[0].bitcast(I32))
+        nc.sync.dma_start(out=rows_b[0:P:BLOCK, :], in_=tab2_scales[0].bitcast(I32))
         rows_a = zeroed("rows_a", [P, T // 4], I32)
-        nc.sync.dma_start(out=rows_a[4:P:8, :], in_=tab_scales[0].bitcast(I32))
+        nc.sync.dma_start(out=rows_a[A_FIRST:P:BLOCK, :], in_=tab_scales[0].bitcast(I32))
         s_rows = zeroed("s_rows", [P, PASSES, P], F32)
         for side, vec in enumerate((sa, sb)):
             nc.sync.dma_start(
-                out=s_rows[PACK * side : PACK * (side + 1)].rearrange("t g (q i) -> t (g q) i", i=8),
-                in_=vec.rearrange("(gq t i) -> t gq i", t=PACK, i=8),
+                out=s_rows[PACK * side : PACK * (side + 1)].rearrange("t g (q i) -> t (g q) i", i=BLOCK),
+                in_=vec.rearrange("(gq t i) -> t gq i", t=PACK, i=BLOCK),
             )
         table_b = keep.tile([P, T], I32, name="table_b", align_bytes=64)
         nc.sync.dma_start(out=table_b[:], in_=words_of(tab2_words))
@@ -98,14 +106,16 @@ def tile_list_biaff_silu_bias_kernel(
 
         def move_scales(picked, first, plane):
             for r in range(4):
-                nc.sync.dma_start(out=plane[r:P:32, :], in_=picked[:].bitcast(I32)[first + 8 * r : P : 32, :])
+                nc.sync.dma_start(out=plane[r:P:32, :], in_=picked[:].bitcast(I32)[first + BLOCK * r : P : 32, :])
 
         wb_words = keep.tile([P, PASSES, HALF], U32, name="wb_words", align_bytes=64)
         wb_scales = keep.tile([P, PASSES, HALF], U8, name="wb_scales", align_bytes=64)
 
         def cast_wb(g):
-            grouped = keep.tile([P, PACK, 16, 8, PACK], BF16, name="wb_grouped%d" % g, tag="grouped%d" % g, align_bytes=64)
-            source = wb_raw[g][:].rearrange("p j (q t i) -> p t q i j", t=PACK, i=8)
+            grouped = keep.tile(
+                [P, PACK, P // BLOCK, BLOCK, PACK], BF16, name="wb_grouped%d" % g, tag="grouped%d" % g, align_bytes=64
+            )
+            source = wb_raw[g][:].rearrange("p k (q t i) -> p t q i k", t=PACK, i=BLOCK)
             for t in range(PACK):
                 nc.scalar.copy(out=grouped[:, t], in_=source[:, t])
             return grouped
@@ -114,28 +124,26 @@ def tile_list_biaff_silu_bias_kernel(
             nc.vector.quantize_mx(
                 out=wb_words[:, g, :].bitcast(FP8X4),
                 scales=wb_scales[:, g, :],
-                in_=grouped[:].rearrange("p t q i j -> p (t q i j)"),
+                in_=grouped[:].rearrange("p t q i k -> p (t q i k)"),
             )
 
         grouped0 = cast_wb(0)
         move_scales(gather_scales("picked_b", rows_b, list_b), 0, vb_plane)
-        wb_raw.append(load_wb(1, keep.tile([P, PACK, HALF], F32, name="wb_raw1", tag="rows_b", align_bytes=64)))
+        wb_raw.append(load_wb(1, "rows_b"))
         picked_a = gather_scales("picked_a", rows_a, list_a)
-        wa_raw = keep.tile([P, R], I32, name="wa_raw", align_bytes=64, tag="picked_b")
+        wa_raw = keep.tile([P, R], I32, name="wa_raw", tag="picked_b", align_bytes=64)
         nc.sync.dma_start(out=wa_raw[:], in_=words_of(wa_words))
         wa_plane = zeroed("wa_plane", [P, R // 4], I32)
         for r in range(4):
             nc.sync.dma_start(out=wa_plane[r:P:32, :], in_=wa_scales[0].bitcast(I32)[r:SCALE_ROWS:4, :])
         table_a = keep.tile([P, T], I32, name="table_a", tag="raw0", align_bytes=64)
         nc.sync.dma_start(out=table_a[:], in_=words_of(tab_words))
-        move_scales(picked_a, 4, va_plane)
+        move_scales(picked_a, A_FIRST, va_plane)
         quantise_wb(0, grouped0)
 
         s_psum = psum.tile([P, PASSES, P], F32, name="s_psum", tag="s_psum", bufs=1)
         for g in range(PASSES):
             nc.tensor.transpose(s_psum[:, g, :], s_rows[:, g, :], ident[:])
-        s_cols = keep.tile([P, PASSES, 2 * PACK], F32, name="s_cols")
-        nc.scalar.copy(out=s_cols[:], in_=s_psum[:, :, 0 : 2 * PACK])
         s_runs = keep.tile([P, PASSES, 2, RUN, PACK], F32, name="s_runs")
         for g in range(PASSES):
             nc.scalar.copy(
@@ -145,24 +153,24 @@ def tile_list_biaff_silu_bias_kernel(
 
         vb_words = keep.tile([P, J], U32, name="vb_words", align_bytes=64)
         va_words = keep.tile([P, M], U32, name="va_words", align_bytes=64)
-
-        def gather_words(dst, table, offsets, h):
-            gather(dst[:, h * HALF : (h + 1) * HALF], table[:].bitcast(U32), offsets[:, h * HALF // 16 : (h + 1) * HALF // 16])
-
-        for h in range(2):
-            gather_words(vb_words, table_b, list_b, h)
+        for half in range(J // HALF):
+            gather(
+                vb_words[:, half * HALF : (half + 1) * HALF],
+                table_b[:].bitcast(U32),
+                list_b[:, half * HALF // 16 : (half + 1) * HALF // 16],
+            )
 
         wa_sorted = keep.tile([P, PASSES, HALF], I32, name="wa_sorted", align_bytes=64)
         wa_sorted_scales = keep.tile([P, PASSES, HALF // 4], I32, name="wa_sorted_scales", align_bytes=64)
 
         def sort_wa():
             nc.vector.tensor_copy(
-                out=wa_sorted[:].rearrange("p g (t q i) -> p g t q i", t=PACK, i=8),
-                in_=wa_raw[:].rearrange("p (g q t i) -> p g t q i", g=PASSES, t=PACK, i=8),
+                out=wa_sorted[:].rearrange("p g (t q i) -> p g t q i", t=PACK, i=BLOCK),
+                in_=wa_raw[:].rearrange("p (g q t i) -> p g t q i", g=PASSES, t=PACK, i=BLOCK),
             )
             nc.vector.tensor_copy(
-                out=wa_sorted_scales[:].rearrange("p g (t q i) -> p g t q i", t=PACK, i=2),
-                in_=wa_plane[:].rearrange("p (g q t i) -> p g t q i", g=PASSES, t=PACK, i=2),
+                out=wa_sorted_scales[:].rearrange("p g (t q i) -> p g t q i", t=PACK, i=BLOCK // 4),
+                in_=wa_plane[:].rearrange("p (g q t i) -> p g t q i", g=PASSES, t=PACK, i=BLOCK // 4),
             )
 
         towers = {
@@ -170,11 +178,11 @@ def tile_list_biaff_silu_bias_kernel(
             "b": (1, wb_words, wb_scales, vb_words, vb_plane[:].bitcast(U8)),
         }
 
-        def front(tower, slabs, width, pool_share, scalar_share, takes_over=None):
+        def hidden(tower, slabs, width, pool_share, scalar_share, h0_takes_over):
             side, w_words, w_scales, v_words, v_scales = towers[tower]
             act = ring.tile([P, 2, width, PACK], F32, name="act", tag="act_%s%d" % (tower, width), bufs=3 if tower == "b" else 2)
             if scalar_share:
-                planes = ring.tile([P, PACK, scalar_share], F32, name="planes", tag="planes", bufs=2)
+                by_byte = ring.tile([P, PACK, scalar_share], F32, name="by_byte", tag="by_byte", bufs=2)
             for k in (1, 0):
                 g, first = slabs[k]
                 for u in reversed(range(width // P)):
@@ -191,45 +199,39 @@ def tile_list_biaff_silu_bias_kernel(
                             stop=True,
                         )
                     if k == 0 and u * P < scalar_share:
-                        nc.scalar.activation(planes[:, :, u * P : (u + 1) * P], bank[:], SILU)
+                        nc.scalar.activation(by_byte[:, :, u * P : (u + 1) * P], bank[:], SILU)
                     else:
                         nc.scalar.activation(act[:, k, u * P : (u + 1) * P], bank[:].rearrange("p t n -> p n t"), SILU)
-            if takes_over:
-                h0 = keep.tile([P, width, PACK], BF16, name="h0_late", tag=takes_over, align_bytes=64)
+            if h0_takes_over:
+                h0 = keep.tile([P, width, PACK], BF16, name="h0_late", tag=h0_takes_over, align_bytes=64)
             else:
                 h0 = ring.tile([P, width, PACK], BF16, name="h0", tag="h0", bufs=3, align_bytes=64)
-            if slabs[1][0] == 1:
+            if slabs[1][0] == 1 and pool_share:
                 h1 = keep.tile([P, width, PACK], BF16, name="h1_late", tag="raw0", align_bytes=64)
             else:
                 h1 = ring.tile([P, width, PACK], BF16, name="h1", tag="h1", bufs=1, align_bytes=64)
             h = [h0, h1]
 
-            def scale(engine, factors, k, lo, hi):
-                if hi > lo:
-                    four = factors[:, slabs[k][0], PACK * side : PACK * (side + 1)]
-                    engine.tensor_tensor(
-                        out=h[k][:, lo:hi], in0=act[:, k, lo:hi], in1=four.unsqueeze(1).to_broadcast([P, hi - lo, PACK]), op=MULT
-                    )
-
             if scalar_share:
                 scaled = ring.tile([P, PACK, scalar_share], BF16, name="scaled", tag="scaled", bufs=3)
                 for t in range(PACK):
-                    col = PACK * side + t
-                    nc.scalar.activation(scaled[:, t], planes[:, t], COPY, scale=s_cols[:, slabs[0][0], col : col + 1])
-                nc.scalar.copy(out=h[0][:, 0:scalar_share], in_=scaled[:].rearrange("p t n -> p n t"))
-            cut = 2 * width - pool_share
-            for k in (1, 0):
-                lo = max(cut - k * width, 0)
-                if lo < width:
-                    run = s_runs[:, slabs[k][0], side].rearrange("p n t -> p (n t)")
-                    nc.gpsimd.tensor_tensor(
-                        out=h[k][:, lo:].rearrange("p (c n) t -> p c (n t)", n=RUN),
-                        in0=act[:, k, lo:].rearrange("p (c n) t -> p c (n t)", n=RUN),
-                        in1=run.unsqueeze(1).to_broadcast([P, (width - lo) // RUN, RUN * PACK]),
-                        op=MULT,
+                    nc.scalar.activation(scaled[:, t], by_byte[:, t], COPY, scale=s_runs[:, slabs[0][0], side, 0, t : t + 1])
+                nc.scalar.copy(out=h0[:, 0:scalar_share], in_=scaled[:].rearrange("p t n -> p n t"))
+            if pool_share:
+                lo = width - pool_share
+                run = s_runs[:, slabs[1][0], side].rearrange("p n t -> p (n t)")
+                nc.gpsimd.tensor_tensor(
+                    out=h1[:, lo:].rearrange("p (c n) t -> p c (n t)", n=RUN),
+                    in0=act[:, 1, lo:].rearrange("p (c n) t -> p c (n t)", n=RUN),
+                    in1=run.unsqueeze(1).to_broadcast([P, pool_share // RUN, RUN * PACK]),
+                    op=MULT,
+                )
+            for k, lo, hi in ((1, 0, width - pool_share), (0, scalar_share, width)):
+                if hi > lo:
+                    four = s_psum[:, slabs[k][0], PACK * side : PACK * (side + 1)]
+                    nc.vector.tensor_tensor(
+                        out=h[k][:, lo:hi], in0=act[:, k, lo:hi], in1=four.unsqueeze(1).to_broadcast([P, hi - lo, PACK]), op=MULT
                     )
-            for k in (1, 0):
-                scale(nc.vector, s_psum, k, scalar_share if k == 0 else 0, min(cut - k * width, width))
             return h
 
         def quantise(h, words, scales):
@@ -240,11 +242,12 @@ def tile_list_biaff_silu_bias_kernel(
         hb_scales = keep.tile([P, PASSES, J], U8, name="hb_scales", align_bytes=64)
 
         def finish(mt, cols, acc):
-            res = ring.tile([P, HALF], F32, name="res", tag="res", bufs=8)
+            res = ring.tile([P, HALF], F32, name="res", tag="res", bufs=(M // P) * (J // HALF))
             nc.vector.scalar_tensor_tensor(out=res[:], in0=acc[:], scalar=OUT_SCALE, in1=bias[:, cols], op0=MULT, op1=ADD)
             nc.sync.dma_start(out=out[mt * P : (mt + 1) * P, cols], in_=res[:])
 
-        def scores(mt, words, scales, hold_last):
+        def scores(mt, words, scales, hold):
+            kept = []
             for jh in range(J // HALF):
                 cols = slice(jh * HALF, (jh + 1) * HALF)
                 acc = psum.tile([P, HALF], F32, name="acc", tag="scores")
@@ -258,37 +261,41 @@ def tile_list_biaff_silu_bias_kernel(
                         start=(g == PASSES - 1),
                         stop=(g == 0),
                     )
-                if hold_last and jh == J // HALF - 1:
-                    return (mt, cols, acc)
-                finish(mt, cols, acc)
-            return None
+                if jh >= J // HALF - hold:
+                    kept.append((mt, cols, acc))
+                else:
+                    finish(mt, cols, acc)
+            return kept
 
         steps = [("b",) + step for step in B_STEPS] + [("a",) + step for step in A_STEPS]
-        held = None
-        h = front(*steps[0])
+        last = len(steps) - 1
+        takes_over = {SORT_AFTER + 1: "picked_b", B_PASS0_END + 1: "picked_a"}
+        held = []
+        h = hidden(*steps[0], takes_over.get(0))
         for n, (tower, slabs, width, pool_share, scalar_share) in enumerate(steps):
             if tower == "b":
                 words = [hb_words[:, g, first : first + width] for g, first in slabs]
                 scales = [hb_scales[:, g, first : first + width] for g, first in slabs]
             else:
-                ha_words = ring.tile([P, PASSES, width], U32, name="ha_words", tag="ha_words", bufs=1, align_bytes=64)
-                ha_scales = ring.tile([P, PASSES, width], U8, name="ha_scales", tag="ha_scales", bufs=1, align_bytes=64)
+                suffix = "_last" if n == last else ""
+                ha_words = ring.tile([P, PASSES, width], U32, name="ha_words", tag="ha_words" + suffix, bufs=1, align_bytes=64)
+                ha_scales = ring.tile([P, PASSES, width], U8, name="ha_scales", tag="ha_scales" + suffix, bufs=1, align_bytes=64)
                 words = [ha_words[:, g, :] for g in range(PASSES)]
                 scales = [ha_scales[:, g, :] for g in range(PASSES)]
             quantise(h, words, scales)
-            if held:
-                finish(*held)
-            if n == 0:
+            for bank in held:
+                finish(*bank)
+            if n == SORT_AFTER:
                 sort_wa()
-            if n == 2:
+            if n == B_PASS0_END:
                 quantise_wb(1, cast_wb(1))
                 bias = keep.tile([P, J], F32, name="bias", tag="grouped1", align_bytes=64)
                 nc.sync.dma_start(out=bias[:], in_=b.partition_broadcast(P))
                 gather(va_words[:], table_a[:].bitcast(U32), list_a[:])
-            if n + 1 < len(steps):
-                h = front(*steps[n + 1], takes_over={0: "picked_b", 2: "picked_a"}.get(n))
+            if n < last:
+                h = hidden(*steps[n + 1], takes_over.get(n + 1))
             if tower == "a":
                 for u in range(width // P):
                     own = slice(u * P, (u + 1) * P)
-                    hold_last = u == width // P - 1 and n + 1 < len(steps)
-                    held = scores(slabs[0][1] // P + u, [w[:, own] for w in words], [s[:, own] for s in scales], hold_last)
+                    hold = {last: 0, last - 1: J // HALF}.get(n, 1) if u == width // P - 1 else 0
+                    held = scores(slabs[0][1] // P + u, [w[:, own] for w in words], [s[:, own] for s in scales], hold)

@@ -29,23 +29,14 @@ A_FIRST = 4
 RUN = 32
 
 NARROW, WIDE = P, 2 * P
-POOL_BARE = WIDE // 2
-B_STEPS = (
-    (((0, 0), (0, NARROW)), NARROW, 0, 0),
-    (((0, 2 * NARROW), (0, 3 * NARROW)), NARROW, 0, 0),
-    (((0, HALF), (0, HALF + WIDE)), WIDE, POOL_BARE, 0),
-    (((1, 0), (1, WIDE)), WIDE, POOL_BARE, 0),
-    (((1, HALF), (1, HALF + WIDE)), WIDE, POOL_BARE, 0),
-)
 A_STEPS = (
-    (((0, 0), (1, 0)), WIDE, POOL_BARE, 0),
-    (((0, WIDE), (1, WIDE)), WIDE, WIDE, 0),
-    (((0, 2 * WIDE), (1, 2 * WIDE)), WIDE, WIDE, P),
-    (((0, 3 * WIDE), (1, 3 * WIDE)), NARROW, NARROW, P),
-    (((0, 3 * WIDE + NARROW), (1, 3 * WIDE + NARROW)), NARROW, 0, P),
+    (0, NARROW, 64, 0, 1),
+    (NARROW, WIDE, 160, P, 1),
+    (NARROW + WIDE, WIDE, WIDE, P, 1),
+    (NARROW + 2 * WIDE, WIDE, WIDE, WIDE, 2),
+    (NARROW + 3 * WIDE, NARROW, NARROW, NARROW, 0),
 )
-SORT_AFTER = 0
-B_PASS0_END = 2
+B1_POOL = 320
 
 
 def tile_list_biaff_silu_bias_kernel(
@@ -64,9 +55,12 @@ def tile_list_biaff_silu_bias_kernel(
         def gather(dst, window, offsets):
             nc.vector.tensor_copy(out=dst, in_=window.indirect(offsets))
 
-        def zeroed(name, shape, dtype):
-            tile = keep.tile(shape, dtype, name=name, tag=name, align_bytes=64)
-            nc.vector.memset(tile[:], 0)
+        def kept(name, shape, dtype, tag=None):
+            return keep.tile(shape, dtype, name=name, tag=tag or name, align_bytes=64)
+
+        def zeroed(name, shape, dtype, engine=nc.gpsimd):
+            tile = kept(name, shape, dtype)
+            engine.memset(tile[:], 0)
             return tile
 
         list_b = lists.tile([P, J // 16], U16, name="list_b")
@@ -74,23 +68,25 @@ def tile_list_biaff_silu_bias_kernel(
         nc.sync.dma_start(list_b[:], offs2)
         nc.sync.dma_start(list_a[:], offs)
 
-        def load_wb(g, tag):
-            raw = keep.tile([P, PACK, HALF], F32, name="wb_raw%d" % g, tag=tag, align_bytes=64)
-            nc.sync.dma_start(out=raw[:], in_=wb[:, g * HALF : (g + 1) * HALF].rearrange("(p i) c -> p i c", i=PACK))
-            return raw
+        wb_raw = [kept("wb_raw%d" % g, [P, PACK, HALF], F32) for g in range(PASSES)]
 
-        wb_raw = [load_wb(0, "raw0")]
+        def load_wb(g, rows):
+            source = wb[:, g * HALF : (g + 1) * HALF].rearrange("(p i) c -> p i c", i=PACK)
+            nc.sync.dma_start(out=wb_raw[g][:, rows, :], in_=source[:, rows, :])
+
         rows_b = zeroed("rows_b", [P, T // 4], I32)
-        nc.sync.dma_start(out=rows_b[0:P:BLOCK, :], in_=tab2_scales[0].bitcast(I32))
-        rows_a = zeroed("rows_a", [P, T // 4], I32)
-        nc.sync.dma_start(out=rows_a[A_FIRST:P:BLOCK, :], in_=tab_scales[0].bitcast(I32))
+        rows_a = zeroed("rows_a", [P, T // 4], I32, nc.vector)
         s_rows = zeroed("s_rows", [P, PASSES, P], F32)
+        load_wb(0, slice(0, PACK // 2))
+        nc.sync.dma_start(out=rows_b[0:P:BLOCK, :], in_=tab2_scales[0].bitcast(I32))
+        load_wb(0, slice(PACK // 2, PACK))
+        nc.sync.dma_start(out=rows_a[A_FIRST:P:BLOCK, :], in_=tab_scales[0].bitcast(I32))
         for side, vec in enumerate((sa, sb)):
             nc.sync.dma_start(
                 out=s_rows[PACK * side : PACK * (side + 1)].rearrange("t g (q i) -> t (g q) i", i=BLOCK),
                 in_=vec.rearrange("(gq t i) -> t gq i", t=PACK, i=BLOCK),
             )
-        table_b = keep.tile([P, T], I32, name="table_b", align_bytes=64)
+        table_b = kept("table_b", [P, T], I32)
         nc.sync.dma_start(out=table_b[:], in_=words_of(tab2_words))
 
         ident = zeroed("ident", [P, P], F32)
@@ -98,9 +94,10 @@ def tile_list_biaff_silu_bias_kernel(
 
         vb_plane = zeroed("vb_plane", [P, J // 4], I32)
         va_plane = zeroed("va_plane", [P, M // 4], I32)
+        wa_plane = zeroed("wa_plane", [P, R // 4], I32)
 
         def gather_scales(name, rows, offsets):
-            picked = keep.tile([P, J], U8, name=name, tag=name, align_bytes=64)
+            picked = kept(name, [P, J], U8)
             gather(picked[:], rows[:].bitcast(U8), offsets[:])
             return picked
 
@@ -108,60 +105,56 @@ def tile_list_biaff_silu_bias_kernel(
             for r in range(4):
                 nc.sync.dma_start(out=plane[r:P:32, :], in_=picked[:].bitcast(I32)[first + BLOCK * r : P : 32, :])
 
-        wb_words = keep.tile([P, PASSES, HALF], U32, name="wb_words", align_bytes=64)
-        wb_scales = keep.tile([P, PASSES, HALF], U8, name="wb_scales", align_bytes=64)
+        wb_words = kept("wb_words", [P, PASSES, HALF], U32)
+        wb_scales = kept("wb_scales", [P, PASSES, HALF], U8)
 
-        def cast_wb(g):
-            grouped = keep.tile(
-                [P, PACK, P // BLOCK, BLOCK, PACK], BF16, name="wb_grouped%d" % g, tag="grouped%d" % g, align_bytes=64
-            )
+        def cast_wb(g, cast):
+            grouped = kept("grouped%d" % g, [P, PACK, P // BLOCK, BLOCK, PACK], BF16)
             source = wb_raw[g][:].rearrange("p k (q t i) -> p t q i k", t=PACK, i=BLOCK)
             for t in range(PACK):
-                nc.scalar.copy(out=grouped[:, t], in_=source[:, t])
+                cast(grouped[:, t], source[:, t])
             return grouped
 
-        def quantise_wb(g, grouped):
-            nc.vector.quantize_mx(
-                out=wb_words[:, g, :].bitcast(FP8X4),
-                scales=wb_scales[:, g, :],
-                in_=grouped[:].rearrange("p t q i k -> p (t q i k)"),
-            )
+        def quantise(h, words, scales):
+            nc.vector.quantize_mx(out=words.bitcast(FP8X4), scales=scales, in_=h)
 
-        grouped0 = cast_wb(0)
+        def quantise_wb(g, grouped):
+            quantise(grouped[:].rearrange("p t q i k -> p (t q i k)"), wb_words[:, g, :], wb_scales[:, g, :])
+
+        grouped0 = cast_wb(0, lambda dst, src: nc.scalar.copy(out=dst, in_=src))
         move_scales(gather_scales("picked_b", rows_b, list_b), 0, vb_plane)
-        wb_raw.append(load_wb(1, "rows_b"))
         picked_a = gather_scales("picked_a", rows_a, list_a)
-        wa_raw = keep.tile([P, R], I32, name="wa_raw", tag="picked_b", align_bytes=64)
+        load_wb(1, slice(0, PACK))
+        table_a = kept("table_a", [P, T], I32)
+        nc.sync.dma_start(out=table_a[:], in_=words_of(tab_words))
+        wa_raw = kept("wa_raw", [P, R], I32)
         nc.sync.dma_start(out=wa_raw[:], in_=words_of(wa_words))
-        wa_plane = zeroed("wa_plane", [P, R // 4], I32)
         for r in range(4):
             nc.sync.dma_start(out=wa_plane[r:P:32, :], in_=wa_scales[0].bitcast(I32)[r:SCALE_ROWS:4, :])
-        table_a = keep.tile([P, T], I32, name="table_a", tag="raw0", align_bytes=64)
-        nc.sync.dma_start(out=table_a[:], in_=words_of(tab_words))
         move_scales(picked_a, A_FIRST, va_plane)
         quantise_wb(0, grouped0)
 
         s_psum = psum.tile([P, PASSES, P], F32, name="s_psum", tag="s_psum", bufs=1)
         for g in range(PASSES):
             nc.tensor.transpose(s_psum[:, g, :], s_rows[:, g, :], ident[:])
-        s_runs = keep.tile([P, PASSES, 2, RUN, PACK], F32, name="s_runs")
+        s_runs = kept("s_runs", [P, PASSES, 2, RUN, PACK], F32)
         for g in range(PASSES):
             nc.scalar.copy(
                 out=s_runs[:, g],
                 in_=s_psum[:, g, 0 : 2 * PACK].rearrange("p (s t) -> p s t", t=PACK).unsqueeze(2).to_broadcast([P, 2, RUN, PACK]),
             )
 
-        vb_words = keep.tile([P, J], U32, name="vb_words", align_bytes=64)
-        va_words = keep.tile([P, M], U32, name="va_words", align_bytes=64)
+        vb_words = [kept("vb_words%d" % half, [P, HALF], U32) for half in range(J // HALF)]
+        va_words = kept("va_words", [P, M], U32)
         for half in range(J // HALF):
             gather(
-                vb_words[:, half * HALF : (half + 1) * HALF],
+                vb_words[half][:],
                 table_b[:].bitcast(U32),
                 list_b[:, half * HALF // 16 : (half + 1) * HALF // 16],
             )
 
-        wa_sorted = keep.tile([P, PASSES, HALF], I32, name="wa_sorted", align_bytes=64)
-        wa_sorted_scales = keep.tile([P, PASSES, HALF // 4], I32, name="wa_sorted_scales", align_bytes=64)
+        wa_sorted = kept("wa_sorted", [P, PASSES, HALF], I32)
+        wa_sorted_scales = kept("wa_sorted_scales", [P, PASSES, HALF // 4], I32)
 
         def sort_wa():
             nc.vector.tensor_copy(
@@ -173,129 +166,155 @@ def tile_list_biaff_silu_bias_kernel(
                 in_=wa_plane[:].rearrange("p (g q t i) -> p g t q i", g=PASSES, t=PACK, i=BLOCK // 4),
             )
 
-        towers = {
-            "a": (0, wa_sorted, wa_sorted_scales[:].bitcast(U8), va_words, va_plane[:].bitcast(U8)),
-            "b": (1, wb_words, wb_scales, vb_words, vb_plane[:].bitcast(U8)),
-        }
+        towers = (
+            (wa_sorted, wa_sorted_scales[:].bitcast(U8), lambda c: va_words[:, c : c + P], va_plane[:].bitcast(U8)),
+            (wb_words, wb_scales, lambda c: vb_words[c // HALF][:, c % HALF : c % HALF + P], vb_plane[:].bitcast(U8)),
+        )
 
-        def hidden(tower, slabs, width, pool_share, scalar_share, h0_takes_over):
-            side, w_words, w_scales, v_words, v_scales = towers[tower]
-            act = ring.tile([P, 2, width, PACK], F32, name="act", tag="act_%s%d" % (tower, width), bufs=3 if tower == "b" else 2)
+        def hidden_bank(side, g, first):
+            w_words, w_scales, v_words, v_scales = towers[side]
+            cols = slice(first, first + P)
+            bank = psum.tile([P, PACK, P], F32, name="bank", tag="hidden", bufs=3)
+            for t in range(PACK):
+                nc.tensor.matmul_mx(
+                    out=bank[:, t, :],
+                    lhsT=w_words[:, g, t * P : (t + 1) * P].bitcast(FP8X4),
+                    lhsT_scale=w_scales[:, g, t * P : (t + 1) * P],
+                    rhs=v_words(first).bitcast(FP8X4),
+                    rhs_scale=v_scales[:, cols],
+                    start=True,
+                    stop=True,
+                )
+            return bank
+
+        def silu_interleaved(act, bank):
+            nc.scalar.activation(act, bank[:].rearrange("p t n -> p n t"), SILU)
+
+        def scale_on_vector(h, act, side, g, count):
+            four = s_psum[:, g, PACK * side : PACK * (side + 1)]
+            nc.vector.tensor_tensor(out=h, in0=act, in1=four.unsqueeze(1).to_broadcast([P, count, PACK]), op=MULT)
+
+        def scale_on_pool(h, act, side, g, count):
+            run = s_runs[:, g, side].rearrange("p n t -> p (n t)")
+            nc.gpsimd.tensor_tensor(
+                out=h.rearrange("p (c n) t -> p c (n t)", n=RUN),
+                in0=act.rearrange("p (c n) t -> p c (n t)", n=RUN),
+                in1=run.unsqueeze(1).to_broadcast([P, count // RUN, RUN * PACK]),
+                op=MULT,
+            )
+
+        def flat(h):
+            return h[:].rearrange("p n t -> p (n t)")
+
+        def front(side, slabs, width, scalar_share, h0, act_bufs):
+            act = ring.tile([P, 2, width, PACK], F32, name="act", tag="act%d" % width, bufs=act_bufs)
             if scalar_share:
                 by_byte = ring.tile([P, PACK, scalar_share], F32, name="by_byte", tag="by_byte", bufs=2)
             for k in (1, 0):
                 g, first = slabs[k]
                 for u in reversed(range(width // P)):
-                    cols = slice(first + u * P, first + (u + 1) * P)
-                    bank = psum.tile([P, PACK, P], F32, name="bank", tag="hidden", bufs=3)
-                    for t in range(PACK):
-                        nc.tensor.matmul_mx(
-                            out=bank[:, t, :],
-                            lhsT=w_words[:, g, t * P : (t + 1) * P].bitcast(FP8X4),
-                            lhsT_scale=w_scales[:, g, t * P : (t + 1) * P],
-                            rhs=v_words[:, cols].bitcast(FP8X4),
-                            rhs_scale=v_scales[:, cols],
-                            start=True,
-                            stop=True,
-                        )
+                    bank = hidden_bank(side, g, first + u * P)
                     if k == 0 and u * P < scalar_share:
                         nc.scalar.activation(by_byte[:, :, u * P : (u + 1) * P], bank[:], SILU)
                     else:
-                        nc.scalar.activation(act[:, k, u * P : (u + 1) * P], bank[:].rearrange("p t n -> p n t"), SILU)
-            if h0_takes_over:
-                h0 = keep.tile([P, width, PACK], BF16, name="h0_late", tag=h0_takes_over, align_bytes=64)
-            else:
-                h0 = ring.tile([P, width, PACK], BF16, name="h0", tag="h0", bufs=3, align_bytes=64)
-            if slabs[1][0] == 1 and pool_share:
-                h1 = keep.tile([P, width, PACK], BF16, name="h1_late", tag="raw0", align_bytes=64)
-            else:
-                h1 = ring.tile([P, width, PACK], BF16, name="h1", tag="h1", bufs=1, align_bytes=64)
-            h = [h0, h1]
-
+                        silu_interleaved(act[:, k, u * P : (u + 1) * P], bank)
             if scalar_share:
-                scaled = ring.tile([P, PACK, scalar_share], BF16, name="scaled", tag="scaled", bufs=3)
+                scaled = ring.tile([P, PACK, scalar_share], BF16, name="scaled", tag="scaled", bufs=2)
                 for t in range(PACK):
                     nc.scalar.activation(scaled[:, t], by_byte[:, t], COPY, scale=s_runs[:, slabs[0][0], side, 0, t : t + 1])
                 nc.scalar.copy(out=h0[:, 0:scalar_share], in_=scaled[:].rearrange("p t n -> p n t"))
-            if pool_share:
-                lo = width - pool_share
-                run = s_runs[:, slabs[1][0], side].rearrange("p n t -> p (n t)")
-                nc.gpsimd.tensor_tensor(
-                    out=h1[:, lo:].rearrange("p (c n) t -> p c (n t)", n=RUN),
-                    in0=act[:, 1, lo:].rearrange("p (c n) t -> p c (n t)", n=RUN),
-                    in1=run.unsqueeze(1).to_broadcast([P, pool_share // RUN, RUN * PACK]),
-                    op=MULT,
-                )
-            for k, lo, hi in ((1, 0, width - pool_share), (0, scalar_share, width)):
-                if hi > lo:
-                    four = s_psum[:, slabs[k][0], PACK * side : PACK * (side + 1)]
-                    nc.vector.tensor_tensor(
-                        out=h[k][:, lo:hi], in0=act[:, k, lo:hi], in1=four.unsqueeze(1).to_broadcast([P, hi - lo, PACK]), op=MULT
-                    )
-            return h
+            return act
 
-        def quantise(h, words, scales):
-            for k in (1, 0):
-                nc.vector.quantize_mx(out=words[k].bitcast(FP8X4), scales=scales[k], in_=h[k][:].rearrange("p n t -> p (n t)"))
+        def back(side, slabs, width, pool_share, scalar_share, act, h0, h1):
+            lo = width - pool_share
+            scale_on_pool(h1[:, lo:], act[:, 1, lo:], side, slabs[1][0], pool_share)
+            if scalar_share < width:
+                scale_on_vector(h0[:, scalar_share:], act[:, 0, scalar_share:], side, slabs[0][0], width - scalar_share)
+            if lo:
+                scale_on_vector(h1[:, 0:lo], act[:, 1, 0:lo], side, slabs[1][0], lo)
 
-        hb_words = keep.tile([P, PASSES, J], U32, name="hb_words", align_bytes=64)
-        hb_scales = keep.tile([P, PASSES, J], U8, name="hb_scales", align_bytes=64)
+        grouped1 = cast_wb(
+            1, lambda dst, src: nc.gpsimd.tensor_scalar(out=dst, in0=src, scalar1=1.0, scalar2=0.0, op0=MULT, op1=ADD)
+        )
+        parts = []
+        for name, first, width in (("h_b0", 0, HALF), ("h_b1", HALF, WIDE), ("grouped1", HALF + WIDE, WIDE)):
+            if name == "grouped1":
+                quantise_wb(1, grouped1)
+            h = kept("h_part", [P, width, PACK], BF16, tag=name)
+            for u in range(width // P):
+                act = ring.tile([P, P, PACK], F32, name="act_bank", tag="act_bank", bufs=4)
+                silu_interleaved(act[:], hidden_bank(1, 0, first + u * P))
+                scale_on_vector(h[:, u * P : (u + 1) * P], act[:], 1, 0, P)
+            parts.append((h, slice(first, first + width)))
+        b_slabs = ((1, 0), (1, HALF))
+        act_b = front(1, b_slabs, HALF, 0, None, 1)
+        gather(va_words[:], table_a[:].bitcast(U32), list_a[:])
+        sort_wa()
+        hb_words = [kept("hb_words0", [P, J], U32, tag="wa_plane"), kept("hb_words1", [P, J], U32)]
+        hb_scales = kept("hb_scales", [P, PASSES, J], U8)
+        for h, cols in parts:
+            quantise(flat(h), hb_words[0][:, cols], hb_scales[:, 0, cols])
+
+        bias = kept("bias", [P, J], F32, tag="wa_raw")
+        nc.sync.dma_start(out=bias[:], in_=b.partition_broadcast(P))
+
+        def a_front(n):
+            first, width, pool_share, scalar_share, hold = A_STEPS[n]
+            h0 = ring.tile([P, width, PACK], BF16, name="h0", tag="h0", bufs=3, align_bytes=64)
+            return front(0, ((0, first), (1, first)), width, scalar_share, h0, 3 if width == WIDE else 2), h0
+
+        def a_back(n, act, h0):
+            first, width, pool_share, scalar_share, hold = A_STEPS[n]
+            h1 = kept("h1", [P, width, PACK], BF16, tag="grouped1")
+            back(0, ((0, first), (1, first)), width, pool_share, scalar_share, act, h0, h1)
+            return [h0, h1]
+
+        fronts = [a_front(0), a_front(1)]
+        h_b = kept("h_b", [P, J, PACK], BF16, tag="grouped1")
+        back(1, b_slabs, HALF, B1_POOL, 0, act_b, h_b[:, 0:HALF], h_b[:, HALF:])
+        quantise(flat(h_b), hb_words[1][:], hb_scales[:, 1, :])
 
         def finish(mt, cols, acc):
-            res = ring.tile([P, HALF], F32, name="res", tag="res", bufs=(M // P) * (J // HALF))
+            res = ring.tile([P, HALF], F32, name="res", tag="res", bufs=12)
             nc.vector.scalar_tensor_tensor(out=res[:], in0=acc[:], scalar=OUT_SCALE, in1=bias[:, cols], op0=MULT, op1=ADD)
             nc.sync.dma_start(out=out[mt * P : (mt + 1) * P, cols], in_=res[:])
 
-        def scores(mt, words, scales, hold):
-            kept = []
+        def scores(mt, words, scales):
             for jh in range(J // HALF):
                 cols = slice(jh * HALF, (jh + 1) * HALF)
                 acc = psum.tile([P, HALF], F32, name="acc", tag="scores")
                 for g in reversed(range(PASSES)):
                     nc.tensor.matmul_mx(
                         out=acc[:],
-                        lhsT=words[g].bitcast(FP8X4),
-                        lhsT_scale=scales[g],
-                        rhs=hb_words[:, g, cols].bitcast(FP8X4),
+                        lhsT=words[:, g].bitcast(FP8X4),
+                        lhsT_scale=scales[:, g],
+                        rhs=hb_words[g][:, cols].bitcast(FP8X4),
                         rhs_scale=hb_scales[:, g, cols],
                         start=(g == PASSES - 1),
                         stop=(g == 0),
                     )
-                if jh >= J // HALF - hold:
-                    kept.append((mt, cols, acc))
-                else:
-                    finish(mt, cols, acc)
-            return kept
+                banks.append((mt, cols, acc))
 
-        steps = [("b",) + step for step in B_STEPS] + [("a",) + step for step in A_STEPS]
-        last = len(steps) - 1
-        takes_over = {SORT_AFTER + 1: "picked_b", B_PASS0_END + 1: "picked_a"}
-        held = []
-        h = hidden(*steps[0], takes_over.get(0))
-        for n, (tower, slabs, width, pool_share, scalar_share) in enumerate(steps):
-            if tower == "b":
-                words = [hb_words[:, g, first : first + width] for g, first in slabs]
-                scales = [hb_scales[:, g, first : first + width] for g, first in slabs]
-            else:
-                suffix = "_last" if n == last else ""
-                ha_words = ring.tile([P, PASSES, width], U32, name="ha_words", tag="ha_words" + suffix, bufs=1, align_bytes=64)
-                ha_scales = ring.tile([P, PASSES, width], U8, name="ha_scales", tag="ha_scales" + suffix, bufs=1, align_bytes=64)
-                words = [ha_words[:, g, :] for g in range(PASSES)]
-                scales = [ha_scales[:, g, :] for g in range(PASSES)]
-            quantise(h, words, scales)
-            for bank in held:
+        last = len(A_STEPS) - 1
+        banks = []
+        h = a_back(0, *fronts[0])
+        for n, (first, width, pool_share, scalar_share, hold) in enumerate(A_STEPS):
+            suffix = "_last" if n == last else ""
+            ha_words = ring.tile([P, PASSES, width], U32, name="ha_words", tag="ha_words" + suffix, bufs=1, align_bytes=64)
+            ha_scales = ring.tile([P, PASSES, width], U8, name="ha_scales", tag="ha_scales" + suffix, bufs=1, align_bytes=64)
+            for g in reversed(range(PASSES)):
+                quantise(flat(h[g]), ha_words[:, g, :], ha_scales[:, g, :])
+            for bank in banks:
                 finish(*bank)
-            if n == SORT_AFTER:
-                sort_wa()
-            if n == B_PASS0_END:
-                quantise_wb(1, cast_wb(1))
-                bias = keep.tile([P, J], F32, name="bias", tag="grouped1", align_bytes=64)
-                nc.sync.dma_start(out=bias[:], in_=b.partition_broadcast(P))
-                gather(va_words[:], table_a[:].bitcast(U32), list_a[:])
+            banks.clear()
+            if n + 2 <= last:
+                fronts.append(a_front(n + 2))
             if n < last:
-                h = hidden(*steps[n + 1], takes_over.get(n + 1))
-            if tower == "a":
-                for u in range(width // P):
-                    own = slice(u * P, (u + 1) * P)
-                    hold = {last: 0, last - 1: J // HALF}.get(n, 1) if u == width // P - 1 else 0
-                    held = scores(slabs[0][1] // P + u, [w[:, own] for w in words], [s[:, own] for s in scales], hold)
+                h = a_back(n + 1, *fronts[n + 1])
+            for u in range(width // P):
+                own = slice(u * P, (u + 1) * P)
+                scores(first // P + u, ha_words[:, :, own], ha_scales[:, :, own])
+                keep_back = hold if u == width // P - 1 else 0
+                for bank in banks[: len(banks) - keep_back]:
+                    finish(*bank)
+                    banks.remove(bank)

@@ -34,9 +34,9 @@ A_STEPS = (
     (NARROW, WIDE, 160, P, 1),
     (NARROW + WIDE, WIDE, WIDE, P, 1),
     (NARROW + 2 * WIDE, WIDE, WIDE, WIDE, 2),
-    (NARROW + 3 * WIDE, NARROW, NARROW, NARROW, 0),
+    (NARROW + 3 * WIDE, NARROW, 0, NARROW, 0),
 )
-B1_POOL = 320
+B1_POOL = 224
 
 
 def tile_list_biaff_silu_bias_kernel(
@@ -58,7 +58,7 @@ def tile_list_biaff_silu_bias_kernel(
         def kept(name, shape, dtype, tag=None):
             return keep.tile(shape, dtype, name=name, tag=tag or name, align_bytes=64)
 
-        def zeroed(name, shape, dtype, engine=nc.gpsimd):
+        def zeroed(name, shape, dtype, engine=nc.vector):
             tile = kept(name, shape, dtype)
             engine.memset(tile[:], 0)
             return tile
@@ -112,7 +112,7 @@ def tile_list_biaff_silu_bias_kernel(
             grouped = kept("grouped%d" % g, [P, PACK, P // BLOCK, BLOCK, PACK], BF16)
             source = wb_raw[g][:].rearrange("p k (q t i) -> p t q i k", t=PACK, i=BLOCK)
             for t in range(PACK):
-                cast(grouped[:, t], source[:, t])
+                cast[t](grouped[:, t], source[:, t])
             return grouped
 
         def quantise(h, words, scales):
@@ -121,7 +121,13 @@ def tile_list_biaff_silu_bias_kernel(
         def quantise_wb(g, grouped):
             quantise(grouped[:].rearrange("p t q i k -> p (t q i k)"), wb_words[:, g, :], wb_scales[:, g, :])
 
-        grouped0 = cast_wb(0, lambda dst, src: nc.scalar.copy(out=dst, in_=src))
+        def cast_on_scalar(dst, src):
+            nc.scalar.copy(out=dst, in_=src)
+
+        def cast_on_pool(dst, src):
+            nc.gpsimd.tensor_scalar(out=dst, in0=src, scalar1=1.0, scalar2=0.0, op0=MULT, op1=ADD)
+
+        grouped0 = cast_wb(0, [cast_on_scalar] * PACK)
         move_scales(gather_scales("picked_b", rows_b, list_b), 0, vb_plane)
         picked_a = gather_scales("picked_a", rows_a, list_a)
         load_wb(1, slice(0, PACK))
@@ -227,15 +233,14 @@ def tile_list_biaff_silu_bias_kernel(
 
         def back(side, slabs, width, pool_share, scalar_share, act, h0, h1):
             lo = width - pool_share
-            scale_on_pool(h1[:, lo:], act[:, 1, lo:], side, slabs[1][0], pool_share)
+            if pool_share:
+                scale_on_pool(h1[:, lo:], act[:, 1, lo:], side, slabs[1][0], pool_share)
             if scalar_share < width:
                 scale_on_vector(h0[:, scalar_share:], act[:, 0, scalar_share:], side, slabs[0][0], width - scalar_share)
             if lo:
                 scale_on_vector(h1[:, 0:lo], act[:, 1, 0:lo], side, slabs[1][0], lo)
 
-        grouped1 = cast_wb(
-            1, lambda dst, src: nc.gpsimd.tensor_scalar(out=dst, in0=src, scalar1=1.0, scalar2=0.0, op0=MULT, op1=ADD)
-        )
+        grouped1 = cast_wb(1, [cast_on_pool] * (PACK - 1) + [cast_on_scalar])
         parts = []
         for name, first, width in (("h_b0", 0, HALF), ("h_b1", HALF, WIDE), ("grouped1", HALF + WIDE, WIDE)):
             if name == "grouped1":
@@ -244,18 +249,23 @@ def tile_list_biaff_silu_bias_kernel(
             for u in range(width // P):
                 act = ring.tile([P, P, PACK], F32, name="act_bank", tag="act_bank", bufs=4)
                 silu_interleaved(act[:], hidden_bank(1, 0, first + u * P))
-                scale_on_vector(h[:, u * P : (u + 1) * P], act[:], 1, 0, P)
+                scale = scale_on_pool if first + (u + 1) * P == J else scale_on_vector
+                scale(h[:, u * P : (u + 1) * P], act[:], 1, 0, P)
             parts.append((h, slice(first, first + width)))
         b_slabs = ((1, 0), (1, HALF))
         act_b = front(1, b_slabs, HALF, 0, None, 1)
+        h_early = kept("h_early", [P, WIDE, PACK], BF16)
+        for u in (1, 0):
+            scale_on_pool(h_early[:, u * P : (u + 1) * P], act_b[:, 1, WIDE + u * P : WIDE + (u + 1) * P], 1, 1, P)
         gather(va_words[:], table_a[:].bitcast(U32), list_a[:])
         sort_wa()
-        hb_words = [kept("hb_words0", [P, J], U32, tag="wa_plane"), kept("hb_words1", [P, J], U32)]
+        hb_both = kept("hb_words", [P, PASSES, J], U32, tag="wa_plane")
+        hb_words = [hb_both[:, g] for g in range(PASSES)]
         hb_scales = kept("hb_scales", [P, PASSES, J], U8)
         for h, cols in parts:
             quantise(flat(h), hb_words[0][:, cols], hb_scales[:, 0, cols])
 
-        bias = kept("bias", [P, J], F32, tag="wa_raw")
+        bias = kept("bias", [P, J], F32, tag="table_a")
         nc.sync.dma_start(out=bias[:], in_=b.partition_broadcast(P))
 
         def a_front(n):
@@ -265,14 +275,20 @@ def tile_list_biaff_silu_bias_kernel(
 
         def a_back(n, act, h0):
             first, width, pool_share, scalar_share, hold = A_STEPS[n]
-            h1 = kept("h1", [P, width, PACK], BF16, tag="grouped1")
+            h1 = kept("h1", [P, width, PACK], BF16, tag="grouped1" if pool_share else "h1_last")
             back(0, ((0, first), (1, first)), width, pool_share, scalar_share, act, h0, h1)
             return [h0, h1]
 
         fronts = [a_front(0), a_front(1)]
-        h_b = kept("h_b", [P, J, PACK], BF16, tag="grouped1")
-        back(1, b_slabs, HALF, B1_POOL, 0, act_b, h_b[:, 0:HALF], h_b[:, HALF:])
-        quantise(flat(h_b), hb_words[1][:], hb_scales[:, 1, :])
+        rest = J - WIDE
+        lo = rest - B1_POOL
+        act_rest = act_b[:].rearrange("p k n t -> p (k n) t")
+        h_b = kept("h_b", [P, rest, PACK], BF16, tag="grouped1")
+        scale_on_pool(h_b[:, lo:], act_rest[:, lo:rest], 1, 1, B1_POOL)
+        scale_on_vector(h_b[:, 0:lo], act_rest[:, 0:lo], 1, 1, lo)
+        quantise(flat(h_early), hb_words[1][:, rest:], hb_scales[:, 1, rest:])
+        for cols in (slice(0, HALF), slice(HALF, rest)):
+            quantise(h_b[:, cols].rearrange("p n t -> p (n t)"), hb_words[1][:, cols], hb_scales[:, 1, cols])
 
         def finish(mt, cols, acc):
             res = ring.tile([P, HALF], F32, name="res", tag="res", bufs=12)

@@ -26,17 +26,17 @@ OUT_SCALE = 0.03125
 SCALE_ROWS = K // 32
 BLOCK = 8
 A_FIRST = 4
-RUN = 32
+RUN = 16
 
 NARROW, WIDE = P, 2 * P
 A_STEPS = (
     (0, NARROW, 64, 0, 1),
     (NARROW, WIDE, 160, P, 1),
     (NARROW + WIDE, WIDE, WIDE, P, 1),
-    (NARROW + 2 * WIDE, WIDE, WIDE, WIDE, 2),
+    (NARROW + 2 * WIDE, WIDE, 224, WIDE, 2),
     (NARROW + 3 * WIDE, NARROW, 0, NARROW, 0),
 )
-B1_POOL = 224
+B1_POOL = 288
 
 
 def tile_list_biaff_silu_bias_kernel(
@@ -65,8 +65,6 @@ def tile_list_biaff_silu_bias_kernel(
 
         list_b = lists.tile([P, J // 16], U16, name="list_b")
         list_a = lists.tile([P, M // 16], U16, name="list_a")
-        nc.sync.dma_start(list_b[:], offs2)
-        nc.sync.dma_start(list_a[:], offs)
 
         wb_raw = [kept("wb_raw%d" % g, [P, PACK, HALF], F32) for g in range(PASSES)]
 
@@ -74,27 +72,30 @@ def tile_list_biaff_silu_bias_kernel(
             source = wb[:, g * HALF : (g + 1) * HALF].rearrange("(p i) c -> p i c", i=PACK)
             nc.sync.dma_start(out=wb_raw[g][:, rows, :], in_=source[:, rows, :])
 
-        rows_b = zeroed("rows_b", [P, T // 4], I32)
-        rows_a = zeroed("rows_a", [P, T // 4], I32, nc.vector)
+        rows_b = zeroed("rows_b", [P, T // 4], I32, nc.gpsimd)
+        rows_a = zeroed("rows_a", [P, T // 4], I32)
+        rows_wa = zeroed("rows_wa", [P, R // 4], I32)
         s_rows = zeroed("s_rows", [P, PASSES, P], F32)
         load_wb(0, slice(0, PACK // 2))
+        nc.sync.dma_start(list_b[:], offs2)
         nc.sync.dma_start(out=rows_b[0:P:BLOCK, :], in_=tab2_scales[0].bitcast(I32))
         load_wb(0, slice(PACK // 2, PACK))
+        nc.sync.dma_start(list_a[:], offs)
         nc.sync.dma_start(out=rows_a[A_FIRST:P:BLOCK, :], in_=tab_scales[0].bitcast(I32))
+        nc.sync.dma_start(out=rows_wa[A_FIRST:P:BLOCK, :], in_=wa_scales[0].bitcast(I32))
+        table_b = kept("table_b", [P, T], I32)
+        nc.sync.dma_start(out=table_b[:], in_=words_of(tab2_words))
         for side, vec in enumerate((sa, sb)):
             nc.sync.dma_start(
                 out=s_rows[PACK * side : PACK * (side + 1)].rearrange("t g (q i) -> t (g q) i", i=BLOCK),
                 in_=vec.rearrange("(gq t i) -> t gq i", t=PACK, i=BLOCK),
             )
-        table_b = kept("table_b", [P, T], I32)
-        nc.sync.dma_start(out=table_b[:], in_=words_of(tab2_words))
 
         ident = zeroed("ident", [P, P], F32)
         make_identity(nc, ident[:], nomemset=True)
 
         vb_plane = zeroed("vb_plane", [P, J // 4], I32)
-        va_plane = zeroed("va_plane", [P, M // 4], I32)
-        wa_plane = zeroed("wa_plane", [P, R // 4], I32)
+        a_planes = zeroed("a_planes", [P, (M + R) // 4], I32)
 
         def gather_scales(name, rows, offsets):
             picked = kept(name, [P, J], U8)
@@ -103,7 +104,7 @@ def tile_list_biaff_silu_bias_kernel(
 
         def move_scales(picked, first, plane):
             for r in range(4):
-                nc.sync.dma_start(out=plane[r:P:32, :], in_=picked[:].bitcast(I32)[first + BLOCK * r : P : 32, :])
+                nc.sync.dma_start(out=plane[r:P:32, :], in_=picked[first + BLOCK * r : P : 32, :])
 
         wb_words = kept("wb_words", [P, PASSES, HALF], U32)
         wb_scales = kept("wb_scales", [P, PASSES, HALF], U8)
@@ -128,27 +129,25 @@ def tile_list_biaff_silu_bias_kernel(
             nc.gpsimd.tensor_scalar(out=dst, in0=src, scalar1=1.0, scalar2=0.0, op0=MULT, op1=ADD)
 
         grouped0 = cast_wb(0, [cast_on_scalar] * PACK)
-        move_scales(gather_scales("picked_b", rows_b, list_b), 0, vb_plane)
+        move_scales(gather_scales("picked_b", rows_b, list_b)[:].bitcast(I32), 0, vb_plane)
+        a_rows = kept("a_rows", [P, (M + R) // 4], I32)
         picked_a = gather_scales("picked_a", rows_a, list_a)
+        nc.vector.tensor_copy(out=a_rows[:, 0 : M // 4], in_=picked_a[:].bitcast(I32))
+        nc.vector.tensor_copy(
+            out=a_rows[:, M // 4 :].rearrange("p (g t q i) -> p g t q i", g=PASSES, t=PACK, i=BLOCK // 4),
+            in_=rows_wa[:].rearrange("p (g q t i) -> p g t q i", g=PASSES, t=PACK, i=BLOCK // 4),
+        )
         load_wb(1, slice(0, PACK))
         table_a = kept("table_a", [P, T], I32)
         nc.sync.dma_start(out=table_a[:], in_=words_of(tab_words))
         wa_raw = kept("wa_raw", [P, R], I32)
         nc.sync.dma_start(out=wa_raw[:], in_=words_of(wa_words))
-        for r in range(4):
-            nc.sync.dma_start(out=wa_plane[r:P:32, :], in_=wa_scales[0].bitcast(I32)[r:SCALE_ROWS:4, :])
-        move_scales(picked_a, A_FIRST, va_plane)
+        move_scales(a_rows, A_FIRST, a_planes)
         quantise_wb(0, grouped0)
 
         s_psum = psum.tile([P, PASSES, P], F32, name="s_psum", tag="s_psum", bufs=1)
         for g in range(PASSES):
             nc.tensor.transpose(s_psum[:, g, :], s_rows[:, g, :], ident[:])
-        s_runs = kept("s_runs", [P, PASSES, 2, RUN, PACK], F32)
-        for g in range(PASSES):
-            nc.scalar.copy(
-                out=s_runs[:, g],
-                in_=s_psum[:, g, 0 : 2 * PACK].rearrange("p (s t) -> p s t", t=PACK).unsqueeze(2).to_broadcast([P, 2, RUN, PACK]),
-            )
 
         vb_words = [kept("vb_words%d" % half, [P, HALF], U32) for half in range(J // HALF)]
         va_words = kept("va_words", [P, M], U32)
@@ -160,20 +159,16 @@ def tile_list_biaff_silu_bias_kernel(
             )
 
         wa_sorted = kept("wa_sorted", [P, PASSES, HALF], I32)
-        wa_sorted_scales = kept("wa_sorted_scales", [P, PASSES, HALF // 4], I32)
+        a_bytes = a_planes[:].bitcast(U8)
 
         def sort_wa():
             nc.vector.tensor_copy(
                 out=wa_sorted[:].rearrange("p g (t q i) -> p g t q i", t=PACK, i=BLOCK),
                 in_=wa_raw[:].rearrange("p (g q t i) -> p g t q i", g=PASSES, t=PACK, i=BLOCK),
             )
-            nc.vector.tensor_copy(
-                out=wa_sorted_scales[:].rearrange("p g (t q i) -> p g t q i", t=PACK, i=BLOCK // 4),
-                in_=wa_plane[:].rearrange("p (g q t i) -> p g t q i", g=PASSES, t=PACK, i=BLOCK // 4),
-            )
 
         towers = (
-            (wa_sorted, wa_sorted_scales[:].bitcast(U8), lambda c: va_words[:, c : c + P], va_plane[:].bitcast(U8)),
+            (wa_sorted, a_bytes[:, M:].rearrange("p (g c) -> p g c", g=PASSES), lambda c: va_words[:, c : c + P], a_bytes[:, 0:M]),
             (wb_words, wb_scales, lambda c: vb_words[c // HALF][:, c % HALF : c % HALF + P], vb_plane[:].bitcast(U8)),
         )
 
@@ -247,19 +242,23 @@ def tile_list_biaff_silu_bias_kernel(
                 quantise_wb(1, grouped1)
             h = kept("h_part", [P, width, PACK], BF16, tag=name)
             for u in range(width // P):
-                act = ring.tile([P, P, PACK], F32, name="act_bank", tag="act_bank", bufs=4)
+                if first + u == 0:
+                    act = kept("act_first", [P, P, PACK], F32)
+                else:
+                    act = ring.tile([P, P, PACK], F32, name="act_bank", tag="act_bank", bufs=4)
                 silu_interleaved(act[:], hidden_bank(1, 0, first + u * P))
-                scale = scale_on_pool if first + (u + 1) * P == J else scale_on_vector
-                scale(h[:, u * P : (u + 1) * P], act[:], 1, 0, P)
+                scale_on_vector(h[:, u * P : (u + 1) * P], act[:], 1, 0, P)
             parts.append((h, slice(first, first + width)))
+        s_runs = kept("s_runs", [P, PASSES, 2, RUN, PACK], F32, tag="act_first")
+        nc.scalar.copy(
+            out=s_runs[:],
+            in_=s_psum[:, :, 0 : 2 * PACK].rearrange("p g (s t) -> p g s t", t=PACK).unsqueeze(3).to_broadcast([P, PASSES, 2, RUN, PACK]),
+        )
         b_slabs = ((1, 0), (1, HALF))
         act_b = front(1, b_slabs, HALF, 0, None, 1)
-        h_early = kept("h_early", [P, WIDE, PACK], BF16)
-        for u in (1, 0):
-            scale_on_pool(h_early[:, u * P : (u + 1) * P], act_b[:, 1, WIDE + u * P : WIDE + (u + 1) * P], 1, 1, P)
         gather(va_words[:], table_a[:].bitcast(U32), list_a[:])
         sort_wa()
-        hb_both = kept("hb_words", [P, PASSES, J], U32, tag="wa_plane")
+        hb_both = kept("hb_words", [P, PASSES, J], U32, tag="wa_raw")
         hb_words = [hb_both[:, g] for g in range(PASSES)]
         hb_scales = kept("hb_scales", [P, PASSES, J], U8)
         for h, cols in parts:
@@ -280,13 +279,12 @@ def tile_list_biaff_silu_bias_kernel(
             return [h0, h1]
 
         fronts = [a_front(0), a_front(1)]
-        rest = J - WIDE
+        rest = J
         lo = rest - B1_POOL
         act_rest = act_b[:].rearrange("p k n t -> p (k n) t")
         h_b = kept("h_b", [P, rest, PACK], BF16, tag="grouped1")
         scale_on_pool(h_b[:, lo:], act_rest[:, lo:rest], 1, 1, B1_POOL)
         scale_on_vector(h_b[:, 0:lo], act_rest[:, 0:lo], 1, 1, lo)
-        quantise(flat(h_early), hb_words[1][:, rest:], hb_scales[:, 1, rest:])
         for cols in (slice(0, HALF), slice(HALF, rest)):
             quantise(h_b[:, cols].rearrange("p n t -> p (n t)"), hb_words[1][:, cols], hb_scales[:, 1, cols])
 

@@ -36,7 +36,7 @@ A_STEPS = (
     (NARROW + 2 * WIDE, WIDE, 224, WIDE, 2),
     (NARROW + 3 * WIDE, NARROW, 0, NARROW, 0),
 )
-B1_POOL = 288
+B1_POOL = 400
 
 
 def tile_list_biaff_silu_bias_kernel(
@@ -235,11 +235,9 @@ def tile_list_biaff_silu_bias_kernel(
             if lo:
                 scale_on_vector(h1[:, 0:lo], act[:, 1, 0:lo], side, slabs[1][0], lo)
 
-        grouped1 = cast_wb(1, [cast_on_pool] * (PACK - 1) + [cast_on_scalar])
+        grouped1 = cast_wb(1, [cast_on_pool] * PACK)
         parts = []
-        for name, first, width in (("h_b0", 0, HALF), ("h_b1", HALF, WIDE), ("grouped1", HALF + WIDE, WIDE)):
-            if name == "grouped1":
-                quantise_wb(1, grouped1)
+        for name, first, width in (("h_b0", 0, HALF), ("h_b1", HALF, WIDE)):
             h = kept("h_part", [P, width, PACK], BF16, tag=name)
             for u in range(width // P):
                 if first + u == 0:
@@ -254,6 +252,11 @@ def tile_list_biaff_silu_bias_kernel(
             out=s_runs[:],
             in_=s_psum[:, :, 0 : 2 * PACK].rearrange("p g (s t) -> p g s t", t=PACK).unsqueeze(3).to_broadcast([P, PASSES, 2, RUN, PACK]),
         )
+        early = HALF + WIDE
+        act_late = kept("act_late", [P, WIDE, PACK], F32)
+        for u in range(WIDE // P):
+            silu_interleaved(act_late[:, u * P : (u + 1) * P], hidden_bank(1, 0, early + u * P))
+        quantise_wb(1, grouped1)
         b_slabs = ((1, 0), (1, HALF))
         act_b = front(1, b_slabs, HALF, 0, None, 1)
         gather(va_words[:], table_a[:].bitcast(U32), list_a[:])
@@ -274,19 +277,19 @@ def tile_list_biaff_silu_bias_kernel(
 
         def a_back(n, act, h0):
             first, width, pool_share, scalar_share, hold = A_STEPS[n]
-            h1 = kept("h1", [P, width, PACK], BF16, tag="grouped1" if pool_share else "h1_last")
+            h1 = kept("h1", [P, width, PACK], BF16, tag="h_b1" if pool_share else "h1_last")
             back(0, ((0, first), (1, first)), width, pool_share, scalar_share, act, h0, h1)
             return [h0, h1]
 
         fronts = [a_front(0), a_front(1)]
-        rest = J
-        lo = rest - B1_POOL
+        lo = J - B1_POOL
         act_rest = act_b[:].rearrange("p k n t -> p (k n) t")
-        h_b = kept("h_b", [P, rest, PACK], BF16, tag="grouped1")
-        scale_on_pool(h_b[:, lo:], act_rest[:, lo:rest], 1, 1, B1_POOL)
+        h_b = kept("h_b", [P, J + WIDE, PACK], BF16, tag="h_b1")
+        scale_on_pool(h_b[:, lo:J], act_rest[:, lo:], 1, 1, B1_POOL)
+        scale_on_vector(h_b[:, J:], act_late[:], 1, 0, WIDE)
         scale_on_vector(h_b[:, 0:lo], act_rest[:, 0:lo], 1, 1, lo)
-        for cols in (slice(0, HALF), slice(HALF, rest)):
-            quantise(h_b[:, cols].rearrange("p n t -> p (n t)"), hb_words[1][:, cols], hb_scales[:, 1, cols])
+        quantise(h_b[:, J:].rearrange("p n t -> p (n t)"), hb_words[0][:, early:], hb_scales[:, 0, early:])
+        quantise(h_b[:, 0:J].rearrange("p n t -> p (n t)"), hb_words[1], hb_scales[:, 1])
 
         def finish(mt, cols, acc):
             res = ring.tile([P, HALF], F32, name="res", tag="res", bufs=12)

@@ -23,20 +23,20 @@ PACK = 4
 PASSES = R // (P * PACK)
 HALF = 512
 OUT_SCALE = 0.03125
-SCALE_ROWS = K // 32
 BLOCK = 8
 A_FIRST = 4
 RUN = 16
 
 NARROW, WIDE = P, 2 * P
+EARLY = HALF + WIDE
+LONG_POOL = 480
 A_STEPS = (
-    (0, NARROW, 64, 0, 1),
+    (0, NARROW, 0, 0, 1),
     (NARROW, WIDE, 160, P, 1),
     (NARROW + WIDE, WIDE, WIDE, P, 1),
-    (NARROW + 2 * WIDE, WIDE, 224, WIDE, 2),
+    (NARROW + 2 * WIDE, WIDE, WIDE, P, 2),
     (NARROW + 3 * WIDE, NARROW, 0, NARROW, 0),
 )
-B1_POOL = 400
 
 
 def tile_list_biaff_silu_bias_kernel(
@@ -102,9 +102,9 @@ def tile_list_biaff_silu_bias_kernel(
             gather(picked[:], rows[:].bitcast(U8), offsets[:])
             return picked
 
-        def move_scales(picked, first, plane):
+        def move_scales(rows, first, plane):
             for r in range(4):
-                nc.sync.dma_start(out=plane[r:P:32, :], in_=picked[first + BLOCK * r : P : 32, :])
+                nc.sync.dma_start(out=plane[r:P:32, :], in_=rows[first + BLOCK * r : P : 32, :])
 
         wb_words = kept("wb_words", [P, PASSES, HALF], U32)
         wb_scales = kept("wb_scales", [P, PASSES, HALF], U8)
@@ -113,7 +113,7 @@ def tile_list_biaff_silu_bias_kernel(
             grouped = kept("grouped%d" % g, [P, PACK, P // BLOCK, BLOCK, PACK], BF16)
             source = wb_raw[g][:].rearrange("p k (q t i) -> p t q i k", t=PACK, i=BLOCK)
             for t in range(PACK):
-                cast[t](grouped[:, t], source[:, t])
+                cast(grouped[:, t], source[:, t])
             return grouped
 
         def quantise(h, words, scales):
@@ -128,7 +128,7 @@ def tile_list_biaff_silu_bias_kernel(
         def cast_on_pool(dst, src):
             nc.gpsimd.tensor_scalar(out=dst, in0=src, scalar1=1.0, scalar2=0.0, op0=MULT, op1=ADD)
 
-        grouped0 = cast_wb(0, [cast_on_scalar] * PACK)
+        grouped0 = cast_wb(0, cast_on_scalar)
         move_scales(gather_scales("picked_b", rows_b, list_b)[:].bitcast(I32), 0, vb_plane)
         a_rows = kept("a_rows", [P, (M + R) // 4], I32)
         picked_a = gather_scales("picked_a", rows_a, list_a)
@@ -160,12 +160,6 @@ def tile_list_biaff_silu_bias_kernel(
 
         wa_sorted = kept("wa_sorted", [P, PASSES, HALF], I32)
         a_bytes = a_planes[:].bitcast(U8)
-
-        def sort_wa():
-            nc.vector.tensor_copy(
-                out=wa_sorted[:].rearrange("p g (t q i) -> p g t q i", t=PACK, i=BLOCK),
-                in_=wa_raw[:].rearrange("p (g q t i) -> p g t q i", g=PASSES, t=PACK, i=BLOCK),
-            )
 
         towers = (
             (wa_sorted, a_bytes[:, M:].rearrange("p (g c) -> p g c", g=PASSES), lambda c: va_words[:, c : c + P], a_bytes[:, 0:M]),
@@ -205,40 +199,12 @@ def tile_list_biaff_silu_bias_kernel(
             )
 
         def flat(h):
-            return h[:].rearrange("p n t -> p (n t)")
+            return h.rearrange("p n t -> p (n t)")
 
-        def front(side, slabs, width, scalar_share, h0, act_bufs):
-            act = ring.tile([P, 2, width, PACK], F32, name="act", tag="act%d" % width, bufs=act_bufs)
-            if scalar_share:
-                by_byte = ring.tile([P, PACK, scalar_share], F32, name="by_byte", tag="by_byte", bufs=2)
-            for k in (1, 0):
-                g, first = slabs[k]
-                for u in reversed(range(width // P)):
-                    bank = hidden_bank(side, g, first + u * P)
-                    if k == 0 and u * P < scalar_share:
-                        nc.scalar.activation(by_byte[:, :, u * P : (u + 1) * P], bank[:], SILU)
-                    else:
-                        silu_interleaved(act[:, k, u * P : (u + 1) * P], bank)
-            if scalar_share:
-                scaled = ring.tile([P, PACK, scalar_share], BF16, name="scaled", tag="scaled", bufs=2)
-                for t in range(PACK):
-                    nc.scalar.activation(scaled[:, t], by_byte[:, t], COPY, scale=s_runs[:, slabs[0][0], side, 0, t : t + 1])
-                nc.scalar.copy(out=h0[:, 0:scalar_share], in_=scaled[:].rearrange("p t n -> p n t"))
-            return act
-
-        def back(side, slabs, width, pool_share, scalar_share, act, h0, h1):
-            lo = width - pool_share
-            if pool_share:
-                scale_on_pool(h1[:, lo:], act[:, 1, lo:], side, slabs[1][0], pool_share)
-            if scalar_share < width:
-                scale_on_vector(h0[:, scalar_share:], act[:, 0, scalar_share:], side, slabs[0][0], width - scalar_share)
-            if lo:
-                scale_on_vector(h1[:, 0:lo], act[:, 1, 0:lo], side, slabs[1][0], lo)
-
-        grouped1 = cast_wb(1, [cast_on_pool] * PACK)
-        parts = []
-        for name, first, width in (("h_b0", 0, HALF), ("h_b1", HALF, WIDE)):
-            h = kept("h_part", [P, width, PACK], BF16, tag=name)
+        grouped1 = cast_wb(1, cast_on_pool)
+        early = []
+        for name, first, width in (("h_first", 0, HALF), ("h_pool", HALF, EARLY - HALF)):
+            h = kept(name, [P, width, PACK], BF16)
             for u in range(width // P):
                 if first + u == 0:
                     act = kept("act_first", [P, P, PACK], F32)
@@ -246,57 +212,76 @@ def tile_list_biaff_silu_bias_kernel(
                     act = ring.tile([P, P, PACK], F32, name="act_bank", tag="act_bank", bufs=4)
                 silu_interleaved(act[:], hidden_bank(1, 0, first + u * P))
                 scale_on_vector(h[:, u * P : (u + 1) * P], act[:], 1, 0, P)
-            parts.append((h, slice(first, first + width)))
+            early.append(h)
         s_runs = kept("s_runs", [P, PASSES, 2, RUN, PACK], F32, tag="act_first")
         nc.scalar.copy(
             out=s_runs[:],
             in_=s_psum[:, :, 0 : 2 * PACK].rearrange("p g (s t) -> p g s t", t=PACK).unsqueeze(3).to_broadcast([P, PASSES, 2, RUN, PACK]),
         )
-        early = HALF + WIDE
-        act_late = kept("act_late", [P, WIDE, PACK], F32)
-        for u in range(WIDE // P):
-            silu_interleaved(act_late[:, u * P : (u + 1) * P], hidden_bank(1, 0, early + u * P))
+        late = J - EARLY
+        act_late = kept("act_late", [P, late, PACK], F32)
+        for u in range(late // P):
+            silu_interleaved(act_late[:, u * P : (u + 1) * P], hidden_bank(1, 0, EARLY + u * P))
         quantise_wb(1, grouped1)
-        b_slabs = ((1, 0), (1, HALF))
-        act_b = front(1, b_slabs, HALF, 0, None, 1)
-        gather(va_words[:], table_a[:].bitcast(U32), list_a[:])
-        sort_wa()
-        hb_both = kept("hb_words", [P, PASSES, J], U32, tag="wa_raw")
-        hb_words = [hb_both[:, g] for g in range(PASSES)]
+        hb_first = kept("hb_first", [P, HALF], U32, tag="wb_raw1")
         hb_scales = kept("hb_scales", [P, PASSES, J], U8)
-        for h, cols in parts:
-            quantise(flat(h), hb_words[0][:, cols], hb_scales[:, 0, cols])
+        quantise(flat(early[0][:]), hb_first[:], hb_scales[:, 0, 0:HALF])
 
+        act_pass1 = kept("act_pass1", [P, J, PACK], F32)
+        for first in reversed(range(0, J, P)):
+            silu_interleaved(act_pass1[:, first : first + P], hidden_bank(1, 1, first))
+        gather(va_words[:], table_a[:].bitcast(U32), list_a[:])
+        nc.vector.tensor_copy(
+            out=wa_sorted[:].rearrange("p g (t q i) -> p g t q i", t=PACK, i=BLOCK),
+            in_=wa_raw[:].rearrange("p (g q t i) -> p g t q i", g=PASSES, t=PACK, i=BLOCK),
+        )
+        hb_rest = kept("hb_rest", [P, J + HALF], U32, tag="wa_raw")
+        hb_words = [[hb_first[:], hb_rest[:, J:]], [hb_rest[:, 0:HALF], hb_rest[:, HALF:J]]]
+        quantise(flat(early[1][:]), hb_rest[:, J : J + EARLY - HALF], hb_scales[:, 0, HALF:EARLY])
         bias = kept("bias", [P, J], F32, tag="table_a")
         nc.sync.dma_start(out=bias[:], in_=b.partition_broadcast(P))
 
-        def a_front(n):
+        def front(n):
             first, width, pool_share, scalar_share, hold = A_STEPS[n]
-            h0 = ring.tile([P, width, PACK], BF16, name="h0", tag="h0", bufs=3, align_bytes=64)
-            return front(0, ((0, first), (1, first)), width, scalar_share, h0, 3 if width == WIDE else 2), h0
+            h0 = kept("h0_%d" % n, [P, width, PACK], BF16)
+            act = ring.tile([P, PASSES, width, PACK], F32, name="act", tag="act%d" % width, bufs=3 if width == WIDE else 2)
+            if scalar_share:
+                by_byte = ring.tile([P, PACK, scalar_share], F32, name="by_byte", tag="by_byte", bufs=2)
+            for g in reversed(range(PASSES)):
+                for u in reversed(range(width // P)):
+                    bank = hidden_bank(0, g, first + u * P)
+                    if g == 0 and u * P < scalar_share:
+                        nc.scalar.activation(by_byte[:, :, u * P : (u + 1) * P], bank[:], SILU)
+                    else:
+                        silu_interleaved(act[:, g, u * P : (u + 1) * P], bank)
+            if scalar_share:
+                scaled = ring.tile([P, PACK, scalar_share], BF16, name="scaled", tag="scaled", bufs=2)
+                for t in range(PACK):
+                    nc.scalar.activation(scaled[:, t], by_byte[:, t], COPY, scale=s_runs[:, 0, 0, 0, t : t + 1])
+                nc.scalar.copy(out=h0[:, 0:scalar_share], in_=scaled[:].rearrange("p t n -> p n t"))
+            return act, h0
 
-        def a_back(n, act, h0):
+        def back(n, act, h0):
             first, width, pool_share, scalar_share, hold = A_STEPS[n]
-            h1 = kept("h1", [P, width, PACK], BF16, tag="h_b1" if pool_share else "h1_last")
-            back(0, ((0, first), (1, first)), width, pool_share, scalar_share, act, h0, h1)
-            return [h0, h1]
+            h1 = kept("h1", [P, width, PACK], BF16, tag="h_pool" if pool_share else "h_vector")
+            lo = width - pool_share
+            if pool_share:
+                scale_on_pool(h1[:, lo:], act[:, 1, lo:], 0, 1, pool_share)
+            if scalar_share < width:
+                scale_on_vector(h0[:, scalar_share:], act[:, 0, scalar_share:], 0, 0, width - scalar_share)
+            if lo:
+                scale_on_vector(h1[:, 0:lo], act[:, 1, 0:lo], 0, 1, lo)
+            return h0, h1
 
-        fronts = [a_front(0), a_front(1)]
-        lo = J - B1_POOL
-        act_rest = act_b[:].rearrange("p k n t -> p (k n) t")
-        h_b = kept("h_b", [P, J + WIDE, PACK], BF16, tag="h_b1")
-        scale_on_pool(h_b[:, lo:J], act_rest[:, lo:], 1, 1, B1_POOL)
-        scale_on_vector(h_b[:, J:], act_late[:], 1, 0, WIDE)
-        scale_on_vector(h_b[:, 0:lo], act_rest[:, 0:lo], 1, 1, lo)
-        quantise(h_b[:, J:].rearrange("p n t -> p (n t)"), hb_words[0][:, early:], hb_scales[:, 0, early:])
-        quantise(h_b[:, 0:J].rearrange("p n t -> p (n t)"), hb_words[1], hb_scales[:, 1])
-
-        def finish(mt, cols, acc):
-            res = ring.tile([P, HALF], F32, name="res", tag="res", bufs=12)
-            nc.vector.scalar_tensor_tensor(out=res[:], in0=acc[:], scalar=OUT_SCALE, in1=bias[:, cols], op0=MULT, op1=ADD)
-            nc.sync.dma_start(out=out[mt * P : (mt + 1) * P, cols], in_=res[:])
+        fronts = [front(0), front(1)]
+        h_long = kept("h_long", [P, J + late, PACK], BF16, tag="h_pool")
+        scale_on_pool(h_long[:, J - LONG_POOL : J], act_pass1[:, J - LONG_POOL :], 1, 1, LONG_POOL)
+        scale_on_vector(h_long[:, J:], act_late[:], 1, 0, late)
+        scale_on_vector(h_long[:, 0 : J - LONG_POOL], act_pass1[:, 0 : J - LONG_POOL], 1, 1, J - LONG_POOL)
+        h = back(0, *fronts[0])
 
         def scores(mt, words, scales):
+            banks = []
             for jh in range(J // HALF):
                 cols = slice(jh * HALF, (jh + 1) * HALF)
                 acc = psum.tile([P, HALF], F32, name="acc", tag="scores")
@@ -305,33 +290,40 @@ def tile_list_biaff_silu_bias_kernel(
                         out=acc[:],
                         lhsT=words[:, g].bitcast(FP8X4),
                         lhsT_scale=scales[:, g],
-                        rhs=hb_words[g][:, cols].bitcast(FP8X4),
+                        rhs=hb_words[g][jh].bitcast(FP8X4),
                         rhs_scale=hb_scales[:, g, cols],
                         start=(g == PASSES - 1),
                         stop=(g == 0),
                     )
                 banks.append((mt, cols, acc))
+            return banks
+
+        def finish(mt, cols, acc):
+            res = ring.tile([P, HALF], F32, name="res", tag="res", bufs=12)
+            nc.vector.scalar_tensor_tensor(out=res[:], in0=acc[:], scalar=OUT_SCALE, in1=bias[:, cols], op0=MULT, op1=ADD)
+            nc.sync.dma_start(out=out[mt * P : (mt + 1) * P, cols], in_=res[:])
 
         last = len(A_STEPS) - 1
-        banks = []
-        h = a_back(0, *fronts[0])
+        held = []
         for n, (first, width, pool_share, scalar_share, hold) in enumerate(A_STEPS):
             suffix = "_last" if n == last else ""
             ha_words = ring.tile([P, PASSES, width], U32, name="ha_words", tag="ha_words" + suffix, bufs=1, align_bytes=64)
             ha_scales = ring.tile([P, PASSES, width], U8, name="ha_scales", tag="ha_scales" + suffix, bufs=1, align_bytes=64)
             for g in reversed(range(PASSES)):
-                quantise(flat(h[g]), ha_words[:, g, :], ha_scales[:, g, :])
-            for bank in banks:
+                quantise(flat(h[g][:]), ha_words[:, g, :], ha_scales[:, g, :])
+            if n == 0:
+                quantise(flat(h_long[:, J:]), hb_rest[:, J + EARLY - HALF :], hb_scales[:, 0, EARLY:])
+                quantise(flat(h_long[:, 0:J]), hb_rest[:, 0:J], hb_scales[:, 1])
+            for bank in held:
                 finish(*bank)
-            banks.clear()
             if n + 2 <= last:
-                fronts.append(a_front(n + 2))
+                fronts.append(front(n + 2))
             if n < last:
-                h = a_back(n + 1, *fronts[n + 1])
+                h = back(n + 1, *fronts[n + 1])
             for u in range(width // P):
                 own = slice(u * P, (u + 1) * P)
-                scores(first // P + u, ha_words[:, :, own], ha_scales[:, :, own])
-                keep_back = hold if u == width // P - 1 else 0
-                for bank in banks[: len(banks) - keep_back]:
+                banks = scores(first // P + u, ha_words[:, :, own], ha_scales[:, :, own])
+                now = len(banks) - hold if u == width // P - 1 else len(banks)
+                for bank in banks[:now]:
                     finish(*bank)
-                    banks.remove(bank)
+                held = banks[now:]

@@ -299,9 +299,14 @@ def tile_list_biaff_silu_bias_kernel(
             return banks
 
         def finish(mt, cols, acc):
-            res = ring.tile([P, HALF], F32, name="res", tag="res", bufs=12)
-            nc.vector.scalar_tensor_tensor(out=res[:], in0=acc[:], scalar=OUT_SCALE, in1=bias[:, cols], op0=MULT, op1=ADD)
-            nc.sync.dma_start(out=out[mt * P : (mt + 1) * P, cols], in_=res[:])
+            piece = WIDE if (mt + 1) * P == M and cols.stop == J else HALF
+            for start in range(0, HALF, piece):
+                part = slice(cols.start + start, cols.start + start + piece)
+                res = ring.tile([P, piece], F32, name="res", tag="res", bufs=12)
+                nc.vector.scalar_tensor_tensor(
+                    out=res[:], in0=acc[:, start : start + piece], scalar=OUT_SCALE, in1=bias[:, part], op0=MULT, op1=ADD
+                )
+                nc.sync.dma_start(out=out[mt * P : (mt + 1) * P, part], in_=res[:])
 
         last = len(A_STEPS) - 1
         held = []
@@ -309,8 +314,11 @@ def tile_list_biaff_silu_bias_kernel(
             suffix = "_last" if n == last else ""
             ha_words = ring.tile([P, PASSES, width], U32, name="ha_words", tag="ha_words" + suffix, bufs=1, align_bytes=64)
             ha_scales = ring.tile([P, PASSES, width], U8, name="ha_scales", tag="ha_scales" + suffix, bufs=1, align_bytes=64)
-            for g in reversed(range(PASSES)):
-                quantise(flat(h[g][:]), ha_words[:, g, :], ha_scales[:, g, :])
+            piece = P if n == last - 1 else width
+            for start in range(0, width, piece):
+                for g in reversed(range(PASSES)):
+                    part = slice(start, start + piece)
+                    quantise(flat(h[g][:, part]), ha_words[:, g, part], ha_scales[:, g, part])
             if n == 0:
                 quantise(flat(h_long[:, J:]), hb_rest[:, J + EARLY - HALF :], hb_scales[:, 0, EARLY:])
                 quantise(flat(h_long[:, 0:J]), hb_rest[:, 0:J], hb_scales[:, 1])

@@ -28,14 +28,14 @@ A_FIRST = 4
 RUN = 16
 
 NARROW, WIDE = P, 2 * P
-EARLY = HALF + WIDE
-LONG_POOL = 480
+EARLY = HALF
+LONG_POOL = 448
 A_STEPS = (
-    (0, NARROW, 0, 0, 1),
+    (0, NARROW, 0, NARROW, 1),
     (NARROW, WIDE, 160, P, 1),
     (NARROW + WIDE, WIDE, WIDE, P, 1),
     (NARROW + 2 * WIDE, WIDE, WIDE, P, 2),
-    (NARROW + 3 * WIDE, NARROW, 0, NARROW, 0),
+    (NARROW + 3 * WIDE, NARROW, NARROW, NARROW, 0),
 )
 
 
@@ -140,7 +140,7 @@ def tile_list_biaff_silu_bias_kernel(
         load_wb(1, slice(0, PACK))
         table_a = kept("table_a", [P, T], I32)
         nc.sync.dma_start(out=table_a[:], in_=words_of(tab_words))
-        wa_raw = kept("wa_raw", [P, R], I32)
+        wa_raw = kept("wa_raw", [P, R], I32, tag="h_pool")
         nc.sync.dma_start(out=wa_raw[:], in_=words_of(wa_words))
         move_scales(a_rows, A_FIRST, a_planes)
         quantise_wb(0, grouped0)
@@ -203,7 +203,7 @@ def tile_list_biaff_silu_bias_kernel(
 
         grouped1 = cast_wb(1, cast_on_pool)
         early = []
-        for name, first, width in (("h_first", 0, HALF), ("h_pool", HALF, EARLY - HALF)):
+        for name, first, width in (("h_first", 0, HALF),):
             h = kept(name, [P, width, PACK], BF16)
             for u in range(width // P):
                 if first + u == 0:
@@ -228,16 +228,15 @@ def tile_list_biaff_silu_bias_kernel(
         quantise(flat(early[0][:]), hb_first[:], hb_scales[:, 0, 0:HALF])
 
         act_pass1 = kept("act_pass1", [P, J, PACK], F32)
-        for first in reversed(range(0, J, P)):
+        for first in range(0, J, P):
             silu_interleaved(act_pass1[:, first : first + P], hidden_bank(1, 1, first))
         gather(va_words[:], table_a[:].bitcast(U32), list_a[:])
         nc.vector.tensor_copy(
             out=wa_sorted[:].rearrange("p g (t q i) -> p g t q i", t=PACK, i=BLOCK),
             in_=wa_raw[:].rearrange("p (g q t i) -> p g t q i", g=PASSES, t=PACK, i=BLOCK),
         )
-        hb_rest = kept("hb_rest", [P, J + HALF], U32, tag="wa_raw")
+        hb_rest = kept("hb_rest", [P, J + HALF], U32)
         hb_words = [[hb_first[:], hb_rest[:, J:]], [hb_rest[:, 0:HALF], hb_rest[:, HALF:J]]]
-        quantise(flat(early[1][:]), hb_rest[:, J : J + EARLY - HALF], hb_scales[:, 0, HALF:EARLY])
         bias = kept("bias", [P, J], F32, tag="table_a")
         nc.sync.dma_start(out=bias[:], in_=b.partition_broadcast(P))
 
@@ -258,7 +257,10 @@ def tile_list_biaff_silu_bias_kernel(
                 scaled = ring.tile([P, PACK, scalar_share], BF16, name="scaled", tag="scaled", bufs=2)
                 for t in range(PACK):
                     nc.scalar.activation(scaled[:, t], by_byte[:, t], COPY, scale=s_runs[:, 0, 0, 0, t : t + 1])
-                nc.scalar.copy(out=h0[:, 0:scalar_share], in_=scaled[:].rearrange("p t n -> p n t"))
+                nc.scalar.copy(
+                    out=h0[:, 0:scalar_share].rearrange("p (c i) t -> p c t i", i=PACK),
+                    in_=scaled[:].rearrange("p t (c i) -> p c t i", i=PACK),
+                )
             return act, h0
 
         def back(n, act, h0):
@@ -275,9 +277,9 @@ def tile_list_biaff_silu_bias_kernel(
 
         fronts = [front(0), front(1)]
         h_long = kept("h_long", [P, J + late, PACK], BF16, tag="h_pool")
-        scale_on_pool(h_long[:, J - LONG_POOL : J], act_pass1[:, J - LONG_POOL :], 1, 1, LONG_POOL)
-        scale_on_vector(h_long[:, J:], act_late[:], 1, 0, late)
-        scale_on_vector(h_long[:, 0 : J - LONG_POOL], act_pass1[:, 0 : J - LONG_POOL], 1, 1, J - LONG_POOL)
+        scale_on_pool(h_long[:, J:], act_late[:], 1, 0, late)
+        for lo, hi in ((0, HALF), (HALF, HALF + WIDE), (HALF + WIDE, J)):
+            scale_on_vector(h_long[:, lo:hi], act_pass1[:, lo:hi], 1, 1, hi - lo)
         h = back(0, *fronts[0])
 
         def scores(mt, words, scales):
@@ -315,12 +317,13 @@ def tile_list_biaff_silu_bias_kernel(
             ha_words = ring.tile([P, PASSES, width], U32, name="ha_words", tag="ha_words" + suffix, bufs=1, align_bytes=64)
             ha_scales = ring.tile([P, PASSES, width], U8, name="ha_scales", tag="ha_scales" + suffix, bufs=1, align_bytes=64)
             piece = P if n == last - 1 else width
+            if n == 0:
+                quantise(flat(h_long[:, J:]), hb_rest[:, J + EARLY - HALF :], hb_scales[:, 0, EARLY:])
             for start in range(0, width, piece):
                 for g in reversed(range(PASSES)):
                     part = slice(start, start + piece)
                     quantise(flat(h[g][:, part]), ha_words[:, g, part], ha_scales[:, g, part])
             if n == 0:
-                quantise(flat(h_long[:, J:]), hb_rest[:, J + EARLY - HALF :], hb_scales[:, 0, EARLY:])
                 quantise(flat(h_long[:, 0:J]), hb_rest[:, 0:J], hb_scales[:, 1])
             for bank in held:
                 finish(*bank)

@@ -66,30 +66,27 @@ def tile_list_biaff_silu_bias_kernel(
         list_b = lists.tile([P, J // 16], U16, name="list_b")
         list_a = lists.tile([P, M // 16], U16, name="list_a")
 
-        wb_raw = [kept("wb_raw%d" % g, [P, PACK, HALF], F32) for g in range(PASSES)]
+        wb_raw0 = [kept("wb_raw0_%d" % half, [P, PACK, WIDE], F32) for half in range(2)]
+        wb_raw1 = kept("wb_raw1", [P, PACK, HALF], F32)
 
-        def load_wb(g, rows):
-            source = wb[:, g * HALF : (g + 1) * HALF].rearrange("(p i) c -> p i c", i=PACK)
-            nc.sync.dma_start(out=wb_raw[g][:, rows, :], in_=source[:, rows, :])
+        def load_wb(tile, first):
+            nc.sync.dma_start(out=tile[:], in_=wb[:, first : first + tile.shape[2]].rearrange("(p i) c -> p i c", i=PACK))
 
         rows_b = zeroed("rows_b", [P, T // 4], I32, nc.gpsimd)
         rows_a = zeroed("rows_a", [P, T // 4], I32)
         rows_wa = zeroed("rows_wa", [P, R // 4], I32)
-        s_rows = zeroed("s_rows", [P, PASSES, P], F32)
-        load_wb(0, slice(0, PACK // 2))
+        s_plain = zeroed("s_plain", [P, HALF], F32)
         nc.sync.dma_start(list_b[:], offs2)
-        nc.sync.dma_start(out=rows_b[0:P:BLOCK, :], in_=tab2_scales[0].bitcast(I32))
-        load_wb(0, slice(PACK // 2, PACK))
         nc.sync.dma_start(list_a[:], offs)
+        load_wb(wb_raw0[0], 0)
+        nc.sync.dma_start(out=rows_b[0:P:BLOCK, :], in_=tab2_scales[0].bitcast(I32))
+        load_wb(wb_raw0[1], WIDE)
         nc.sync.dma_start(out=rows_a[A_FIRST:P:BLOCK, :], in_=tab_scales[0].bitcast(I32))
         nc.sync.dma_start(out=rows_wa[A_FIRST:P:BLOCK, :], in_=wa_scales[0].bitcast(I32))
+        for side, vec in enumerate((sa, sb)):
+            nc.sync.dma_start(out=s_plain[PASSES * side : PASSES * (side + 1), :], in_=vec.rearrange("(g c) -> g c", g=PASSES))
         table_b = kept("table_b", [P, T], I32)
         nc.sync.dma_start(out=table_b[:], in_=words_of(tab2_words))
-        for side, vec in enumerate((sa, sb)):
-            nc.sync.dma_start(
-                out=s_rows[PACK * side : PACK * (side + 1)].rearrange("t g (q i) -> t (g q) i", i=BLOCK),
-                in_=vec.rearrange("(gq t i) -> t gq i", t=PACK, i=BLOCK),
-            )
 
         ident = zeroed("ident", [P, P], F32)
         make_identity(nc, ident[:], nomemset=True)
@@ -109,12 +106,12 @@ def tile_list_biaff_silu_bias_kernel(
         wb_words = kept("wb_words", [P, PASSES, HALF], U32)
         wb_scales = kept("wb_scales", [P, PASSES, HALF], U8)
 
-        def cast_wb(g, cast):
-            grouped = kept("grouped%d" % g, [P, PACK, P // BLOCK, BLOCK, PACK], BF16)
-            source = wb_raw[g][:].rearrange("p k (q t i) -> p t q i k", t=PACK, i=BLOCK)
+        grouped0, grouped1 = [kept("grouped%d" % g, [P, PACK, P // BLOCK, BLOCK, PACK], BF16) for g in range(PASSES)]
+
+        def cast_wb(grouped, raw, cast):
+            source = raw[:].rearrange("p k (q t i) -> p t q i k", t=PACK, i=BLOCK)
             for t in range(PACK):
                 cast(grouped[:, t], source[:, t])
-            return grouped
 
         def quantise(h, words, scales):
             nc.vector.quantize_mx(out=words.bitcast(FP8X4), scales=scales, in_=h)
@@ -123,31 +120,35 @@ def tile_list_biaff_silu_bias_kernel(
             quantise(grouped[:].rearrange("p t q i k -> p (t q i k)"), wb_words[:, g, :], wb_scales[:, g, :])
 
         def cast_on_scalar(dst, src):
-            nc.scalar.copy(out=dst, in_=src)
+            nc.scalar.copy(out=dst.rearrange("p q (h l) k -> p q h k l", l=PACK), in_=src.rearrange("p q (h l) k -> p q h k l", l=PACK))
 
         def cast_on_pool(dst, src):
             nc.gpsimd.tensor_scalar(out=dst, in0=src, scalar1=1.0, scalar2=0.0, op0=MULT, op1=ADD)
 
-        grouped0 = cast_wb(0, cast_on_scalar)
-        move_scales(gather_scales("picked_b", rows_b, list_b)[:].bitcast(I32), 0, vb_plane)
-        a_rows = kept("a_rows", [P, (M + R) // 4], I32)
-        picked_a = gather_scales("picked_a", rows_a, list_a)
-        nc.vector.tensor_copy(out=a_rows[:, 0 : M // 4], in_=picked_a[:].bitcast(I32))
-        nc.vector.tensor_copy(
-            out=a_rows[:, M // 4 :].rearrange("p (g t q i) -> p g t q i", g=PASSES, t=PACK, i=BLOCK // 4),
-            in_=rows_wa[:].rearrange("p (g q t i) -> p g t q i", g=PASSES, t=PACK, i=BLOCK // 4),
+        for half in range(2):
+            cast_wb(grouped0[:, :, half * BLOCK : (half + 1) * BLOCK], wb_raw0[half], cast_on_scalar)
+        s_rows = kept("s_rows", [P, PACK, P], F32)
+        nc.scalar.copy(
+            out=s_rows[:].rearrange("p t (q i) -> p t q i", i=BLOCK),
+            in_=s_plain[:].rearrange("p (q t i) -> p t q i", t=PACK, i=BLOCK),
         )
-        load_wb(1, slice(0, PACK))
+        s_psum = psum.tile([P, PACK, P], F32, name="s_psum", tag="s_psum", bufs=1)
+        for t in range(PACK):
+            nc.tensor.transpose(s_psum[:, t, :], s_rows[:, t, :], ident[:])
+        s_runs = kept("s_runs", [P, 2 * PASSES, RUN, PACK], F32)
+        nc.scalar.copy(
+            out=s_runs[:],
+            in_=s_psum[:, :, 0 : 2 * PASSES].rearrange("p t v -> p v t").unsqueeze(2).to_broadcast([P, 2 * PASSES, RUN, PACK]),
+        )
+        move_scales(gather_scales("picked_b", rows_b, list_b)[:].bitcast(I32), 0, vb_plane)
+        picked_a = gather_scales("picked_a", rows_a, list_a)
+        load_wb(wb_raw1, HALF)
         table_a = kept("table_a", [P, T], I32)
         nc.sync.dma_start(out=table_a[:], in_=words_of(tab_words))
         wa_raw = kept("wa_raw", [P, R], I32, tag="h_pool")
         nc.sync.dma_start(out=wa_raw[:], in_=words_of(wa_words))
-        move_scales(a_rows, A_FIRST, a_planes)
         quantise_wb(0, grouped0)
 
-        s_psum = psum.tile([P, PASSES, P], F32, name="s_psum", tag="s_psum", bufs=1)
-        for g in range(PASSES):
-            nc.tensor.transpose(s_psum[:, g, :], s_rows[:, g, :], ident[:])
 
         vb_words = [kept("vb_words%d" % half, [P, HALF], U32) for half in range(J // HALF)]
         va_words = kept("va_words", [P, M], U32)
@@ -157,6 +158,15 @@ def tile_list_biaff_silu_bias_kernel(
                 table_b[:].bitcast(U32),
                 list_b[:, half * HALF // 16 : (half + 1) * HALF // 16],
             )
+
+
+        a_rows = kept("a_rows", [P, (M + R) // 4], I32, tag="table_b")
+        nc.vector.tensor_copy(out=a_rows[:, 0 : M // 4], in_=picked_a[:].bitcast(I32))
+        nc.vector.tensor_copy(
+            out=a_rows[:, M // 4 :].rearrange("p (g t q i) -> p g t q i", g=PASSES, t=PACK, i=BLOCK // 4),
+            in_=rows_wa[:].rearrange("p (g q t i) -> p g t q i", g=PASSES, t=PACK, i=BLOCK // 4),
+        )
+        move_scales(a_rows, A_FIRST, a_planes)
 
         wa_sorted = kept("wa_sorted", [P, PASSES, HALF], I32)
         a_bytes = a_planes[:].bitcast(U8)
@@ -186,11 +196,11 @@ def tile_list_biaff_silu_bias_kernel(
             nc.scalar.activation(act, bank[:].rearrange("p t n -> p n t"), SILU)
 
         def scale_on_vector(h, act, side, g, count):
-            four = s_psum[:, g, PACK * side : PACK * (side + 1)]
+            four = s_psum[:, :, PASSES * side + g]
             nc.vector.tensor_tensor(out=h, in0=act, in1=four.unsqueeze(1).to_broadcast([P, count, PACK]), op=MULT)
 
         def scale_on_pool(h, act, side, g, count):
-            run = s_runs[:, g, side].rearrange("p n t -> p (n t)")
+            run = s_runs[:, PASSES * side + g].rearrange("p n t -> p (n t)")
             nc.gpsimd.tensor_tensor(
                 out=h.rearrange("p (c n) t -> p c (n t)", n=RUN),
                 in0=act.rearrange("p (c n) t -> p c (n t)", n=RUN),
@@ -201,7 +211,7 @@ def tile_list_biaff_silu_bias_kernel(
         def flat(h):
             return h.rearrange("p n t -> p (n t)")
 
-        grouped1 = cast_wb(1, cast_on_pool)
+        cast_wb(grouped1, wb_raw1, cast_on_pool)
         early = []
         for name, first, width in (("h_first", 0, HALF),):
             h = kept(name, [P, width, PACK], BF16)
@@ -213,11 +223,6 @@ def tile_list_biaff_silu_bias_kernel(
                 silu_interleaved(act[:], hidden_bank(1, 0, first + u * P))
                 scale_on_vector(h[:, u * P : (u + 1) * P], act[:], 1, 0, P)
             early.append(h)
-        s_runs = kept("s_runs", [P, PASSES, 2, RUN, PACK], F32, tag="act_first")
-        nc.scalar.copy(
-            out=s_runs[:],
-            in_=s_psum[:, :, 0 : 2 * PACK].rearrange("p g (s t) -> p g s t", t=PACK).unsqueeze(3).to_broadcast([P, PASSES, 2, RUN, PACK]),
-        )
         late = J - EARLY
         act_late = kept("act_late", [P, late, PACK], F32)
         for u in range(late // P):
@@ -256,7 +261,7 @@ def tile_list_biaff_silu_bias_kernel(
             if scalar_share:
                 scaled = ring.tile([P, PACK, scalar_share], BF16, name="scaled", tag="scaled", bufs=2)
                 for t in range(PACK):
-                    nc.scalar.activation(scaled[:, t], by_byte[:, t], COPY, scale=s_runs[:, 0, 0, 0, t : t + 1])
+                    nc.scalar.activation(scaled[:, t], by_byte[:, t], COPY, scale=s_runs[:, 0, 0, t : t + 1])
                 nc.scalar.copy(
                     out=h0[:, 0:scalar_share].rearrange("p (c i) t -> p c t i", i=PACK),
                     in_=scaled[:].rearrange("p t (c i) -> p c t i", i=PACK),

@@ -66,25 +66,25 @@ def tile_list_biaff_silu_bias_kernel(
         list_b = lists.tile([P, J // 16], U16, name="list_b")
         list_a = lists.tile([P, M // 16], U16, name="list_a")
 
-        wb_raw0 = [kept("wb_raw0_%d" % half, [P, PACK, WIDE], F32) for half in range(2)]
-        wb_raw1 = kept("wb_raw1", [P, PACK, HALF], F32)
+        wb_raw = [kept("wb_raw%d" % g, [P, PACK, HALF], F32) for g in range(PASSES)]
 
-        def load_wb(tile, first):
-            nc.sync.dma_start(out=tile[:], in_=wb[:, first : first + tile.shape[2]].rearrange("(p i) c -> p i c", i=PACK))
+        def load_wb(g, rows):
+            source = wb[:, g * HALF : (g + 1) * HALF].rearrange("(p i) c -> p i c", i=PACK)
+            nc.sync.dma_start(out=wb_raw[g][:, rows, :], in_=source[:, rows, :])
 
         rows_b = zeroed("rows_b", [P, T // 4], I32, nc.gpsimd)
+        s_plain = zeroed("s_plain", [P, HALF], F32)
         rows_a = zeroed("rows_a", [P, T // 4], I32)
         rows_wa = zeroed("rows_wa", [P, R // 4], I32)
-        s_plain = zeroed("s_plain", [P, HALF], F32)
         nc.sync.dma_start(list_b[:], offs2)
         nc.sync.dma_start(list_a[:], offs)
-        load_wb(wb_raw0[0], 0)
+        load_wb(0, slice(0, PACK // 2))
         nc.sync.dma_start(out=rows_b[0:P:BLOCK, :], in_=tab2_scales[0].bitcast(I32))
-        load_wb(wb_raw0[1], WIDE)
-        nc.sync.dma_start(out=rows_a[A_FIRST:P:BLOCK, :], in_=tab_scales[0].bitcast(I32))
-        nc.sync.dma_start(out=rows_wa[A_FIRST:P:BLOCK, :], in_=wa_scales[0].bitcast(I32))
         for side, vec in enumerate((sa, sb)):
             nc.sync.dma_start(out=s_plain[PASSES * side : PASSES * (side + 1), :], in_=vec.rearrange("(g c) -> g c", g=PASSES))
+        load_wb(0, slice(PACK // 2, PACK))
+        nc.sync.dma_start(out=rows_a[A_FIRST:P:BLOCK, :], in_=tab_scales[0].bitcast(I32))
+        nc.sync.dma_start(out=rows_wa[A_FIRST:P:BLOCK, :], in_=wa_scales[0].bitcast(I32))
         table_b = kept("table_b", [P, T], I32)
         nc.sync.dma_start(out=table_b[:], in_=words_of(tab2_words))
 
@@ -125,24 +125,23 @@ def tile_list_biaff_silu_bias_kernel(
         def cast_on_pool(dst, src):
             nc.gpsimd.tensor_scalar(out=dst, in0=src, scalar1=1.0, scalar2=0.0, op0=MULT, op1=ADD)
 
-        for half in range(2):
-            cast_wb(grouped0[:, :, half * BLOCK : (half + 1) * BLOCK], wb_raw0[half], cast_on_scalar)
+        cast_wb(grouped0, wb_raw[0], cast_on_scalar)
         s_rows = kept("s_rows", [P, PACK, P], F32)
         nc.scalar.copy(
             out=s_rows[:].rearrange("p t (q i) -> p t q i", i=BLOCK),
             in_=s_plain[:].rearrange("p (q t i) -> p t q i", t=PACK, i=BLOCK),
         )
-        s_psum = psum.tile([P, PACK, P], F32, name="s_psum", tag="s_psum", bufs=1)
+        s_psum = psum.tile([P, P, PACK], F32, name="s_psum", tag="s_psum", bufs=1)
         for t in range(PACK):
-            nc.tensor.transpose(s_psum[:, t, :], s_rows[:, t, :], ident[:])
+            nc.tensor.transpose(s_psum[:, :, t], s_rows[:, t, :], ident[:])
         s_runs = kept("s_runs", [P, 2 * PASSES, RUN, PACK], F32)
         nc.scalar.copy(
             out=s_runs[:],
-            in_=s_psum[:, :, 0 : 2 * PASSES].rearrange("p t v -> p v t").unsqueeze(2).to_broadcast([P, 2 * PASSES, RUN, PACK]),
+            in_=s_psum[:, 0 : 2 * PASSES].unsqueeze(2).to_broadcast([P, 2 * PASSES, RUN, PACK]),
         )
         move_scales(gather_scales("picked_b", rows_b, list_b)[:].bitcast(I32), 0, vb_plane)
         picked_a = gather_scales("picked_a", rows_a, list_a)
-        load_wb(wb_raw1, HALF)
+        load_wb(1, slice(0, PACK))
         table_a = kept("table_a", [P, T], I32)
         nc.sync.dma_start(out=table_a[:], in_=words_of(tab_words))
         wa_raw = kept("wa_raw", [P, R], I32, tag="h_pool")
@@ -160,7 +159,7 @@ def tile_list_biaff_silu_bias_kernel(
             )
 
 
-        a_rows = kept("a_rows", [P, (M + R) // 4], I32, tag="table_b")
+        a_rows = kept("a_rows", [P, (M + R) // 4], I32)
         nc.vector.tensor_copy(out=a_rows[:, 0 : M // 4], in_=picked_a[:].bitcast(I32))
         nc.vector.tensor_copy(
             out=a_rows[:, M // 4 :].rearrange("p (g t q i) -> p g t q i", g=PASSES, t=PACK, i=BLOCK // 4),
@@ -196,7 +195,7 @@ def tile_list_biaff_silu_bias_kernel(
             nc.scalar.activation(act, bank[:].rearrange("p t n -> p n t"), SILU)
 
         def scale_on_vector(h, act, side, g, count):
-            four = s_psum[:, :, PASSES * side + g]
+            four = s_psum[:, PASSES * side + g]
             nc.vector.tensor_tensor(out=h, in0=act, in1=four.unsqueeze(1).to_broadcast([P, count, PACK]), op=MULT)
 
         def scale_on_pool(h, act, side, g, count):
@@ -211,7 +210,7 @@ def tile_list_biaff_silu_bias_kernel(
         def flat(h):
             return h.rearrange("p n t -> p (n t)")
 
-        cast_wb(grouped1, wb_raw1, cast_on_pool)
+        cast_wb(grouped1, wb_raw[1], cast_on_pool)
         early = []
         for name, first, width in (("h_first", 0, HALF),):
             h = kept(name, [P, width, PACK], BF16)

@@ -17,6 +17,7 @@ MULT = mybir.AluOpType.mult
 ADD = mybir.AluOpType.add
 SILU = mybir.ActivationFunctionType.Silu
 COPY = mybir.ActivationFunctionType.Copy
+IDENTITY = mybir.ActivationFunctionType.Identity
 
 P = 128
 PACK = 4
@@ -91,6 +92,7 @@ def tile_list_biaff_silu_bias_kernel(
         ident = zeroed("ident", [P, P], F32)
         make_identity(nc, ident[:], nomemset=True)
 
+        zero = zeroed("zero", [P, 1], F32)
         vb_plane = zeroed("vb_plane", [P, J // 4], I32)
         a_planes = zeroed("a_planes", [P, (M + R) // 4], I32)
 
@@ -210,7 +212,9 @@ def tile_list_biaff_silu_bias_kernel(
         def flat(h):
             return h.rearrange("p n t -> p (n t)")
 
-        cast_wb(grouped1, wb_raw[1], cast_on_pool)
+        source1 = wb_raw[1][:].rearrange("p k (q t i) -> p t q i k", t=PACK, i=BLOCK)
+        for t in range(PACK - 1):
+            cast_on_pool(grouped1[:, t], source1[:, t])
         early = []
         for name, first, width in (("h_first", 0, HALF),):
             h = kept(name, [P, width, PACK], BF16)
@@ -223,7 +227,8 @@ def tile_list_biaff_silu_bias_kernel(
                 scale_on_vector(h[:, u * P : (u + 1) * P], act[:], 1, 0, P)
             early.append(h)
         late = J - EARLY
-        act_late = kept("act_late", [P, late, PACK], F32)
+        nc.scalar.activation(grouped1[:, PACK - 1], source1[:, PACK - 1], IDENTITY, bias=zero[:])
+        act_late = kept("act_late", [P, late, PACK], F32, tag="zero")
         for u in range(late // P):
             silu_interleaved(act_late[:, u * P : (u + 1) * P], hidden_bank(1, 0, EARLY + u * P))
         quantise_wb(1, grouped1)

@@ -177,10 +177,13 @@ def tile_list_biaff_silu_bias_kernel(
             (wb_words, wb_scales, lambda c: vb_words[c // HALF][:, c % HALF : c % HALF + P], vb_plane[:].bitcast(U8)),
         )
 
-        def hidden_bank(side, g, first):
+        def hidden_bank(side, g, first, late=False):
             w_words, w_scales, v_words, v_scales = towers[side]
             cols = slice(first, first + P)
-            bank = psum.tile([P, PACK, P], F32, name="bank", tag="hidden", bufs=3)
+            if late:
+                bank = psum.tile([P, PACK, P], F32, name="bank", tag="scores")
+            else:
+                bank = psum.tile([P, PACK, P], F32, name="bank", tag="hidden", bufs=3)
             for t in range(PACK):
                 nc.tensor.matmul_mx(
                     out=bank[:, t, :],
@@ -253,24 +256,21 @@ def tile_list_biaff_silu_bias_kernel(
             first, width, pool_share, scalar_share, hold = A_STEPS[n]
             h0 = kept("h0_%d" % n, [P, width, PACK], BF16)
             act = ring.tile([P, PASSES, width, PACK], F32, name="act", tag="act%d" % width, bufs=3 if width == WIDE else 2)
-            if scalar_share:
-                by_byte = ring.tile([P, PACK, scalar_share], F32, name="by_byte", tag="by_byte", bufs=2)
             for g in reversed(range(PASSES)):
                 for u in reversed(range(width // P)):
-                    bank = hidden_bank(0, g, first + u * P)
-                    if g == 0 and u * P < scalar_share:
-                        nc.scalar.activation(by_byte[:, :, u * P : (u + 1) * P], bank[:], SILU)
-                    else:
-                        silu_interleaved(act[:, g, u * P : (u + 1) * P], bank)
-            if scalar_share:
-                scaled = ring.tile([P, PACK, scalar_share], BF16, name="scaled", tag="scaled", bufs=2)
-                for t in range(PACK):
-                    nc.scalar.activation(scaled[:, t], by_byte[:, t], COPY, scale=s_runs[:, 0, 0, t : t + 1])
-                nc.scalar.copy(
-                    out=h0[:, 0:scalar_share].rearrange("p (c i) t -> p c t i", i=PACK),
-                    in_=scaled[:].rearrange("p t (c i) -> p c t i", i=PACK),
-                )
+                    if g or u:
+                        silu_interleaved(act[:, g, u * P : (u + 1) * P], hidden_bank(0, g, first + u * P))
             return act, h0
+
+        def scalar_bank(n, h0):
+            by_byte = ring.tile([P, PACK, P], F32, name="by_byte", tag="by_byte", bufs=2)
+            nc.scalar.activation(by_byte[:], hidden_bank(0, 0, A_STEPS[n][0], late=2 <= n < len(A_STEPS) - 1)[:], SILU)
+            scaled = ring.tile([P, PACK, P], BF16, name="scaled", tag="scaled", bufs=2)
+            for t in range(PACK):
+                nc.scalar.activation(scaled[:, t], by_byte[:, t], COPY, scale=s_runs[:, 0, 0, t : t + 1])
+            nc.scalar.copy(
+                out=h0[:, 0:P].rearrange("p (c i) t -> p c t i", i=PACK), in_=scaled[:].rearrange("p t (c i) -> p c t i", i=PACK)
+            )
 
         def back(n, act, h0):
             first, width, pool_share, scalar_share, hold = A_STEPS[n]
@@ -284,7 +284,10 @@ def tile_list_biaff_silu_bias_kernel(
                 scale_on_vector(h1[:, 0:lo], act[:, 1, 0:lo], 0, 1, lo)
             return h0, h1
 
-        fronts = [front(0), front(1)]
+        fronts = []
+        for n in range(2):
+            fronts.append(front(n))
+            scalar_bank(n, fronts[n][1])
         h_long = kept("h_long", [P, J + late, PACK], BF16, tag="h_pool")
         scale_on_pool(h_long[:, J:], act_late[:], 1, 0, late)
         for lo, hi in ((0, HALF), (HALF, HALF + WIDE), (HALF + WIDE, J)):
@@ -338,6 +341,8 @@ def tile_list_biaff_silu_bias_kernel(
                 finish(*bank)
             if n + 2 <= last:
                 fronts.append(front(n + 2))
+            if n + 2 == last:
+                scalar_bank(last, fronts[last][1])
             if n < last:
                 h = back(n + 1, *fronts[n + 1])
             for u in range(width // P):
@@ -347,3 +352,5 @@ def tile_list_biaff_silu_bias_kernel(
                 for bank in banks[:now]:
                     finish(*bank)
                 held = banks[now:]
+            if n + 2 < last:
+                scalar_bank(n + 2, fronts[n + 2][1])

@@ -255,7 +255,10 @@ def tile_list_biaff_silu_bias_kernel(
         def front(n):
             first, width, pool_share, scalar_share, hold = A_STEPS[n]
             h0 = kept("h0_%d" % n, [P, width, PACK], BF16)
-            act = ring.tile([P, PASSES, width, PACK], F32, name="act", tag="act%d" % width, bufs=3 if width == WIDE else 2)
+            if width == WIDE:
+                act = ring.tile([P, PASSES, width, PACK], F32, name="act", tag="act", bufs=3)
+            else:
+                act = kept("act%d" % n, [P, PASSES, width, PACK], F32)
             for g in reversed(range(PASSES)):
                 for u in reversed(range(width // P)):
                     if g or u:
@@ -265,7 +268,7 @@ def tile_list_biaff_silu_bias_kernel(
         def scalar_bank(n, h0):
             by_byte = ring.tile([P, PACK, P], F32, name="by_byte", tag="by_byte", bufs=2)
             nc.scalar.activation(by_byte[:], hidden_bank(0, 0, A_STEPS[n][0], late=2 <= n < len(A_STEPS) - 1)[:], SILU)
-            scaled = ring.tile([P, PACK, P], BF16, name="scaled", tag="scaled", bufs=2)
+            scaled = kept("scaled%d" % n, [P, PACK, P], BF16)
             for t in range(PACK):
                 nc.scalar.activation(scaled[:, t], by_byte[:, t], COPY, scale=s_runs[:, 0, 0, t : t + 1])
             nc.scalar.copy(
@@ -325,9 +328,8 @@ def tile_list_biaff_silu_bias_kernel(
         last = len(A_STEPS) - 1
         held = []
         for n, (first, width, pool_share, scalar_share, hold) in enumerate(A_STEPS):
-            suffix = "_last" if n == last else ""
-            ha_words = ring.tile([P, PASSES, width], U32, name="ha_words", tag="ha_words" + suffix, bufs=1, align_bytes=64)
-            ha_scales = ring.tile([P, PASSES, width], U8, name="ha_scales", tag="ha_scales" + suffix, bufs=1, align_bytes=64)
+            ha_words = kept("ha_words", [P, PASSES, width], U32, tag="scaled%d" % n if n else None)
+            ha_scales = kept("ha_scales", [P, PASSES, width], U8, tag="act%d" % n if n == last else None)
             piece = P if n == last - 1 else width
             if n == 0:
                 quantise(flat(h_long[:, J:]), hb_rest[:, J + EARLY - HALF :], hb_scales[:, 0, EARLY:])

from contextlib import ExitStack

import concourse.mybir as mybir
from concourse.masks import make_identity

K, R, T, M, J = 512, 1024, 4096, 1024, 1024
FLOPS = 2 * K * R * M + 2 * K * R * J + 2 * R * M * J

F32 = mybir.dt.float32
BF16 = mybir.dt.bfloat16
I32 = mybir.dt.int32
U32 = mybir.dt.uint32
U16 = mybir.dt.uint16
U8 = mybir.dt.uint8
FP8X4 = mybir.dt.float8_e4m3fn_x4
MULT = mybir.AluOpType.mult
ADD = mybir.AluOpType.add
SILU = mybir.ActivationFunctionType.Silu
COPY = mybir.ActivationFunctionType.Copy
IDENTITY = mybir.ActivationFunctionType.Identity

P = 128
PACK = 4
PASSES = R // (P * PACK)
HALF = 512
OUT_SCALE = 0.03125
BLOCK = 8
A_FIRST = 4
RUN = 16

NARROW, WIDE = P, 2 * P
EARLY = HALF
LONG_POOL = 448
A_STEPS = (
    (0, NARROW, 0, NARROW, 1),
    (NARROW, WIDE, 160, P, 1),
    (NARROW + WIDE, WIDE, WIDE, P, 1),
    (NARROW + 2 * WIDE, WIDE, WIDE, P, 2),
    (NARROW + 3 * WIDE, NARROW, NARROW, NARROW, 0),
)


def tile_list_biaff_silu_bias_kernel(
    tc, tab_words, tab_scales, tab2_words, tab2_scales, wa_words, wa_scales, wb, sa, sb, b, offs, offs2, out
):
    nc = tc.nc
    with ExitStack() as ctx:
        lists = ctx.enter_context(tc.tile_pool(name="lists", bufs=1))
        keep = ctx.enter_context(tc.tile_pool(name="keep", bufs=1))
        ring = ctx.enter_context(tc.tile_pool(name="ring", bufs=3))
        psum = ctx.enter_context(tc.psum_pool(name="psum", bufs=4))

        def words_of(dram):
            return dram[0].rearrange("p n i -> p (n i)").bitcast(I32)

        def gather(dst, window, offsets):
            nc.vector.tensor_copy(out=dst, in_=window.indirect(offsets))

        def kept(name, shape, dtype, tag=None):
            return keep.tile(shape, dtype, name=name, tag=tag or name, align_bytes=64)

        def zeroed(name, shape, dtype, engine=nc.vector):
            tile = kept(name, shape, dtype)
            engine.memset(tile[:], 0)
            return tile

        list_b = lists.tile([P, J // 16], U16, name="list_b")
        list_a = lists.tile([P, M // 16], U16, name="list_a")

        wb_raw = [kept("wb_raw%d" % g, [P, PACK, HALF], F32) for g in range(PASSES)]

        def load_wb(g, rows):
            source = wb[:, g * HALF : (g + 1) * HALF].rearrange("(p i) c -> p i c", i=PACK)
            nc.sync.dma_start(out=wb_raw[g][:, rows, :], in_=source[:, rows, :])

        rows_b = zeroed("rows_b", [P, T // 4], I32, nc.gpsimd)
        s_plain = zeroed("s_plain", [P, HALF], F32)
        rows_a = zeroed("rows_a", [P, T // 4], I32)
        rows_wa = zeroed("rows_wa", [P, R // 4], I32)
        nc.sync.dma_start(list_b[:], offs2)
        nc.sync.dma_start(list_a[:], offs)
        load_wb(0, slice(0, PACK // 2))
        nc.sync.dma_start(out=rows_b[0:P:BLOCK, :], in_=tab2_scales[0].bitcast(I32))
        for side, vec in enumerate((sa, sb)):
            nc.sync.dma_start(out=s_plain[PASSES * side : PASSES * (side + 1), :], in_=vec.rearrange("(g c) -> g c", g=PASSES))
        load_wb(0, slice(PACK // 2, PACK))
        nc.sync.dma_start(out=rows_a[A_FIRST:P:BLOCK, :], in_=tab_scales[0].bitcast(I32))
        nc.sync.dma_start(out=rows_wa[A_FIRST:P:BLOCK, :], in_=wa_scales[0].bitcast(I32))
        table_b = kept("table_b", [P, T], I32)
        nc.sync.dma_start(out=table_b[:], in_=words_of(tab2_words))

        ident = zeroed("ident", [P, P], F32)
        make_identity(nc, ident[:], nomemset=True)

        zero = zeroed("zero", [P, 1], F32)
        vb_plane = zeroed("vb_plane", [P, J // 4], I32)
        a_planes = zeroed("a_planes", [P, (M + R) // 4], I32)

        def gather_scales(name, rows, offsets):
            picked = kept(name, [P, J], U8)
            gather(picked[:], rows[:].bitcast(U8), offsets[:])
            return picked

        def move_scales(rows, first, plane):
            for r in range(4):
                nc.sync.dma_start(out=plane[r:P:32, :], in_=rows[first + BLOCK * r : P : 32, :])

        wb_words = kept("wb_words", [P, PASSES, HALF], U32)
        wb_scales = kept("wb_scales", [P, PASSES, HALF], U8)

        grouped0, grouped1 = [kept("grouped%d" % g, [P, PACK, P // BLOCK, BLOCK, PACK], BF16) for g in range(PASSES)]

        def cast_wb(grouped, raw, cast):
            source = raw[:].rearrange("p k (q t i) -> p t q i k", t=PACK, i=BLOCK)
            for t in range(PACK):
                cast(grouped[:, t], source[:, t])

        def quantise(h, words, scales):
            nc.vector.quantize_mx(out=words.bitcast(FP8X4), scales=scales, in_=h)

        def quantise_wb(g, grouped):
            quantise(grouped[:].rearrange("p t q i k -> p (t q i k)"), wb_words[:, g, :], wb_scales[:, g, :])

        def cast_on_scalar(dst, src):
            nc.scalar.copy(out=dst.rearrange("p q (h l) k -> p q h k l", l=PACK), in_=src.rearrange("p q (h l) k -> p q h k l", l=PACK))

        def cast_on_pool(dst, src):
            nc.gpsimd.tensor_scalar(out=dst, in0=src, scalar1=1.0, scalar2=0.0, op0=MULT, op1=ADD)

        cast_wb(grouped0, wb_raw[0], cast_on_scalar)
        s_rows = kept("s_rows", [P, PACK, P], F32)
        nc.scalar.copy(
            out=s_rows[:].rearrange("p t (q i) -> p t q i", i=BLOCK),
            in_=s_plain[:].rearrange("p (q t i) -> p t q i", t=PACK, i=BLOCK),
        )
        s_psum = psum.tile([P, P, PACK], F32, name="s_psum", tag="s_psum", bufs=1)
        for t in range(PACK):
            nc.tensor.transpose(s_psum[:, :, t], s_rows[:, t, :], ident[:])
        s_runs = kept("s_runs", [P, 2 * PASSES, RUN, PACK], F32)
        nc.scalar.copy(
            out=s_runs[:],
            in_=s_psum[:, 0 : 2 * PASSES].unsqueeze(2).to_broadcast([P, 2 * PASSES, RUN, PACK]),
        )
        move_scales(gather_scales("picked_b", rows_b, list_b)[:].bitcast(I32), 0, vb_plane)
        picked_a = gather_scales("picked_a", rows_a, list_a)
        load_wb(1, slice(0, PACK))
        table_a = kept("table_a", [P, T], I32)
        nc.sync.dma_start(out=table_a[:], in_=words_of(tab_words))
        wa_raw = kept("wa_raw", [P, R], I32, tag="h_pool")
        nc.sync.dma_start(out=wa_raw[:], in_=words_of(wa_words))
        quantise_wb(0, grouped0)


        vb_words = [kept("vb_words%d" % half, [P, HALF], U32) for half in range(J // HALF)]
        va_words = kept("va_words", [P, M], U32)
        for half in range(J // HALF):
            gather(
                vb_words[half][:],
                table_b[:].bitcast(U32),
                list_b[:, half * HALF // 16 : (half + 1) * HALF // 16],
            )


        a_rows = kept("a_rows", [P, (M + R) // 4], I32)
        nc.vector.tensor_copy(out=a_rows[:, 0 : M // 4], in_=picked_a[:].bitcast(I32))
        nc.vector.tensor_copy(
            out=a_rows[:, M // 4 :].rearrange("p (g t q i) -> p g t q i", g=PASSES, t=PACK, i=BLOCK // 4),
            in_=rows_wa[:].rearrange("p (g q t i) -> p g t q i", g=PASSES, t=PACK, i=BLOCK // 4),
        )
        move_scales(a_rows, A_FIRST, a_planes)

        wa_sorted = kept("wa_sorted", [P, PASSES, HALF], I32)
        a_bytes = a_planes[:].bitcast(U8)

        towers = (
            (wa_sorted, a_bytes[:, M:].rearrange("p (g c) -> p g c", g=PASSES), lambda c: va_words[:, c : c + P], a_bytes[:, 0:M]),
            (wb_words, wb_scales, lambda c: vb_words[c // HALF][:, c % HALF : c % HALF + P], vb_plane[:].bitcast(U8)),
        )

        def hidden_bank(side, g, first, late=False):
            w_words, w_scales, v_words, v_scales = towers[side]
            cols = slice(first, first + P)
            if late:
                bank = psum.tile([P, PACK, P], F32, name="bank", tag="scores")
            else:
                bank = psum.tile([P, PACK, P], F32, name="bank", tag="hidden", bufs=3)
            for t in range(PACK):
                nc.tensor.matmul_mx(
                    out=bank[:, t, :],
                    lhsT=w_words[:, g, t * P : (t + 1) * P].bitcast(FP8X4),
                    lhsT_scale=w_scales[:, g, t * P : (t + 1) * P],
                    rhs=v_words(first).bitcast(FP8X4),
                    rhs_scale=v_scales[:, cols],
                    start=True,
                    stop=True,
                )
            return bank

        def silu_interleaved(act, bank):
            nc.scalar.activation(act, bank[:].rearrange("p t n -> p n t"), SILU)

        def scale_on_vector(h, act, side, g, count):
            four = s_psum[:, PASSES * side + g]
            nc.vector.tensor_tensor(out=h, in0=act, in1=four.unsqueeze(1).to_broadcast([P, count, PACK]), op=MULT)

        def scale_on_pool(h, act, side, g, count):
            run = s_runs[:, PASSES * side + g].rearrange("p n t -> p (n t)")
            nc.gpsimd.tensor_tensor(
                out=h.rearrange("p (c n) t -> p c (n t)", n=RUN),
                in0=act.rearrange("p (c n) t -> p c (n t)", n=RUN),
                in1=run.unsqueeze(1).to_broadcast([P, count // RUN, RUN * PACK]),
                op=MULT,
            )

        def flat(h):
            return h.rearrange("p n t -> p (n t)")

        source1 = wb_raw[1][:].rearrange("p k (q t i) -> p t q i k", t=PACK, i=BLOCK)
        for t in range(PACK - 1):
            cast_on_pool(grouped1[:, t], source1[:, t])
        early = []
        for name, first, width in (("h_first", 0, HALF),):
            h = kept(name, [P, width, PACK], BF16)
            for u in range(width // P):
                if first + u == 0:
                    act = kept("act_first", [P, P, PACK], F32)
                else:
                    act = ring.tile([P, P, PACK], F32, name="act_bank", tag="act_bank", bufs=4)
                silu_interleaved(act[:], hidden_bank(1, 0, first + u * P))
                scale_on_vector(h[:, u * P : (u + 1) * P], act[:], 1, 0, P)
            early.append(h)
        late = J - EARLY
        nc.scalar.activation(grouped1[:, PACK - 1], source1[:, PACK - 1], IDENTITY, bias=zero[:])
        act_late = kept("act_late", [P, late, PACK], F32, tag="zero")
        for u in range(late // P):
            silu_interleaved(act_late[:, u * P : (u + 1) * P], hidden_bank(1, 0, EARLY + u * P))
        quantise_wb(1, grouped1)
        hb_first = kept("hb_first", [P, HALF], U32, tag="wb_raw1")
        hb_scales = kept("hb_scales", [P, PASSES, J], U8)
        quantise(flat(early[0][:]), hb_first[:], hb_scales[:, 0, 0:HALF])

        act_pass1 = kept("act_pass1", [P, J, PACK], F32)
        for first in range(0, J, P):
            silu_interleaved(act_pass1[:, first : first + P], hidden_bank(1, 1, first))
        gather(va_words[:], table_a[:].bitcast(U32), list_a[:])
        nc.vector.tensor_copy(
            out=wa_sorted[:].rearrange("p g (t q i) -> p g t q i", t=PACK, i=BLOCK),
            in_=wa_raw[:].rearrange("p (g q t i) -> p g t q i", g=PASSES, t=PACK, i=BLOCK),
        )
        hb_rest = kept("hb_rest", [P, J + HALF], U32)
        hb_words = [[hb_first[:], hb_rest[:, J:]], [hb_rest[:, 0:HALF], hb_rest[:, HALF:J]]]
        bias = kept("bias", [P, J], F32, tag="table_a")
        nc.sync.dma_start(out=bias[:], in_=b.partition_broadcast(P))

        def front(n):
            first, width, pool_share, scalar_share, hold = A_STEPS[n]
            h0 = kept("h0_%d" % n, [P, width, PACK], BF16)
            if width == WIDE:
                act = ring.tile([P, PASSES, width, PACK], F32, name="act", tag="act", bufs=3)
            else:
                act = kept("act%d" % n, [P, PASSES, width, PACK], F32)
            for g in reversed(range(PASSES)):
                for u in reversed(range(width // P)):
                    if g or u:
                        silu_interleaved(act[:, g, u * P : (u + 1) * P], hidden_bank(0, g, first + u * P))
            return act, h0

        def scalar_bank(n, h0):
            by_byte = ring.tile([P, PACK, P], F32, name="by_byte", tag="by_byte", bufs=2)
            nc.scalar.activation(by_byte[:], hidden_bank(0, 0, A_STEPS[n][0], late=2 <= n < len(A_STEPS) - 1)[:], SILU)
            scaled = kept("scaled%d" % n, [P, PACK, P], BF16)
            for t in range(PACK):
                nc.scalar.activation(scaled[:, t], by_byte[:, t], COPY, scale=s_runs[:, 0, 0, t : t + 1])
            nc.scalar.copy(
                out=h0[:, 0:P].rearrange("p (c i) t -> p c t i", i=PACK), in_=scaled[:].rearrange("p t (c i) -> p c t i", i=PACK)
            )

        def back(n, act, h0):
            first, width, pool_share, scalar_share, hold = A_STEPS[n]
            h1 = kept("h1", [P, width, PACK], BF16, tag="h_pool" if pool_share else "h_vector")
            lo = width - pool_share
            if pool_share:
                scale_on_pool(h1[:, lo:], act[:, 1, lo:], 0, 1, pool_share)
            if scalar_share < width:
                scale_on_vector(h0[:, scalar_share:], act[:, 0, scalar_share:], 0, 0, width - scalar_share)
            if lo:
                scale_on_vector(h1[:, 0:lo], act[:, 1, 0:lo], 0, 1, lo)
            return h0, h1

        fronts = []
        for n in range(2):
            fronts.append(front(n))
            scalar_bank(n, fronts[n][1])
        h_long = kept("h_long", [P, J + late, PACK], BF16, tag="h_pool")
        scale_on_pool(h_long[:, J:], act_late[:], 1, 0, late)
        for lo, hi in ((0, HALF), (HALF, HALF + WIDE), (HALF + WIDE, J)):
            scale_on_vector(h_long[:, lo:hi], act_pass1[:, lo:hi], 1, 1, hi - lo)
        h = back(0, *fronts[0])

        def scores(mt, words, scales):
            banks = []
            for jh in range(J // HALF):
                cols = slice(jh * HALF, (jh + 1) * HALF)
                acc = psum.tile([P, HALF], F32, name="acc", tag="scores")
                for g in reversed(range(PASSES)):
                    nc.tensor.matmul_mx(
                        out=acc[:],
                        lhsT=words[:, g].bitcast(FP8X4),
                        lhsT_scale=scales[:, g],
                        rhs=hb_words[g][jh].bitcast(FP8X4),
                        rhs_scale=hb_scales[:, g, cols],
                        start=(g == PASSES - 1),
                        stop=(g == 0),
                    )
                banks.append((mt, cols, acc))
            return banks

        def finish(mt, cols, acc):
            piece = WIDE if (mt + 1) * P == M and cols.stop == J else HALF
            for start in range(0, HALF, piece):
                part = slice(cols.start + start, cols.start + start + piece)
                res = ring.tile([P, piece], F32, name="res", tag="res", bufs=12)
                nc.vector.scalar_tensor_tensor(
                    out=res[:], in0=acc[:, start : start + piece], scalar=OUT_SCALE, in1=bias[:, part], op0=MULT, op1=ADD
                )
                nc.sync.dma_start(out=out[mt * P : (mt + 1) * P, part], in_=res[:])

        last = len(A_STEPS) - 1
        held = []
        for n, (first, width, pool_share, scalar_share, hold) in enumerate(A_STEPS):
            ha_words = kept("ha_words", [P, PASSES, width], U32, tag="scaled%d" % n if n else None)
            ha_scales = kept("ha_scales", [P, PASSES, width], U8, tag="act%d" % n if n == last else None)
            piece = P if n == last - 1 else width
            if n == 0:
                quantise(flat(h_long[:, J:]), hb_rest[:, J + EARLY - HALF :], hb_scales[:, 0, EARLY:])
            for start in range(0, width, piece):
                for g in reversed(range(PASSES)):
                    part = slice(start, start + piece)
                    quantise(flat(h[g][:, part]), ha_words[:, g, part], ha_scales[:, g, part])
            if n == 0:
                quantise(flat(h_long[:, 0:J]), hb_rest[:, 0:J], hb_scales[:, 1])
            for bank in held:
                finish(*bank)
            if n + 2 <= last:
                fronts.append(front(n + 2))
            if n + 2 == last:
                scalar_bank(last, fronts[last][1])
            if n < last:
                h = back(n + 1, *fronts[n + 1])
            for u in range(width // P):
                own = slice(u * P, (u + 1) * P)
                banks = scores(first // P + u, ha_words[:, :, own], ha_scales[:, :, own])
                now = len(banks) - hold if u == width // P - 1 else len(banks)
                for bank in banks[:now]:
                    finish(*bank)
                held = banks[now:]
            if n + 2 < last:
                scalar_bank(n + 2, fronts[n + 2][1])
